import numpy as np, ml_dtypes
CORES = [25,29,65,69,153,157,193,197]
N = 8
import mx_ref
BF = ml_dtypes.bfloat16
def gcols(t, e):
    v = np.concatenate([t.reshape(8, 16, -1, 4), np.zeros((8, 16, 1, 4), BF)], axis=2)
    return np.ascontiguousarray(np.stack([v[g][:, e[g]] for g in range(8)])).reshape(128, -1)
def gpick(z, e):
    return np.concatenate([z[16 * g:16 * g + 16][:, e[g]] for g in range(8)])
def tile(rs):
    return np.stack(rs, axis=2).reshape(128, -1).astype(BF)
def pick(q, e):
    c = np.concatenate([q[0].reshape(128, -1, 4), np.zeros((128, 1, 4), np.uint8)], axis=1); s = np.concatenate([q[1], np.ones((16, 1), np.uint8)], axis=1)
    return (np.ascontiguousarray(c[:, e].reshape(128, -1)), np.ascontiguousarray(s[:, e]))
def join(*qs):
    return (np.concatenate([q[0] for q in qs], axis=1), np.concatenate([q[1] for q in qs], axis=1))
def put(q, e, v):
    c, s = q[0].reshape(128, -1, 4).copy(), q[1].copy(); c[:, e] = v[0].reshape(128, -1, 4); s[:, e] = v[1]
    return (c.reshape(128, -1), s)
def pk(c, s):
    return (np.ascontiguousarray(c), mx_ref.live(s))
def emit(q):
    return q[0], q[1]
def packed(v, rng):
    q = [mx_ref.quantize(np.ascontiguousarray(v[r])) for r in range(N)]
    return np.stack([a for a, b in q]), np.stack([mx_ref.plane(b, rng) for a, b in q])
def values_of_codes():
    e, c = np.zeros((128, 128, 4), np.float32), np.zeros((128, 2, 4), np.uint8)
    e[np.arange(128), np.arange(128), 0] = 1
    c[:127, :, 0] = np.arange(256).reshape(2, 128).T[:127]
    return mx_ref.matmul(mx_ref.quantize(e.reshape(128, 512).astype(BF)), (c.reshape(128, 8), np.full((16, 2), 127, np.uint8))).T.reshape(-1).astype(np.float64)
CODE_VALUE, SCALE_VALUE = values_of_codes(), 2.0 ** (np.arange(256) - 127.0)
def decode(q):
    return (CODE_VALUE[q[0]].reshape(16, 8, -1, 4) * SCALE_VALUE[q[1]][:, None, :, None] + 0.0).reshape(128, -1).astype(np.float32)
def f(rng, *shape):
    return mx_ref.flush((rng.standard_normal(shape, dtype=np.float32) * np.exp2(rng.integers(-2, 3, shape[:-1] + (1,)))).astype(BF))
def wide(rng, *shape, cols=0):
    v = rng.standard_normal(shape, dtype=np.float32) * np.exp2(rng.integers(-12, 13, shape)).astype(np.float32)
    if cols: v *= np.repeat(np.exp2(rng.integers(-cols, cols + 1, shape[:-2] + (1, shape[-1] // 4))) * (rng.random(shape[:-2] + (1, shape[-1] // 4)) > 0.0625), 4, axis=-1).astype(np.float32)
    return mx_ref.flush(v.astype(BF))
C, A, K = 320, 96, 128
STEP = [1, 2, 4]
MANY = np.repeat(np.array([2, 1, 0]), [A, K, A])
def numbers_of(rng):
    return {"x": np.array(f(rng, N, 128, 4 * C)), "u": np.array(f(rng, N, 128, 512)), "v": np.array(f(rng, N, 128, 512))}
def layers(rng, still=[]):
    w = np.array(f(rng, N, 128, 2048)).reshape(N, 8, 16, 4, 8, 16, 4)
    for i in still:
        w[:, :, i] = 0
        w[:, :, :, :, :, i] = 0
    return w
def weights(rng, w):
    c, p = packed(np.ascontiguousarray(w).reshape(N, 128, 2048), rng)
    return {"wc": c, "ws": p}
def numbers_to(x, u, v):
    return {"x": x.astype(np.float32).reshape(N, 128, 4 * C).astype(BF), "u": u.reshape(N, 128, 512), "v": v}
def setup_inputs(rng):
    return {**numbers_of(rng), **weights(rng, layers(rng))}
def setup_inputs_ties(rng):
    d = numbers_of(rng)
    x = d["x"].astype(np.float32).reshape(N, 8, 16, C, 4)
    x[:, :, 0] = 0
    x[:, :, 0, :, 0] = np.exp2(rng.integers(0, 3, (N, 8, C)))
    u = d["u"].reshape(N, 128, 128, 4)
    u[:, :, ::16] = 0
    o = rng.permutation(N)
    g = rng.permutation(8)[:2]
    for r in range(N):
        for h in range(0, 128, 16): u[r, h, h, 0] = 0.0 if r == o[0] else -1.0 if r == o[1] else 1.0
        if r != o[0] and r ^ 1 != o[0]:
            for i in range(2):
                s = np.ones(C)
                s[A * (r % 2):A * (r % 2) + A] = 0
                s[C - 1 - i * (r % 2)] = 2
                x[r, g[i], 0, :, 0] = np.exp2(2 - s if r == o[1] else s)
    return {**numbers_to(x, u, d["v"]), **weights(rng, layers(rng, [0]))}
def setup_inputs_near(rng):
    d = numbers_of(rng)
    x = d["x"].astype(np.float32).reshape(N, 8, 16, C, 4)
    x[:, :, 0] = 0
    x[:, :, 8:] = 0
    u = d["u"].reshape(N, 128, 128, 4)
    u[:, :, ::16] = 0
    o = rng.permutation(N) % 4
    for r in range(N):
        s = rng.integers(0, 256, (8, C))
        if o[r] < 3:
            for t in range(8): x[r, :, 8 + t // 4, :, t % 4] = ((s >> t) & 1) * 2.0 ** (t - 23)
        if o[r] < 2:
            x[r, :, 0, :, 0] = rng.integers(0, 2, (8, C)) * 2.0 - 1.0
            x[r, :, 11, :, 0] = 2.0 ** -10
        if o[r] == 2:
            for g in range(8): x[r, g, 0, rng.permutation(C)[:2], 0] = np.array([2.0 ** 29, -2.0 ** 29])
        if o[r] == 3:
            x[r, :, 10, :, 0] = rng.integers(-7, 8, (8, C)) * 2.0 ** -30
            for g in rng.permutation(8)[:4]:
                a = rng.permutation(C) % 16
                x[r, g, 10, :, 0] = np.where(a < 8, a + 8, -a) * 2.0 ** -30
                x[r, g, 15, :, 0] = 1.96875 * 2.0 ** -14
        k = 1.0 if o[r] == 0 else 2.0 ** -30
        for h in range(0, 128, 16):
            if o[r] < 2:
                u[r, h, h, 0] = k
                u[r, h + 11, h, 0] = k
            if o[r] == 2: u[r, h, h, 0] = 1.0
            if o[r] < 3: u[r, h + 8:h + 10, h] = k
            else: u[r, h + 10, h, 0] = k
    return {**numbers_to(x, u, d["v"]), **weights(rng, layers(rng, [0, 8, 9, 10, 11, 12, 13, 14, 15]))}
def setup_inputs_huge(rng):
    d = numbers_of(rng)
    h, o = rng.permutation(8), rng.permutation(N)
    x = (0.75 + 0.25 * rng.random((N, 8, 1, C, 1))) * (0.9 + 0.1 * rng.random((N, 8, 16, C, 4))) * 2.0 ** 30
    c = rng.integers(0, 2, (N, 1, 1, C, 1))
    x[:, h[4:6]] *= 0.0625 + 0.9375 * c
    x[:, h[6:]] *= 1.0 - 0.9375 * c
    x[o[0]] = (0.95 + 0.05 * rng.random((8, 16, C, 4))) * 2.0 ** 30
    u = d["u"].reshape(N, 128, 128, 4)
    u[:, :, ::16] = 0
    for r in range(N):
        k = rng.permutation(8)
        for g in range(8):
            e = float(k[g] % 2 * 2 - 1)
            if r == o[0]: u[r, :, 16 * g] = 2.0 ** 30 * e
            else:
                for i in (h[:4] if k[g] < 4 else h[4:]):
                    t = -e if i in h[6:] else e
                    u[r, 16 * i:16 * i + 16, 16 * g] = (2.0 ** 30 * (1 - 0.1 * rng.random((16, 4))) * t).astype(np.float32).astype(BF)
    w = np.zeros((N, 128, 4, 128, 4), np.float32)
    i = np.arange(128)
    for b in range(4): w[:, i, b, i, b] = -4
    return {**numbers_to(x, u, d["v"]), **weights(rng, w.astype(BF))}
def setup_inputs_edges(rng):
    d = numbers_of(rng)
    s = (8, 16, C, 4)
    x = (2 * rng.integers(4, 8, (N,) + s) + 1) * 0.125 * (rng.integers(0, 2, (N,) + s) * 2.0 - 1.0) * np.exp2(rng.integers(-2, 2, (1, 8, 1, C, 1)))
    x[:, :, 0] = 0
    x[:, :, 0, :, 0] = 1.96875 * 2.0 ** 12
    x[:, :, 8:] = 0
    for t in range(9): x[:, :, 8 + t // 4, :, t % 4] = (np.arange(C) >> t) & 1
    u = d["u"].reshape(N, 128, 128, 4)
    u[:, :, ::16] = 0
    w = layers(rng, [0, 8, 9, 10, 11, 12, 13, 14, 15])
    k, e = rng.permutation(8) % N, rng.integers(0, 2, 8)
    for r in range(N):
        for t in range(2):
            c = ((r >> t) & 1) * 2.0 - 1.0
            x[r, :, 11, :, t] = c
            for g in range(8): w[r, g, 11, 0, g, 0, t] = -4096.0 * c
        for g in range(8):
            if (bin(r & int(k[g])).count("1") + int(e[g])) % 2 == 1:
                for t in range(9): u[r, 16 * g + 8 + t // 4, 16 * g, t % 4] = 2.0 ** t
    return {**numbers_to(x, u, d["v"]), **weights(rng, w)}
def setup_inputs_spread(rng):
    d = setup_inputs(rng)
    d["x"] = wide(rng, N, 128, 4 * C, cols=6)
    return d
def check_inputs(d):
    b = []
    for k in ("x", "u", "v"):
        a = np.abs(d[k].astype(np.float32))
        if not (np.isfinite(a).all() and ((a == 0) | (a >= 2.0 ** -30) & (a <= 2.0 ** 30)).all()): b.append("a value of " + k)
    none, least, most = [emit(mx_ref.quantize(np.full((128, 16), k, np.float32).astype(BF)))[1][0, 0] for k in (0.0, 2.0 ** -30, 2.0 ** 30)]
    for r in range(N):
        if ((d["wc"][r] == 0x7F) | (d["wc"][r] == 0xFF)).any(): b.append("wc: a code that is no number")
        s = mx_ref.live(d["ws"][r])
        if ((s != none) & ((s < least) | (s > most))).any(): b.append("ws: a scale out of range")
        if ((s == none)[:, None, :, None] & ((d["wc"][r].reshape(16, 8, -1, 4) & 0x7F) != 0)).any(): b.append("wc: a code that isn't zero beside the scale of zeros")
    return b
def reference(x, u, v, wc, ws):
    qu = [mx_ref.quantize(u[r]) for r in range(N)]
    lay = [pk(wc[r], ws[r]) for r in range(N)]
    now = [x[r] for r in range(N)]
    last = np.zeros((N, 8, C), np.int64)
    for h in STEP:
        own, times_of = [], np.zeros((N, 8, C), np.int64)
        for r in range(N):
            q = mx_ref.quantize(now[r])
            own.append(decode(q).astype(BF))
            s = mx_ref.matmul(qu[r], q)[::16] + np.float32(0.0)
            np.put_along_axis(times_of[r], np.argsort(-s, axis=1, kind="stable"), np.stack([MANY] * 8), axis=1)
        first = np.full((N, 8, C), K)
        part, packs = [], []
        for r in range(N):
            both = np.minimum(times_of[r], times_of[r ^ h])
            e = np.zeros((8, K), np.int64)
            for g in range(8):
                e[g] = np.flatnonzero(both[g])[:K]
                shared = np.repeat(np.arange(C), both[g])
                last[r, g] = np.concatenate([shared, np.repeat(np.arange(C), times_of[r, g] - both[g])])
                first[r, g, np.searchsorted(shared, e[g])] = np.arange(K)
            part.append(gcols(own[r], e))
            packs.append(mx_ref.quantize(part[r]))
        for r in range(N):
            z = mx_ref.quantize((part[r].astype(np.float32) - decode(packs[r ^ h])).astype(BF))
            a = gcols(own[r], last[r]).astype(np.float32)
            made = []
            for b in range(4):
                p = mx_ref.matmul(pick(lay[r], np.arange(128 * b, 128 * b + 128)), z) * np.float32(0.015625)
                made.append(a[:, b::4] + gpick(np.concatenate([p, np.zeros((128, 1), np.float32)], axis=1), first[r]))
            now[r] = tile(made)
    y, nl = np.zeros((N, 128, C), np.float32), np.zeros((N, 8, C), np.float32)
    oc, osc = np.zeros((N, 128, 4 * C), np.uint8), np.zeros((N, 16, C), np.uint8)
    for r in range(N):
        q = mx_ref.quantize(now[r])
        y[r] = mx_ref.matmul(mx_ref.quantize(v[r]), q)
        nl[r] = last[r]
        oc[r], osc[r] = emit(q)
    return {"y": y, "nl": nl, "oc": oc, "osc": osc}

@@ -1,0 +1,518 @@
+from concourse.mybir import dt, AluOpType, ActivationFunctionType
+
+ALU = AluOpType
+ACT = ActivationFunctionType
+C, A, K = 320, 96, 128
+STEP = [1, 2, 4]
+NC = C // 16
+N1, N2 = (A + K) // 16, A // 16
+NV = 13
+WW = C + K
+BIG = 1e25
+DROP = 262144.0
+CODE = "float8_e4m3fn_x4"
+TILES = [([0, 19, 18, 17], 320), ([16, 15, 14, 13], 256), ([12, 11, 10, 9], 192), ([8, 7, 6, 5], 128), ([4, 3, 2, 1], 128)]
+TOFF = [sum(n for _, n in TILES[:k]) for k in range(len(TILES) + 1)]
+RS = 128
+EW = 520
+ES = 8
+AFTER = "shared count_s sums pick_v before hold copies e far_s far_v pack_far near named values diff near64 list add new"
+LATE = (("s", 0, 0, 20), ("s", 1, 0, 20), ("s", 2, 0, 8), ("v", 2, 8, 20), ("v", 3, 0, 20))
+
+
+def _sb(n, d):
+    return ("sbuf", [128, n], d)
+
+
+SCRATCH = {
+    "x0": _sb(4 * C, "bfloat16"), "x1": _sb(4 * C, "bfloat16"), "ut": _sb(512, "bfloat16"), "vt": _sb(512, "bfloat16"),
+    "qu": _sb(128, CODE), "su": _sb(128, "uint8"),
+    "qu2": _sb(128, CODE), "su2": _sb(128, "uint8"), "qv": _sb(128, CODE), "sv": _sb(128, "uint8"),
+    "qw": _sb(512, CODE), "sw": _sb(512, "uint8"), "et": _sb(2 * EW, "bfloat16"),
+    "qe": _sb(512, CODE), "se": _sb(512, "uint8"), "qf": _sb(K, CODE), "sf": _sb(K, "uint8"),
+    "qz": _sb(128, CODE), "sz": _sb(128, "uint8"), "zt": _sb(512, "bfloat16"), "ft": _sb(512, "bfloat16"), "ff": _sb(512, "bfloat16"),
+    "f64": _sb(512, "bfloat16"), "win": _sb(4 * WW, "bfloat16"), "far": _sb(4 * C, "bfloat16"), "ysb": _sb(C, "float32"),
+    "wt": _sb(4 * TOFF[-1], "bfloat16"), "qt": _sb(TOFF[-1], CODE), "stp": _sb(TOFF[-1], "uint8"),
+    "ig": _sb(512, "bfloat16"), "gt": _sb(512, "bfloat16"), "qg": _sb(128, CODE), "sg": _sb(128, "uint8"),
+    "iu": _sb(8, "int32"), "offu": _sb(8, "uint16"), "idg": _sb(C, "int32"), "idg2": _sb(C, "int32"),
+    "ipc": _sb(4, "int32"), "i16": _sb(NC, "float32"), "qcol": _sb(4, "float32"), "ka": _sb(8, "float32"),
+    "kb": _sb(8, "float32"), "vals": _sb(2 * C, "float32"), "val3": _sb(K, "float32"),
+    "dg": _sb(C, "float32"), "mk": _sb(C, "float32"), "d0s": _sb(C, "float32"), "seg": _sb(C, "bfloat16"),
+    "d0g": _sb(WW, "float32"), "nb": _sb(NC, "float32"), "tab": _sb(C, "bfloat16"), "zero": _sb(EW, "bfloat16"),
+    "rm": _sb(C, "float32"), "wf": _sb(C, "float32"), "eqs": _sb(C, "bfloat16"), "e2": _sb(NC, "float32"), "e3": _sb(NC, "float32"),
+    "rk": _sb(NV * RS, "bfloat16"), "pa": _sb(NC, "float32"), "cw": _sb(C, "float32"), "pd": _sb(NC, "float32"),
+    "fr": _sb(C, "bfloat16"), "cf": _sb(C + 16, "float32"), "orow": _sb(C, "float32"), "ox": _sb(A + K, "float32"),
+    "fg": _sb(A + K, "float32"), "fx": _sb(A + K, "float32"), "f20": _sb(NC, "float32"),
+    "sh": _sb(C, "bfloat16"), "cs": _sb(C, "bfloat16"), "ec": _sb(8 * 208, "bfloat16"), "ej": _sb(8 * 256, "bfloat16"),
+    "ea": _sb(8 * 104, "float32"), "eo": _sb(8, "uint16"),
+    "mr": _sb(C, "bfloat16"), "cm": _sb(C + 16, "float32"), "cg": _sb(WW, "float32"), "cx": _sb(WW, "float32"),
+    "oa": _sb(2 * N1, "uint16"), "mw": _sb(N1, "float32"),
+    "ns": _sb(NC, "float32"), "r1": _sb(NC, "float32"), "r2": _sb(NC, "float32"), "t1": _sb(NC, "float32"),
+    "sl": _sb(NC, "float32"), "so": _sb(NC, "uint16"), "sval": _sb(C, "float32"), "nrow": _sb(C, "float32"), "nlb": _sb(C, "float32"),
+    "ntab": _sb(WW, "float32"), "nx": _sb(C, "float32"), "no": _sb(NC, "uint16"),
+    "hr": _sb(NC, "uint16"), "hq": _sb(C, CODE), "hs": _sb(C, "uint8"),
+}
+for _r in range(4):
+    SCRATCH["qx%d" % _r] = _sb(C, CODE)
+    SCRATCH["sx%d" % _r] = _sb(C, "uint8")
+for _r in range(3):
+    SCRATCH["rw%d" % _r] = _sb(NC, "uint16")
+    SCRATCH["lr%d" % _r] = _sb(NC, "uint16")
+    SCRATCH["lq%d" % _r] = _sb(C, CODE)
+    SCRATCH["ls%d" % _r] = _sb(C, "uint8")
+for _b in range(7):
+    SCRATCH["ps%d" % _b] = ("psum", [128, 512], "float32")
+
+SEMAPHORES = ["cv", "cs", "cp", "cg", "ldx", "ldu", "ldv", "ldw", "lds", "st", "sent", "ha", "hc", "hp",
+              "ra0", "ra1", "ra2", "rf0", "rf1", "rf2"]
+
+
+def _helpers(T, topo, src, dst):
+    if topo.may_write(src, dst):
+        return []
+    c = [h for h in topo.cores_of(src) if T.rank_of(h) is None and topo.may_write(h, dst)]
+    near = [h for h in c if topo.die(h) == topo.die(src)]
+    return (near or c)[:2]
+
+
+def _hand_on(g, core, T, topo):
+    for r, h in enumerate(STEP):
+        for i, src in enumerate(T.cores):
+            dst = T.cores[i ^ h]
+            hs = _helpers(T, topo, src, dst)
+            if core not in hs:
+                continue
+            j, w = hs.index(core), C // len(hs)
+            n_in, n, m = len(topo.engines(src, core)), len(topo.engines(core, dst)), topo.mask(core, dst)
+            rid, pid = topo.addr(dst, core)
+            g.wait_ge(T.sem.hc, n_in)
+            g.remote_dma(T["lq%d" % r][:, j * w:j * w + w].bitcast(dt.uint8), T.hq[:, 0:w].bitcast(dt.uint8),
+                         T.sem["rf%d" % r], T.sem.sent, pid, rid, m)
+            g.wait_ge(T.sem.hp, n_in)
+            g.remote_dma(T["ls%d" % r][:, j * w:j * w + w], T.hs[:, 0:w], T.sem["rf%d" % r], T.sem.sent, pid, rid, m)
+            if j == 0:
+                g.wait_ge(T.sem.ha, n_in)
+                g.remote_dma(T["lr%d" % r][:], T.hr[:], T.sem["ra%d" % r], T.sem.sent, pid, rid, m)
+            g.wait_ge(T.sem.sent, (3 if j == 0 else 2) * n)
+
+
+def rank_program(g, core, T, topo):
+    rank = T.rank_of(core)
+    if rank is None:
+        _hand_on(g, core, T, topo)
+        return
+    Q = {"v": g.vector, "s": g.scalar, "p": g.tensor, "g": g, "y": g.sync}
+    own = {"v": "cv", "s": "cs", "p": "cp", "g": "cg"}
+    total = {}
+    know = {q: {} for q in Q}
+    hist = {}
+
+    def V(name, lo=0, hi=None, step=1):
+        return (name, lo, SCRATCH[name][1][1] if hi is None else hi, step)
+
+    def ap(v):
+        return T[v[0]][:, v[1]:v[2]:v[3]] if v[3] != 1 else T[v[0]][:, v[1]:v[2]]
+
+    def cols(v):
+        return frozenset([0]) if v[0].startswith("ps") else frozenset(range(v[1], v[2], v[3]))
+
+    def order(q, reads, writes):
+        need = {}
+        for vs, wr in ((reads, False), (writes, True)):
+            for v in vs:
+                cs_, bank_ = cols(v), v[0].startswith("ps")
+                for (c2, w2, q2, s, n, k) in hist.get(v[0], []):
+                    if (wr or w2 or (bank_ and q2 != q)) and know[q].get(s, 0) < n and cs_ & c2:
+                        if need.get(s, (0, None))[0] < n:
+                            need[s] = (n, k)
+        for s in sorted(need, key=lambda a: -len(need[a][1])):
+            n, k = need[s]
+            if know[q].get(s, 0) >= n:
+                continue
+            Q[q].wait_ge(T.sem[s], n)
+            for a, b in k.items():
+                if know[q].get(a, 0) < b:
+                    know[q][a] = b
+
+    def note(q, s, inc, reads, writes):
+        total[s] = total.get(s, 0) + inc
+        k = dict(know[q]) if q else {}
+        k[s] = total[s]
+        for vs, wr in ((reads, False), (writes, True)):
+            for v in vs:
+                hist.setdefault(v[0], []).append((cols(v), wr, q, s, total[s], k))
+
+    def op(q, make, reads, writes):
+        order(q, reads, writes)
+        make().then_inc(T.sem[own[q]], 1)
+        note(q, own[q], 1, reads, writes)
+
+    def dma(q, s, out, in_, reads, writes):
+        order(q, reads, writes)
+        Q[q].dma_start(out, in_).then_inc(T.sem[s], 16)
+        note(q, s, 16, reads, writes)
+
+    def aps(x):
+        return [x] if isinstance(x, tuple) else []
+
+    def val(x):
+        return ap(x) if isinstance(x, tuple) else x
+
+    def src(v, off):
+        return ap(v).indirect(ap(off)) if off else ap(v)
+
+    def ts(out, in0, s1, op0, s2=None, op1=None, off=None):
+        rd = [in0] + aps(s1) + aps(s2) + aps(off)
+        if op1 is None:
+            op("v", lambda: g.vector.tensor_scalar(ap(out), src(in0, off), val(s1), None, op0), rd, [out])
+        else:
+            op("v", lambda: g.vector.tensor_scalar(ap(out), src(in0, off), val(s1), val(s2), op0, op1), rd, [out])
+
+    def tt(out, in0, in1, o, off=None):
+        op("v", lambda: g.vector.tensor_tensor(ap(out), src(in0, off), ap(in1), o), [in0, in1] + aps(off), [out])
+
+    def cp(out, in_, off=None):
+        op("v", lambda: g.vector.tensor_copy(ap(out), src(in_, off)), [in_] + aps(off), [out])
+
+    def scatter(w, off, in_):
+        op("v", lambda: g.vector.tensor_copy(ap(w).indirect(ap(off)), ap(in_)), [in_, off], [w])
+
+    def scan(out, d0, d1, init, o0, o1):
+        op("v", lambda: g.vector.tensor_tensor_scan(ap(out), ap(d0), ap(d1), val(init), o0, o1), [d0, d1] + aps(init), [out])
+
+    def hold(out, in_):
+        scan(out, V("d0g", 0, in_[2] - in_[1]), in_, 0.0, ALU.add, ALU.min)
+
+    def fill(out, c):
+        op("v", lambda: g.vector.memset(ap(out), c), [], [out])
+
+    def quant(q, s, in_):
+        op("v", lambda: g.vector.quantize_mx(ap(q), ap(s), ap(in_)), [in_], [q, s])
+
+    def act(out, in_, f, bias=None, scale=None, acc=None, off=None):
+        kw = {}
+        if bias is not None:
+            kw["bias"] = val(bias)
+        if scale is not None:
+            kw["scale"] = scale
+        if acc is not None:
+            kw["accum_out"] = ap(acc)
+        op("s", lambda: g.scalar.activation(ap(out), src(in_, off), f, **kw), [in_] + aps(bias) + aps(off), [out] + aps(acc))
+
+    def gather(q, out, w, off, scale):
+        if q == "s":
+            act(out, w, ACT.Copy, scale=scale, off=off)
+        else:
+            ts(out, w, scale, ALU.mult, off=off)
+
+    def mm(out, lq, ls, rq, rs, start=True, stop=True):
+        op("p", lambda: g.tensor.matmul_mx(ap(out), ap(lq), ap(ls), ap(rq), ap(rs), start, stop), [lq, ls, rq, rs], [out])
+
+    def iota(out, pattern, base, cm, small=False):
+        if small:
+            op("g", lambda: g.iota(ap(out), pattern, base, cm, allow_small_or_imprecise_dtypes=True), [], [out])
+        else:
+            op("g", lambda: g.iota(ap(out), pattern, base, cm), [], [out])
+
+    def send(r, what):
+        dst = T.cores[rank ^ STEP[r]]
+        hs, back = _helpers(T, topo, core, dst), _helpers(T, topo, dst, core)
+        n_in = [len(topo.engines(h, core)) for h in (back or [dst])]
+
+        def write(to, out, in_, s):
+            rid, pid = topo.addr(to, core)
+            g.remote_dma(out, in_, T.sem[s], T.sem.sent, pid, rid, topo.mask(core, to))
+            total["sent"] = total.get("sent", 0) + len(topo.engines(core, to))
+
+        if what == "places":
+            order("g", [V("rw%d" % r)], [])
+            write(hs[0] if hs else dst, T["hr" if hs else "lr%d" % r][:], T["rw%d" % r][:], "ha" if hs else "ra%d" % r)
+            note(None, "ra%d" % r, n_in[0], [], [V("lr%d" % r)])
+            return
+        q, s = T["qx%d" % r], T["sx%d" % r]
+        order("g", [V("qx%d" % r), V("sx%d" % r)], [])
+        if hs:
+            w = C // len(hs)
+            for j, h in enumerate(hs):
+                write(h, T.hq[:, 0:w].bitcast(dt.uint8), q[:, j * w:j * w + w].bitcast(dt.uint8), "hc")
+            for j, h in enumerate(hs):
+                write(h, T.hs[:, 0:w], s[:, j * w:j * w + w], "hp")
+        else:
+            write(dst, T["lq%d" % r][:].bitcast(dt.uint8), q[:].bitcast(dt.uint8), "rf%d" % r)
+            write(dst, T["ls%d" % r][:], s[:], "rf%d" % r)
+        note(None, "rf%d" % r, 2 * sum(n_in), [], [V("lq%d" % r), V("ls%d" % r)])
+
+    def col(name, c):
+        return V(name, c, c + 1)
+
+    def wrapped(name, lo=0, hi=None):
+        v = V(name, lo, hi)
+        return (name, lo + 15, v[2], 16)
+
+    def win(b, lo, hi):
+        return V("win", b * WW + lo, b * WW + hi)
+
+    def slot(c, lo, hi):
+        for k, (runs, n) in enumerate(TILES):
+            if c in runs:
+                o = 4 * TOFF[k] + runs.index(c)
+                return V("wt", o + 4 * lo, o + 4 * hi - 3, 4)
+
+    def eb(b):
+        return V("qe", 128 * b, 128 * b + 128), V("se", 128 * b, 128 * b + 128)
+
+    def bank(b, n):
+        return V("ps%d" % (2 + b), 0, n)
+
+    BACK, BACK1 = col("qcol", 2), col("qcol", 3)
+
+    dma("y", "ldx", T.x0[:], T.x[:], [], [V("x0")])
+    dma("s", "ldu", T.ut[:], T.u[:], [], [V("ut")])
+    dma("y", "ldw", T.qw[:].bitcast(dt.uint8), T.wc[:], [], [V("qw")])
+    dma("y", "lds", T.sw[:], T.ws[:], [], [V("sw")])
+    dma("y", "ldv", T.vt[:], T.v[:], [], [V("vt")])
+
+    iota(V("iu"), [[16, 8]], 0, 0)
+    iota(V("idg"), [[0, NC], [1, 16]], 128, -1)
+    iota(col("ipc", 0), [[0, 1]], 0, 1)
+    iota(V("i16"), [[16, NC]], 0, 0, True)
+    iota(V("ig"), [[1, 8], [0, 64]], 0, 0, True)
+    fill(V("zero"), 0.0)
+    for h in range(2):
+        o = V("et", h * EW, h * EW + EW)
+        op("g", lambda: g.affine_select(ap(o), ap(V("zero")), [[-1, EW]], ALU.not_equal, 1.0, 2 + h, 4), [V("zero")], [o])
+    fill(V("d0s"), 0.0)
+    fill(col("rk", RS - 1), 0.0)
+    fill(V("d0s", 0, C, 16), -BIG)
+    for k, (runs, n) in enumerate(TILES):
+        a, b = 4 * (TOFF[k] + 16 * runs[-1]), 4 * TOFF[k + 1]
+        act(V("wt", a, b), V("zero", 0, b - a), ACT.Copy)
+    act(V("seg"), V("zero", 0, C), ACT.Identity, bias=1.0)
+    cp(V("offu"), V("iu"))
+    ts(V("idg2"), V("idg"), 15, ALU.bitwise_and)
+    ts(col("ipc", 1), col("ipc", 0), 15, ALU.bitwise_and)
+    ts(V("dg"), V("idg2"), 0.0, ALU.is_equal)
+    ts(col("ipc", 2), col("ipc", 0), 4, ALU.arith_shift_right)
+    quant(V("qu"), V("su"), V("ut"))
+    cp(V("qcol", 0, 2), V("ipc", 1, 3))
+    act(V("mk"), V("dg"), ACT.Identity, bias=-BIG, scale=2 * BIG)
+    act(V("d0g", 0, C), V("dg"), ACT.Identity, bias=-DROP, scale=64 * DROP)
+    act(V("d0g", C, WW), V("dg", 0, K), ACT.Identity, bias=-DROP, scale=64 * DROP)
+    op("v", lambda: g.vector.tensor_copy(T.qu2[:, 0:128].bitcast(dt.uint32), T.qu[:, 0:128].bitcast(dt.uint32).indirect(T.offu[:, 0:8])),
+       [V("qu"), V("offu")], [V("qu2")])
+    cp(V("su2"), V("su"), V("offu"))
+    fill(V("seg", 0, C, 16), 0.0)
+    ts(V("nb"), V("i16"), col("qcol", 0), ALU.subtract, 15.0, ALU.add)
+    ts(BACK, col("qcol", 0), -DROP, ALU.mult, 15 * DROP, ALU.add)
+    ts(V("gt"), V("ig"), col("qcol", 1), ALU.is_equal)
+    act(V("tab", 0, A), V("zero", 0, A), ACT.Identity, bias=2.0)
+    act(V("tab", A, A + K), V("zero", 0, K), ACT.Identity, bias=1.0)
+    act(V("tab", A + K, C), V("zero", 0, A), ACT.Copy)
+    act(col("cf", 0), col("zero", 0), ACT.Copy)
+    act(col("cm", 0), col("zero", 0), ACT.Copy)
+    act(V("ka"), V("i16", 0, 8), ACT.Identity, bias=col("qcol", 0))
+    act(BACK1, BACK, ACT.Identity, bias=-1.0)
+    act(V("kb"), V("ka"), ACT.Identity, bias=0.5)
+
+    for r in range(3):
+        rw, lr, qx, sx = "rw%d" % r, "lr%d" % r, V("qx%d" % r), V("sx%d" % r)
+        quant(qx, sx, V("x0" if r == 0 else "x1"))
+        send(r, "codes")
+        mm(V("ps0", 0, C), V("qu2"), V("su2"), qx, sx)
+        mm(V("ps1", 0, C), V("qu2"), V("su2"), qx, sx)
+        if r == 0:
+            iota(V("vals", C, 2 * C), [[1, C]], 0, 0, True)
+            iota(V("val3"), [[1, K]], C, 0, True)
+            quant(V("qg"), V("sg"), V("gt"))
+        else:
+            for b in range(4):
+                mm(bank(b, C), *eb(b), qx, sx)
+            act(V("vals", 0, C), V("vals", C, 2 * C), ACT.Copy)
+        if r == 1:
+            quant(V("qv"), V("sv"), V("vt"))
+        for lo, hi in ((256, C), (0, 256)):
+            tt(V("rm", lo, hi), V("ps0", lo, hi), V("mk", lo, hi), ALU.min)
+            scan(V("wf", lo, hi), V("d0s", lo, hi), V("rm", lo, hi), -BIG, ALU.add, ALU.max)
+
+        def compare(c):
+            ts(slot(c, 0, 16 * c), V("ps0", 0, 16 * c), col("wf", 16 * c + 15), ALU.is_lt)
+
+        def count(c):
+            scan(V("rk", RS * (c + 1) - 8 * c, RS * (c + 1)), slot(c, 0, 8 * c), slot(c, 8 * c, 16 * c), 0.0, ALU.add, ALU.add)
+
+        def sign(c):
+            act(slot(c, 0, 16 * c), V("ps1", 0, 16 * c), ACT.Sign, bias=col("wf", 16 * c + 15), scale=-1.0)
+
+        def sums(c):
+            act(slot(c, 0, 16 * c), slot(c, 0, 16 * c), ACT.Relu, acc=col("pa", c))
+
+        def pack(k):
+            a, b = TOFF[k], TOFF[k + 1]
+            quant(V("qt", a, b), V("stp", a, b), V("wt", 4 * a, 4 * b))
+
+        sign(NC - 1)
+        for c in range(NC - 1, NV - 1, -1):
+            if c - 1 >= NV:
+                sign(c - 1)
+            sums(c)
+        tt(slot(0, 0, C), V("ps0", 0, C), V("wf"), ALU.is_le)
+        compare(NV - 1)
+        scan(V("eqs"), V("seg"), slot(0, 0, C), 0.0, ALU.mult, ALU.add)
+        for c in range(NV - 1, 6, -1):
+            compare(c - 1)
+            count(c)
+            if c == NV - 1:
+                tt(V("e2"), V("nb"), wrapped("eqs"), ALU.subtract)
+            if c == 9:
+                pack(2)
+            if c == 8:
+                pack(0)
+        for c in (5, 4, 3, 2, 1):
+            compare(c)
+            if c == 4:
+                pack(3)
+        count(6)
+        pack(4)
+        pack(1)
+        for k in (0, 2, 3, 4, 1):
+            a, b = TOFF[k], TOFF[k + 1]
+            mm(V("ps6", 0, b - a), V("qg"), V("sg"), V("qt", a, b), V("stp", a, b), k == 0, k == 1)
+        tt(V("e3", NV, NC), V("e2", NV, NC), V("pa", NV, NC), ALU.subtract)
+        for c in (5, 4, 3, 2, 1):
+            count(c)
+        hold(V("cw"), V("ps6", 0, C))
+        tt(V("e3", 0, NV), V("e2", 0, NV), V("rk", RS - 1, NV * RS, RS), ALU.subtract)
+        tt(V("pd"), V("e3"), wrapped("cw"), ALU.add)
+        ts(V(rw), V("pd"), BACK, ALU.add)
+        send(r, "places")
+
+        if r == 0:
+            for b in range(4):
+                o = EW * (b % 2) + 2 - 2 * (b // 2)
+                quant(*eb(b), V("et", o, o + 512))
+                mm(bank(b, C), *eb(b), qx, sx)
+        for b in range(4):
+            act(win(b, 0, C), bank(b, C), ACT.Copy, scale=64.0)
+        for b in range(4):
+            mm(bank(b, C), *eb(b), V("lq%d" % r), V("ls%d" % r))
+        scatter(V("orow"), V(rw), V("vals", C, 2 * C))
+        cp(V("fr"), V("tab"), V(rw))
+        hold(V("ox"), V("orow", 0, A + K))
+        scan(V("cf", 1, C + 1), V("zero", 0, C), V("fr"), 0.0, ALU.add, ALU.add)
+        ts(V("oa", 0, N1), wrapped("ox"), BACK, ALU.add)
+        ts(V("oa", N1, 2 * N1), wrapped("ox"), BACK, ALU.add, 1.0, ALU.add)
+        for b in range(4):
+            act(V("far", b * C, b * C + C), bank(b, C), ACT.Copy)
+        oo = V("oa", 0, N1)
+        act(V("fg"), V("cf", 0, C), ACT.Copy, off=oo)
+        if r == 0:
+            act(V("vals", 0, C), V("vals", C, 2 * C), ACT.Copy)
+        act(V("sval", A + K, C), V("orow", 0, A), ACT.Copy)
+
+        def shared():
+            tt(V("mr"), V("tab"), V("fr"), ALU.min, off=V(lr))
+            ts(V("sh"), V("mr"), 1.0, ALU.min)
+            scan(V("cs"), V("zero", 0, C), V("sh"), 0.0, ALU.add, ALU.add)
+
+        def count_s():
+            for c in range(ES):
+                o = 64 * (c // 4)
+                act(V("ej", 256 * c, 256 * c + 256), V("cs", o, o + 256), ACT.Sign, bias=col("kb", c), scale=-1.0, acc=col("ea", 104 * c + 103))
+
+        def count_v():
+            for c in range(ES, 8):
+                ts(V("ec", 208 * c, 208 * c + 208), V("cs", 16 * c, 16 * c + 208), col("kb", c), ALU.is_le, 2.0, ALU.mult)
+            for c in range(ES, 8):
+                scan(V("ea", 104 * c, 104 * c + 104), V("ec", 208 * c, 208 * c + 104), V("ec", 208 * c + 104, 208 * c + 208),
+                     32.0 * c - (384.0 if ES > 4 else 256.0), ALU.add, ALU.add)
+
+        def list_e():
+            if ES > 4:
+                ts(V("eo", 0, 4), V("ea", 103, 4 * 104, 104), 0.5, ALU.mult, 128.0, ALU.add)
+                ts(V("eo", 4, 8), V("ea", 4 * 104 + 103, 8 * 104, 104), 0.5, ALU.mult, 192.0, ALU.add)
+            else:
+                ts(V("eo"), V("ea", 103, 8 * 104, 104), 0.5, ALU.mult, 128.0, ALU.add)
+
+        def far(q, bs):
+            for b in bs:
+                gather(q, V("ff", b, 512, 4), V("far", b * C, b * C + C), V("eo"), 1.0)
+
+        def pack_far():
+            quant(V("qf"), V("sf"), V("ff"))
+            for b in range(4):
+                mm(bank(b, K), *eb(b), V("qf"), V("sf"))
+
+        def near():
+            for b in range(4):
+                gather("s", V("ft", b, 512, 4), win(b, 0, C), V("eo"), 0.015625)
+
+        def diff():
+            for b in range(4):
+                tt(V("zt", b, 512, 4), V("ft", b, 512, 4), bank(b, K), ALU.subtract)
+            quant(V("qz"), V("sz"), V("zt"))
+            for b in range(4):
+                mm(bank(b, K), V("qw", 128 * b, 128 * b + 128), V("sw", 128 * b, 128 * b + 128), V("qz"), V("sz"))
+
+        def add():
+            for b in range(4):
+                tt(win(b, C, WW), bank(b, K), V("f64", b, 512, 4), ALU.add)
+
+        def before():
+            hold(V("fx"), V("fg"))
+            ts(V("f20", 0, N1), wrapped("fx"), BACK, ALU.subtract)
+            ts(V("f20", N1, NC), wrapped("fx", 0, A), BACK, ALU.subtract, 2.0, ALU.add)
+
+        def copies():
+            tt(V("mw"), wrapped("cx", A + K, WW), wrapped("cx", 0, A + K), ALU.subtract)
+            ts(V("r1"), wrapped("cx", 0, C), -1.0, ALU.mult, col("cm", C), ALU.add)
+            ts(V("ns", 0, N1), V("mw"), 0.5, ALU.is_lt, 8192.0, ALU.mult)
+            ts(V("ns", N1, NC), V("mw", 0, N2), 1.5, ALU.is_lt, 8192.0, ALU.mult)
+            tt(V("r2"), V("r1"), V("f20"), ALU.add)
+            tt(V("t1"), V("ns"), wrapped("cx", 0, C), ALU.add)
+            tt(V("sl"), V("r2"), V("t1"), ALU.min)
+            ts(V("so", 0, N1), V("sl", 0, N1), BACK, ALU.add)
+            ts(V("so", N1, NC), V("sl", N1, NC), BACK1, ALU.add)
+
+        def slots():
+            scatter(V("nrow"), V("so"), V("sval"))
+            hold(V("nx"), V("nrow"))
+            ts(V("no"), wrapped("nx"), BACK, ALU.add)
+
+        def new():
+            for q, b, lo, hi in LATE:
+                gather(q, V("x1", 64 * lo + b, 64 * hi, 4), win(b, 0, WW), V("no", lo, hi), 0.015625)
+
+        steps = {
+            "shared": shared, "count_s": count_s, "count_v": count_v, "e": list_e, "before": before,
+            "sums": lambda: scan(V("cm", 1, C + 1), V("zero", 0, C), V("mr"), 0.0, ALU.add, ALU.add),
+            "far_s": lambda: far("s", (2, 3)), "far_v": lambda: far("v", (0, 1)), "pack_far": pack_far, "near": near,
+            "named": lambda: scatter(V("vals", 0, C), V("eo"), V("val3")),
+            "values": lambda: act(V("sval", 0, A + K), V("vals", 0, C), ACT.Copy, off=oo),
+            "pick_v": lambda: cp(V("cg"), V("cm", 0, C + 1), V("oa")),
+            "hold": lambda: hold(V("cx"), V("cg")),
+            "near64": lambda: act(V("f64"), V("ft"), ACT.Copy, scale=64.0),
+            "diff": diff, "copies": copies, "add": add, "list": slots, "new": new,
+        }
+        for name in AFTER.split():
+            steps[name]()
+            if r == 2 and name == "near64":
+                act(V("ntab", 0, C), V("vals", C, 2 * C), ACT.Copy)
+                act(V("ntab", C, WW), V("vals", C, 2 * C), ACT.Copy, off=V("eo"))
+
+    act(V("nlb"), V("ntab"), ACT.Copy, off=V("no"))
+    qx, sx = "qx3", "sx3"
+    quant(V(qx), V(sx), V("x1"))
+    H = C // 2
+    mm(V("ps0", 0, H), V("qv"), V("sv"), V(qx, 0, H), V(sx, 0, H))
+    mm(V("ps1", 0, H), V("qv"), V("sv"), V(qx, H, C), V(sx, H, C))
+    dma("y", "st", T.oc[:], T[qx][:].bitcast(dt.uint8), [V(qx)], [])
+    for k in range(4):
+        dma("y", "st", T.osc[4 * k:4 * k + 4, :], T[sx][32 * k:32 * k + 4, :], [V(sx)], [])
+    cp(V("ysb", 0, H), V("ps0", 0, H))
+    act(V("ysb", H, C), V("ps1", 0, H), ACT.Copy)
+    dma("s", "st", T.y[:], T.ysb[:], [V("ysb")], [])
+    for k in range(8):
+        dma("y" if k % 2 else "s", "st", T.nl[k:k + 1, :], T.nlb[16 * k:16 * k + 1, :], [V("nlb")], [])
+    for s in SEMAPHORES:
+        if total.get(s, 0):
+            g.wait_ge(T.sem[s], total[s])

@@ -10,14 +10,18 @@ NV = 13
 WW = C + K
 BIG = 1e25
 DROP = 262144.0
+EL = 2 * A + 16
 CODE = "float8_e4m3fn_x4"
 TILES = [([0, 19, 18, 17], 320), ([16, 15, 14, 13], 256), ([12, 11, 10, 9], 192), ([8, 7, 6, 5], 128), ([4, 3, 2, 1], 128)]
 TOFF = [sum(n for _, n in TILES[:k]) for k in range(len(TILES) + 1)]
 RS = 128
 EW = 520
-ES = 8
-AFTER = "shared count_s sums pick_v before hold copies e far_s far_v pack_far near named values diff near64 list add new"
-LATE = (("s", 0, 0, 20), ("s", 1, 0, 20), ("s", 2, 0, 8), ("v", 2, 8, 20), ("v", 3, 0, 20))
+_END = " far_s far_v pack_far near named values diff near64 sc a0 nx a1 no a2 a3 new"
+_MID = " m sh cs count_s sums pick_v hold split copies e1 sl e2 so"
+AFTER = ["fr f512 orow tfar m ox sh oa cs count_s sums pick_v sv2 hold split copies e1 sl e2 so" + _END,
+         "orow frs f512 ox oa sv2 tfar" + _MID + _END,
+         "orow tfa frs tfb f512 ox oa sv2" + _MID + _END]
+LATE = (("s", 0, 0, 20), ("s", 1, 0, 20), ("v", 2, 0, 20), ("v", 3, 0, 20))
 
 
 def _sb(n, d):
@@ -35,16 +39,16 @@ SCRATCH = {
     "wt": _sb(4 * TOFF[-1], "bfloat16"), "qt": _sb(TOFF[-1], CODE), "stp": _sb(TOFF[-1], "uint8"),
     "ig": _sb(512, "bfloat16"), "gt": _sb(512, "bfloat16"), "qg": _sb(128, CODE), "sg": _sb(128, "uint8"),
     "iu": _sb(8, "int32"), "offu": _sb(8, "uint16"), "idg": _sb(C, "int32"), "idg2": _sb(C, "int32"),
-    "ipc": _sb(4, "int32"), "i16": _sb(NC, "float32"), "qcol": _sb(4, "float32"), "ka": _sb(8, "float32"),
+    "ipc": _sb(4, "int32"), "i16": _sb(NC, "float32"), "qcol": _sb(4, "float32"), "ka": _sb(8, "float32"), "kc": _sb(8, "float32"),
     "kb": _sb(8, "float32"), "vals": _sb(2 * C, "float32"), "val3": _sb(K, "float32"),
     "dg": _sb(C, "float32"), "mk": _sb(C, "float32"), "d0s": _sb(C, "float32"), "seg": _sb(C, "bfloat16"),
     "d0g": _sb(WW, "float32"), "nb": _sb(NC, "float32"), "tab": _sb(C, "bfloat16"), "zero": _sb(EW, "bfloat16"),
     "rm": _sb(C, "float32"), "wf": _sb(C, "float32"), "eqs": _sb(C, "bfloat16"), "e2": _sb(NC, "float32"), "e3": _sb(NC, "float32"),
     "rk": _sb(NV * RS, "bfloat16"), "pa": _sb(NC, "float32"), "cw": _sb(C, "float32"), "pd": _sb(NC, "float32"),
-    "fr": _sb(C, "bfloat16"), "cf": _sb(C + 16, "float32"), "orow": _sb(C, "float32"), "ox": _sb(A + K, "float32"),
-    "fg": _sb(A + K, "float32"), "fx": _sb(A + K, "float32"), "f20": _sb(NC, "float32"),
-    "sh": _sb(C, "bfloat16"), "cs": _sb(C, "bfloat16"), "ec": _sb(8 * 208, "bfloat16"), "ej": _sb(8 * 256, "bfloat16"),
-    "ea": _sb(8 * 104, "float32"), "eo": _sb(8, "uint16"),
+    "fr": _sb(C, "bfloat16"), "f512": _sb(C, "bfloat16"), "orow": _sb(C, "float32"), "ox": _sb(A + K, "float32"),
+    "pi": _sb(2 * N1, "int32"), "xi": _sb(2 * N1, "int32"), "fi": _sb(NC, "int32"), "tot": _sb(2, "float32"),
+    "sh": _sb(C, "bfloat16"), "cs": _sb(C, "bfloat16"), "ej": _sb(8 * EL, "bfloat16"),
+    "ea": _sb(8, "float32"), "eo": _sb(8, "uint16"),
     "mr": _sb(C, "bfloat16"), "cm": _sb(C + 16, "float32"), "cg": _sb(WW, "float32"), "cx": _sb(WW, "float32"),
     "oa": _sb(2 * N1, "uint16"), "mw": _sb(N1, "float32"),
     "ns": _sb(NC, "float32"), "r1": _sb(NC, "float32"), "r2": _sb(NC, "float32"), "t1": _sb(NC, "float32"),
@@ -235,7 +239,6 @@ def rank_program(g, core, T, topo):
             w = C // len(hs)
             for j, h in enumerate(hs):
                 write(h, T.hq[:, 0:w].bitcast(dt.uint8), q[:, j * w:j * w + w].bitcast(dt.uint8), "hc")
-            for j, h in enumerate(hs):
                 write(h, T.hs[:, 0:w], s[:, j * w:j * w + w], "hp")
         else:
             write(dst, T["lq%d" % r][:].bitcast(dt.uint8), q[:].bitcast(dt.uint8), "rf%d" % r)
@@ -264,11 +267,11 @@ def rank_program(g, core, T, topo):
     def bank(b, n):
         return V("ps%d" % (2 + b), 0, n)
 
-    BACK, BACK1 = col("qcol", 2), col("qcol", 3)
+    BACK = col("qcol", 2)
 
     dma("y", "ldx", T.x0[:], T.x[:], [], [V("x0")])
     dma("s", "ldu", T.ut[:], T.u[:], [], [V("ut")])
-    dma("y", "ldw", T.qw[:].bitcast(dt.uint8), T.wc[:], [], [V("qw")])
+    dma("y", "ldw", T.qw[:].bitcast(dt.uint8), T.wc[:], [V("x0"), V("ut")], [V("qw")])
     dma("y", "lds", T.sw[:], T.ws[:], [], [V("sw")])
     dma("y", "ldv", T.vt[:], T.v[:], [], [V("vt")])
 
@@ -293,25 +296,21 @@ def rank_program(g, core, T, topo):
     ts(col("ipc", 1), col("ipc", 0), 15, ALU.bitwise_and)
     ts(V("dg"), V("idg2"), 0.0, ALU.is_equal)
     ts(col("ipc", 2), col("ipc", 0), 4, ALU.arith_shift_right)
-    quant(V("qu"), V("su"), V("ut"))
     cp(V("qcol", 0, 2), V("ipc", 1, 3))
     act(V("mk"), V("dg"), ACT.Identity, bias=-BIG, scale=2 * BIG)
     act(V("d0g", 0, C), V("dg"), ACT.Identity, bias=-DROP, scale=64 * DROP)
     act(V("d0g", C, WW), V("dg", 0, K), ACT.Identity, bias=-DROP, scale=64 * DROP)
+    quant(V("qu"), V("su"), V("ut"))
+    fill(V("seg", 0, C, 16), 0.0)
     op("v", lambda: g.vector.tensor_copy(T.qu2[:, 0:128].bitcast(dt.uint32), T.qu[:, 0:128].bitcast(dt.uint32).indirect(T.offu[:, 0:8])),
        [V("qu"), V("offu")], [V("qu2")])
     cp(V("su2"), V("su"), V("offu"))
-    fill(V("seg", 0, C, 16), 0.0)
-    ts(V("nb"), V("i16"), col("qcol", 0), ALU.subtract, 15.0, ALU.add)
-    ts(BACK, col("qcol", 0), -DROP, ALU.mult, 15 * DROP, ALU.add)
-    ts(V("gt"), V("ig"), col("qcol", 1), ALU.is_equal)
     act(V("tab", 0, A), V("zero", 0, A), ACT.Identity, bias=2.0)
     act(V("tab", A, A + K), V("zero", 0, K), ACT.Identity, bias=1.0)
     act(V("tab", A + K, C), V("zero", 0, A), ACT.Copy)
-    act(col("cf", 0), col("zero", 0), ACT.Copy)
     act(col("cm", 0), col("zero", 0), ACT.Copy)
     act(V("ka"), V("i16", 0, 8), ACT.Identity, bias=col("qcol", 0))
-    act(BACK1, BACK, ACT.Identity, bias=-1.0)
+    act(V("kc"), V("i16", 0, 8), ACT.Identity, bias=float(EL), scale=2.0)
     act(V("kb"), V("ka"), ACT.Identity, bias=0.5)
 
     for r in range(3):
@@ -322,8 +321,11 @@ def rank_program(g, core, T, topo):
         mm(V("ps1", 0, C), V("qu2"), V("su2"), qx, sx)
         if r == 0:
             iota(V("vals", C, 2 * C), [[1, C]], 0, 0, True)
+            iota(V("vals", 0, C), [[1, C]], 0, 0, True)
             iota(V("val3"), [[1, K]], C, 0, True)
-            quant(V("qg"), V("sg"), V("gt"))
+            ts(V("gt"), V("ig"), col("qcol", 1), ALU.is_equal)
+            ts(V("nb"), V("i16"), col("qcol", 0), ALU.subtract, 15.0, ALU.add)
+            ts(BACK, col("qcol", 0), -DROP, ALU.mult, 15 * DROP, ALU.add)
         else:
             for b in range(4):
                 mm(bank(b, C), *eb(b), qx, sx)
@@ -332,6 +334,8 @@ def rank_program(g, core, T, topo):
             quant(V("qv"), V("sv"), V("vt"))
         for lo, hi in ((256, C), (0, 256)):
             tt(V("rm", lo, hi), V("ps0", lo, hi), V("mk", lo, hi), ALU.min)
+            if r == 0 and lo == 0:
+                quant(V("qg"), V("sg"), V("gt"))
             scan(V("wf", lo, hi), V("d0s", lo, hi), V("rm", lo, hi), -BIG, ALU.add, ALU.max)
 
         def compare(c):
@@ -395,43 +399,19 @@ def rank_program(g, core, T, topo):
             act(win(b, 0, C), bank(b, C), ACT.Copy, scale=64.0)
         for b in range(4):
             mm(bank(b, C), *eb(b), V("lq%d" % r), V("ls%d" % r))
-        scatter(V("orow"), V(rw), V("vals", C, 2 * C))
-        cp(V("fr"), V("tab"), V(rw))
-        hold(V("ox"), V("orow", 0, A + K))
-        scan(V("cf", 1, C + 1), V("zero", 0, C), V("fr"), 0.0, ALU.add, ALU.add)
-        ts(V("oa", 0, N1), wrapped("ox"), BACK, ALU.add)
-        ts(V("oa", N1, 2 * N1), wrapped("ox"), BACK, ALU.add, 1.0, ALU.add)
-        for b in range(4):
-            act(V("far", b * C, b * C + C), bank(b, C), ACT.Copy)
         oo = V("oa", 0, N1)
-        act(V("fg"), V("cf", 0, C), ACT.Copy, off=oo)
-        if r == 0:
-            act(V("vals", 0, C), V("vals", C, 2 * C), ACT.Copy)
-        act(V("sval", A + K, C), V("orow", 0, A), ACT.Copy)
 
-        def shared():
-            tt(V("mr"), V("tab"), V("fr"), ALU.min, off=V(lr))
-            ts(V("sh"), V("mr"), 1.0, ALU.min)
-            scan(V("cs"), V("zero", 0, C), V("sh"), 0.0, ALU.add, ALU.add)
+        def keep_far(bs):
+            for b in bs:
+                act(V("far", b * C, b * C + C), bank(b, C), ACT.Copy)
+
+        def in_order():
+            ts(oo, wrapped("ox"), BACK, ALU.add)
+            ts(V("oa", N1, 2 * N1), wrapped("ox"), BACK, ALU.add, 1.0, ALU.add)
 
         def count_s():
-            for c in range(ES):
-                o = 64 * (c // 4)
-                act(V("ej", 256 * c, 256 * c + 256), V("cs", o, o + 256), ACT.Sign, bias=col("kb", c), scale=-1.0, acc=col("ea", 104 * c + 103))
-
-        def count_v():
-            for c in range(ES, 8):
-                ts(V("ec", 208 * c, 208 * c + 208), V("cs", 16 * c, 16 * c + 208), col("kb", c), ALU.is_le, 2.0, ALU.mult)
-            for c in range(ES, 8):
-                scan(V("ea", 104 * c, 104 * c + 104), V("ec", 208 * c, 208 * c + 104), V("ec", 208 * c + 104, 208 * c + 208),
-                     32.0 * c - (384.0 if ES > 4 else 256.0), ALU.add, ALU.add)
-
-        def list_e():
-            if ES > 4:
-                ts(V("eo", 0, 4), V("ea", 103, 4 * 104, 104), 0.5, ALU.mult, 128.0, ALU.add)
-                ts(V("eo", 4, 8), V("ea", 4 * 104 + 103, 8 * 104, 104), 0.5, ALU.mult, 192.0, ALU.add)
-            else:
-                ts(V("eo"), V("ea", 103, 8 * 104, 104), 0.5, ALU.mult, 128.0, ALU.add)
+            for c in range(8):
+                act(V("ej", EL * c, EL * c + EL), V("cs", 16 * c, 16 * c + EL), ACT.Sign, bias=col("kb", c), scale=-1.0, acc=col("ea", c))
 
         def far(q, bs):
             for b in bs:
@@ -453,47 +433,57 @@ def rank_program(g, core, T, topo):
             for b in range(4):
                 mm(bank(b, K), V("qw", 128 * b, 128 * b + 128), V("sw", 128 * b, 128 * b + 128), V("qz"), V("sz"))
 
-        def add():
-            for b in range(4):
-                tt(win(b, C, WW), bank(b, K), V("f64", b, 512, 4), ALU.add)
+        def add(b):
+            tt(win(b, C, WW), bank(b, K), V("f64", b, 512, 4), ALU.add)
 
-        def before():
-            hold(V("fx"), V("fg"))
-            ts(V("f20", 0, N1), wrapped("fx"), BACK, ALU.subtract)
-            ts(V("f20", N1, NC), wrapped("fx", 0, A), BACK, ALU.subtract, 2.0, ALU.add)
+        def split():
+            ts(V("pi"), wrapped("cx"), BACK, ALU.add)
+            ts(col("tot", 0), col("cm", C), -(512.0 * C + 8192.0), ALU.add)
+            ts(V("xi"), V("pi"), 511, ALU.bitwise_and)
+            ts(V("fi"), V("pi", 0, NC), 9, ALU.arith_shift_right)
 
         def copies():
-            tt(V("mw"), wrapped("cx", A + K, WW), wrapped("cx", 0, A + K), ALU.subtract)
-            ts(V("r1"), wrapped("cx", 0, C), -1.0, ALU.mult, col("cm", C), ALU.add)
-            ts(V("ns", 0, N1), V("mw"), 0.5, ALU.is_lt, 8192.0, ALU.mult)
-            ts(V("ns", N1, NC), V("mw", 0, N2), 1.5, ALU.is_lt, 8192.0, ALU.mult)
-            tt(V("r2"), V("r1"), V("f20"), ALU.add)
-            tt(V("t1"), V("ns"), wrapped("cx", 0, C), ALU.add)
-            tt(V("sl"), V("r2"), V("t1"), ALU.min)
-            ts(V("so", 0, N1), V("sl", 0, N1), BACK, ALU.add)
-            ts(V("so", N1, NC), V("sl", N1, NC), BACK1, ALU.add)
+            tt(V("mw"), V("xi", N1, 2 * N1), V("xi", 0, N1), ALU.subtract)
+            ts(V("r1"), V("xi", 0, NC), -1.0, ALU.mult, col("tot", 0), ALU.add)
+            ts(V("ns", 0, N1), V("mw"), 0.5, ALU.is_ge, -8192.0, ALU.mult)
+            ts(V("ns", N1, NC), V("mw", 0, N2), 1.5, ALU.is_ge, -8192.0, ALU.mult)
+            tt(V("r2"), V("r1"), V("fi"), ALU.add)
+            tt(V("t1"), V("ns"), V("xi", 0, NC), ALU.add)
 
-        def slots():
-            scatter(V("nrow"), V("so"), V("sval"))
-            hold(V("nx"), V("nrow"))
-            ts(V("no"), wrapped("nx"), BACK, ALU.add)
+        def offsets():
+            ts(V("so", 0, N1), V("sl", 0, N1), 8192.0, ALU.add)
+            ts(V("so", N1, NC), V("sl", N1, NC), 8191.0, ALU.add)
 
         def new():
             for q, b, lo, hi in LATE:
                 gather(q, V("x1", 64 * lo + b, 64 * hi, 4), win(b, 0, WW), V("no", lo, hi), 0.015625)
 
         steps = {
-            "shared": shared, "count_s": count_s, "count_v": count_v, "e": list_e, "before": before,
-            "sums": lambda: scan(V("cm", 1, C + 1), V("zero", 0, C), V("mr"), 0.0, ALU.add, ALU.add),
+            "orow": lambda: scatter(V("orow"), V(rw), V("vals", C, 2 * C)),
+            "fr": lambda: cp(V("fr"), V("tab"), V(rw)),
+            "frs": lambda: act(V("fr"), V("tab"), ACT.Copy, off=V(rw)),
+            "f512": lambda: act(V("f512"), V("fr"), ACT.Copy, scale=512.0),
+            "ox": lambda: hold(V("ox"), V("orow", 0, A + K)), "oa": in_order,
+            "tfar": lambda: keep_far((0, 1, 2, 3)), "tfa": lambda: keep_far((0, 1, 2)), "tfb": lambda: keep_far((3,)),
+            "sv2": lambda: act(V("sval", A + K, C), V("orow", 0, A), ACT.Copy),
+            "m": lambda: tt(V("mr"), V("tab"), V("fr"), ALU.min, off=V(lr)),
+            "sh": lambda: ts(V("sh"), V("mr"), 1.0, ALU.min),
+            "cs": lambda: scan(V("cs"), V("zero", 0, C), V("sh"), 0.0, ALU.add, ALU.add),
+            "sums": lambda: scan(V("cm", 1, C + 1), V("f512"), V("mr"), 0.0, ALU.add, ALU.add),
+            "count_s": count_s,
+            "e1": lambda: tt(V("ka"), V("ea"), V("kc"), ALU.add), "e2": lambda: ts(V("eo"), V("ka"), 0.5, ALU.mult),
             "far_s": lambda: far("s", (2, 3)), "far_v": lambda: far("v", (0, 1)), "pack_far": pack_far, "near": near,
             "named": lambda: scatter(V("vals", 0, C), V("eo"), V("val3")),
             "values": lambda: act(V("sval", 0, A + K), V("vals", 0, C), ACT.Copy, off=oo),
             "pick_v": lambda: cp(V("cg"), V("cm", 0, C + 1), V("oa")),
             "hold": lambda: hold(V("cx"), V("cg")),
             "near64": lambda: act(V("f64"), V("ft"), ACT.Copy, scale=64.0),
-            "diff": diff, "copies": copies, "add": add, "list": slots, "new": new,
+            "split": split, "copies": copies, "sl": lambda: tt(V("sl"), V("r2"), V("t1"), ALU.min), "so": offsets,
+            "diff": diff, "sc": lambda: scatter(V("nrow"), V("so"), V("sval")), "nx": lambda: hold(V("nx"), V("nrow")),
+            "no": lambda: ts(V("no"), wrapped("nx"), BACK, ALU.add),
+            "a0": lambda: add(0), "a1": lambda: add(1), "a2": lambda: add(2), "a3": lambda: add(3), "new": new,
         }
-        for name in AFTER.split():
+        for name in AFTER[r].split():
             steps[name]()
             if r == 2 and name == "near64":
                 act(V("ntab", 0, C), V("vals", C, 2 * C), ACT.Copy)
@@ -505,14 +495,13 @@ def rank_program(g, core, T, topo):
     H = C // 2
     mm(V("ps0", 0, H), V("qv"), V("sv"), V(qx, 0, H), V(sx, 0, H))
     mm(V("ps1", 0, H), V("qv"), V("sv"), V(qx, H, C), V(sx, H, C))
+    dma("s", "st", T.nl[:, :], T.nlb[0:128:16, :], [V("nlb")], [])
     dma("y", "st", T.oc[:], T[qx][:].bitcast(dt.uint8), [V(qx)], [])
     for k in range(4):
         dma("y", "st", T.osc[4 * k:4 * k + 4, :], T[sx][32 * k:32 * k + 4, :], [V(sx)], [])
     cp(V("ysb", 0, H), V("ps0", 0, H))
     act(V("ysb", H, C), V("ps1", 0, H), ACT.Copy)
     dma("s", "st", T.y[:], T.ysb[:], [V("ysb")], [])
-    for k in range(8):
-        dma("y" if k % 2 else "s", "st", T.nl[k:k + 1, :], T.nlb[16 * k:16 * k + 1, :], [V("nlb")], [])
     for s in SEMAPHORES:
         if total.get(s, 0):
             g.wait_ge(T.sem[s], total[s])

@@ -6,22 +6,29 @@ C, A, K = 320, 96, 128
 STEP = [1, 2, 4]
 NC = C // 16
 N1, N2 = (A + K) // 16, A // 16
-NV = 13
+NV = 14
 WW = C + K
-BIG = 1e25
-DROP = 262144.0
+BIG = 2.0 ** 83
+DROP = 2.0 ** 19
 EL = 2 * A + 16
+EH = EL // 2
+MU = 255.0
+FLAG = 2.0 ** 17
 CODE = "float8_e4m3fn_x4"
 TILES = [([0, 19, 18, 17], 320), ([16, 15, 14, 13], 256), ([12, 11, 10, 9], 192), ([8, 7, 6, 5], 128), ([4, 3, 2, 1], 128)]
 TOFF = [sum(n for _, n in TILES[:k]) for k in range(len(TILES) + 1)]
 RS = 128
 EW = 520
-_END = " far_s far_v pack_far near named values diff near64 sc a0 nx a1 no a2 a3 new"
-_MID = " m sh cs count_s sums pick_v hold split copies e1 sl e2 so"
-AFTER = ["fr f512 orow tfar m ox sh oa cs count_s sums pick_v sv2 hold split copies e1 sl e2 so" + _END,
-         "orow frs f512 ox oa sv2 tfar" + _MID + _END,
-         "orow tfa frs tfb f512 ox oa sv2" + _MID + _END]
-LATE = (("s", 0, 0, 20), ("s", 1, 0, 20), ("v", 2, 0, 20), ("v", 3, 0, 20))
+RANK = ("wf s19 s18 r19 s17 r18 s16 r17 s15 r16 s14 r15 r14 in c13 eq c12 n13 e2 c11 n12 c10 n11 c9 n10 c8 n9 p2 c7 n8 p0 c6 n7 c5 c4 p3 "
+        "c3 n6 c2 n5 c1 p1 p4 t0 t1 t3 n4 n3 n2 n1 e3s e3v cw pd rw places ")
+WAIT = "u0 u1 d0 d3 d1 fq u2 u3 t2 orow f1 d2 ox qf oa "
+POST = ("m z0 sv sh ml cm cs cg k0 z2 k6 k3 cx mq pi k1 hr k2 rr k5 k7 k4 sl e1 z1 so z3 e2o g2 sc sk g3 skh sk1 sk2 g0 fix g1 near qz "
+        "nx a0 no a1 a2 a3 new")
+ORDER = [RANK + WAIT + POST] * 3
+COUNT_V = (0, 1, 2)
+ZG = "ssss"
+TC = "ssss"
+LATE = (("s", 0), ("s", 1), ("v", 2), ("v", 3))
 
 
 def _sb(n, d):
@@ -32,28 +39,27 @@ SCRATCH = {
     "x0": _sb(4 * C, "bfloat16"), "x1": _sb(4 * C, "bfloat16"), "ut": _sb(512, "bfloat16"), "vt": _sb(512, "bfloat16"),
     "qu": _sb(128, CODE), "su": _sb(128, "uint8"),
     "qu2": _sb(128, CODE), "su2": _sb(128, "uint8"), "qv": _sb(128, CODE), "sv": _sb(128, "uint8"),
-    "qw": _sb(512, CODE), "sw": _sb(512, "uint8"), "et": _sb(2 * EW, "bfloat16"),
-    "qe": _sb(512, CODE), "se": _sb(512, "uint8"), "qf": _sb(K, CODE), "sf": _sb(K, "uint8"),
-    "qz": _sb(128, CODE), "sz": _sb(128, "uint8"), "zt": _sb(512, "bfloat16"), "ft": _sb(512, "bfloat16"), "ff": _sb(512, "bfloat16"),
-    "f64": _sb(512, "bfloat16"), "win": _sb(4 * WW, "bfloat16"), "far": _sb(4 * C, "bfloat16"), "ysb": _sb(C, "float32"),
+    "qw": _sb(512, CODE), "sw": _sb(512, "uint8"), "et": _sb(4 * EW, "bfloat16"),
+    "qe": _sb(1024, CODE), "se": _sb(1024, "uint8"), "qf": _sb(C, CODE), "sf": _sb(C, "uint8"),
+    "qz": _sb(K, CODE), "sz": _sb(K, "uint8"), "zt": _sb(4 * K, "bfloat16"), "ff": _sb(4 * C, "bfloat16"),
+    "f64": _sb(4 * K, "bfloat16"), "win": _sb(4 * WW, "bfloat16"), "zw": _sb(4 * C, "bfloat16"), "ysb": _sb(C, "float32"),
     "wt": _sb(4 * TOFF[-1], "bfloat16"), "qt": _sb(TOFF[-1], CODE), "stp": _sb(TOFF[-1], "uint8"),
     "ig": _sb(512, "bfloat16"), "gt": _sb(512, "bfloat16"), "qg": _sb(128, CODE), "sg": _sb(128, "uint8"),
-    "iu": _sb(8, "int32"), "offu": _sb(8, "uint16"), "idg": _sb(C, "int32"), "idg2": _sb(C, "int32"),
+    "iu": _sb(8, "int32"), "offu": _sb(8, "uint16"), "jr": _sb(C, "bfloat16"),
     "ipc": _sb(4, "int32"), "i16": _sb(NC, "float32"), "qcol": _sb(4, "float32"), "ka": _sb(8, "float32"), "kc": _sb(8, "float32"),
-    "kb": _sb(8, "float32"), "vals": _sb(2 * C, "float32"), "val3": _sb(K, "float32"),
-    "dg": _sb(C, "float32"), "mk": _sb(C, "float32"), "d0s": _sb(C, "float32"), "seg": _sb(C, "bfloat16"),
-    "d0g": _sb(WW, "float32"), "nb": _sb(NC, "float32"), "tab": _sb(C, "bfloat16"), "zero": _sb(EW, "bfloat16"),
+    "kb": _sb(8, "bfloat16"), "cols": _sb(C, "float32"), "val3": _sb(K, "float32"),
+    "dg": _sb(C, "bfloat16"), "mk": _sb(C, "bfloat16"), "d0s": _sb(C, "bfloat16"), "seg": _sb(C, "bfloat16"),
+    "d0g": _sb(C, "bfloat16"), "nb": _sb(NC, "float32"), "tab": _sb(C, "bfloat16"), "zero": _sb(EW, "bfloat16"),
     "rm": _sb(C, "float32"), "wf": _sb(C, "float32"), "eqs": _sb(C, "bfloat16"), "e2": _sb(NC, "float32"), "e3": _sb(NC, "float32"),
-    "rk": _sb(NV * RS, "bfloat16"), "pa": _sb(NC, "float32"), "cw": _sb(C, "float32"), "pd": _sb(NC, "float32"),
-    "fr": _sb(C, "bfloat16"), "f512": _sb(C, "bfloat16"), "orow": _sb(C, "float32"), "ox": _sb(A + K, "float32"),
-    "pi": _sb(2 * N1, "int32"), "xi": _sb(2 * N1, "int32"), "fi": _sb(NC, "int32"), "tot": _sb(2, "float32"),
-    "sh": _sb(C, "bfloat16"), "cs": _sb(C, "bfloat16"), "ej": _sb(8 * EL, "bfloat16"),
-    "ea": _sb(8, "float32"), "eo": _sb(8, "uint16"),
-    "mr": _sb(C, "bfloat16"), "cm": _sb(C + 16, "float32"), "cg": _sb(WW, "float32"), "cx": _sb(WW, "float32"),
-    "oa": _sb(2 * N1, "uint16"), "mw": _sb(N1, "float32"),
-    "ns": _sb(NC, "float32"), "r1": _sb(NC, "float32"), "r2": _sb(NC, "float32"), "t1": _sb(NC, "float32"),
-    "sl": _sb(NC, "float32"), "so": _sb(NC, "uint16"), "sval": _sb(C, "float32"), "nrow": _sb(C, "float32"), "nlb": _sb(C, "float32"),
-    "ntab": _sb(WW, "float32"), "nx": _sb(C, "float32"), "no": _sb(NC, "uint16"),
+    "rk": _sb(16 * RS, "bfloat16"), "pa": _sb(NC, "float32"), "cw": _sb(C, "float32"), "pd": _sb(NC, "float32"),
+    "fq": _sb(C, "bfloat16"), "fr": _sb(C, "bfloat16"), "sval": _sb(A + C, "float32"), "ox": _sb(A + K, "float32"),
+    "pi": _sb(NC, "int32"), "hi": _sb(NC, "int32"), "lo": _sb(NC, "int32"), "tot": _sb(2, "float32"),
+    "sh": _sb(C, "bfloat16"), "cs": _sb(C, "bfloat16"), "ej": _sb(8 * EL, "bfloat16"), "er": _sb(8 * EH, "float32"),
+    "eo": _sb(8, "uint16"), "mr": _sb(C, "bfloat16"), "cm": _sb(C + 16, "float32"), "ml": _sb(A + K, "float32"),
+    "cg": _sb(A + K, "float32"), "cx": _sb(A + K, "float32"), "oa": _sb(N1, "uint16"), "rr": _sb(NC, "float32"),
+    "sl": _sb(NC, "float32"), "so": _sb(NC, "uint16"), "nrow": _sb(C, "float32"), "nlb": _sb(C, "float32"),
+    "sk": _sb(K, "float32"), "skx": _sb(K, "float32"), "ski": _sb(8, "int32"), "sko": _sb(8, "uint16"),
+    "nx": _sb(C, "float32"), "no": _sb(NC, "uint16"),
     "hr": _sb(NC, "uint16"), "hq": _sb(C, CODE), "hs": _sb(C, "uint8"),
 }
 for _r in range(4):
@@ -64,7 +70,7 @@ for _r in range(3):
     SCRATCH["lr%d" % _r] = _sb(NC, "uint16")
     SCRATCH["lq%d" % _r] = _sb(C, CODE)
     SCRATCH["ls%d" % _r] = _sb(C, "uint8")
-for _b in range(7):
+for _b in range(8):
     SCRATCH["ps%d" % _b] = ("psum", [128, 512], "float32")
 
 SEMAPHORES = ["cv", "cs", "cp", "cg", "ldx", "ldu", "ldv", "ldw", "lds", "st", "sent", "ha", "hc", "hp",
@@ -120,12 +126,14 @@ def rank_program(g, core, T, topo):
     def cols(v):
         return frozenset([0]) if v[0].startswith("ps") else frozenset(range(v[1], v[2], v[3]))
 
-    def order(q, reads, writes):
+    def order(q, reads, writes, adds=False):
         need = {}
         for vs, wr in ((reads, False), (writes, True)):
             for v in vs:
                 cs_, bank_ = cols(v), v[0].startswith("ps")
                 for (c2, w2, q2, s, n, k) in hist.get(v[0], []):
+                    if adds and wr and q2 == q:
+                        continue
                     if (wr or w2 or (bank_ and q2 != q)) and know[q].get(s, 0) < n and cs_ & c2:
                         if need.get(s, (0, None))[0] < n:
                             need[s] = (n, k)
@@ -146,8 +154,8 @@ def rank_program(g, core, T, topo):
             for v in vs:
                 hist.setdefault(v[0], []).append((cols(v), wr, q, s, total[s], k))
 
-    def op(q, make, reads, writes):
-        order(q, reads, writes)
+    def op(q, make, reads, writes, adds=False):
+        order(q, reads, writes, adds)
         make().then_inc(T.sem[own[q]], 1)
         note(q, own[q], 1, reads, writes)
 
@@ -203,14 +211,14 @@ def rank_program(g, core, T, topo):
             kw["accum_out"] = ap(acc)
         op("s", lambda: g.scalar.activation(ap(out), src(in_, off), f, **kw), [in_] + aps(bias) + aps(off), [out] + aps(acc))
 
-    def gather(q, out, w, off, scale):
+    def move(q, out, w, off=None, scale=1.0):
         if q == "s":
             act(out, w, ACT.Copy, scale=scale, off=off)
         else:
             ts(out, w, scale, ALU.mult, off=off)
 
     def mm(out, lq, ls, rq, rs, start=True, stop=True):
-        op("p", lambda: g.tensor.matmul_mx(ap(out), ap(lq), ap(ls), ap(rq), ap(rs), start, stop), [lq, ls, rq, rs], [out])
+        op("p", lambda: g.tensor.matmul_mx(ap(out), ap(lq), ap(ls), ap(rq), ap(rs), start, stop), [lq, ls, rq, rs], [out], not start)
 
     def iota(out, pattern, base, cm, small=False):
         if small:
@@ -264,6 +272,10 @@ def rank_program(g, core, T, topo):
     def eb(b):
         return V("qe", 128 * b, 128 * b + 128), V("se", 128 * b, 128 * b + 128)
 
+    def cut(b):
+        o = EW * (2 * (b // 4) + b % 2) + 2 - 2 * (b % 4 // 2)
+        quant(*eb(b), V("et", o, o + 512))
+
     def bank(b, n):
         return V("ps%d" % (2 + b), 0, n)
 
@@ -276,42 +288,43 @@ def rank_program(g, core, T, topo):
     dma("y", "ldv", T.vt[:], T.v[:], [], [V("vt")])
 
     iota(V("iu"), [[16, 8]], 0, 0)
-    iota(V("idg"), [[0, NC], [1, 16]], 128, -1)
     iota(col("ipc", 0), [[0, 1]], 0, 1)
+    iota(V("jr"), [[0, NC], [1, 16]], 0, 0, True)
     iota(V("i16"), [[16, NC]], 0, 0, True)
-    iota(V("ig"), [[1, 8], [0, 64]], 0, 0, True)
     fill(V("zero"), 0.0)
+    fill(V("et", 0, 2 * EW), 0.0)
     for h in range(2):
-        o = V("et", h * EW, h * EW + EW)
-        op("g", lambda: g.affine_select(ap(o), ap(V("zero")), [[-1, EW]], ALU.not_equal, 1.0, 2 + h, 4), [V("zero")], [o])
-    fill(V("d0s"), 0.0)
-    fill(col("rk", RS - 1), 0.0)
-    fill(V("d0s", 0, C, 16), -BIG)
+        o, z = V("et", h * EW + 2 + h, h * EW + EW, 4), V("zero", 0, EW // 4)
+        op("g", lambda: g.affine_select(ap(o), ap(z), [[-1, EW // 4]], ALU.not_equal, 1.0, 0, 1), [z], [o])
     for k, (runs, n) in enumerate(TILES):
         a, b = 4 * (TOFF[k] + 16 * runs[-1]), 4 * TOFF[k + 1]
         act(V("wt", a, b), V("zero", 0, b - a), ACT.Copy)
     act(V("seg"), V("zero", 0, C), ACT.Identity, bias=1.0)
+    act(V("d0s"), V("zero", 0, C), ACT.Copy)
     cp(V("offu"), V("iu"))
-    ts(V("idg2"), V("idg"), 15, ALU.bitwise_and)
     ts(col("ipc", 1), col("ipc", 0), 15, ALU.bitwise_and)
-    ts(V("dg"), V("idg2"), 0.0, ALU.is_equal)
     ts(col("ipc", 2), col("ipc", 0), 4, ALU.arith_shift_right)
+    fill(col("rk", RS - 1), 0.0)
     cp(V("qcol", 0, 2), V("ipc", 1, 3))
-    act(V("mk"), V("dg"), ACT.Identity, bias=-BIG, scale=2 * BIG)
-    act(V("d0g", 0, C), V("dg"), ACT.Identity, bias=-DROP, scale=64 * DROP)
-    act(V("d0g", C, WW), V("dg", 0, K), ACT.Identity, bias=-DROP, scale=64 * DROP)
     quant(V("qu"), V("su"), V("ut"))
-    fill(V("seg", 0, C, 16), 0.0)
+    ts(V("mk"), V("jr"), col("qcol", 0), ALU.not_equal, -BIG, ALU.mult)
     op("v", lambda: g.vector.tensor_copy(T.qu2[:, 0:128].bitcast(dt.uint32), T.qu[:, 0:128].bitcast(dt.uint32).indirect(T.offu[:, 0:8])),
        [V("qu"), V("offu")], [V("qu2")])
-    cp(V("su2"), V("su"), V("offu"))
-    act(V("tab", 0, A), V("zero", 0, A), ACT.Identity, bias=2.0)
-    act(V("tab", A, A + K), V("zero", 0, K), ACT.Identity, bias=1.0)
-    act(V("tab", A + K, C), V("zero", 0, A), ACT.Copy)
-    act(col("cm", 0), col("zero", 0), ACT.Copy)
-    act(V("ka"), V("i16", 0, 8), ACT.Identity, bias=col("qcol", 0))
+    act(V("su2"), V("su"), ACT.Copy, off=V("offu"))
+    ts(V("dg"), V("jr"), col("qcol", 0), ALU.is_equal)
+    fill(V("seg", 0, C, 16), 0.0)
+    fill(V("d0s", 0, C, 16), -BIG)
+    iota(V("ig"), [[1, 8], [0, 64]], 0, 0, True)
+    for b in (0, 2, 1, 3):
+        cut(b)
+    ts(V("nb"), V("i16"), col("qcol", 0), ALU.subtract, 15.0, ALU.add)
+    ts(BACK, col("qcol", 0), -DROP, ALU.mult, 15 * DROP, ALU.add)
+    act(V("d0g"), V("dg"), ACT.Identity, bias=-DROP, scale=64 * DROP)
+    act(V("kb"), V("i16", 0, 8), ACT.Identity, bias=col("qcol", 0))
     act(V("kc"), V("i16", 0, 8), ACT.Identity, bias=float(EL), scale=2.0)
-    act(V("kb"), V("ka"), ACT.Identity, bias=0.5)
+    act(col("cm", 0), col("zero", 0), ACT.Copy)
+    act(V("kb"), V("kb"), ACT.Identity, bias=0.5)
+    act(col("qcol", 3), BACK, ACT.Identity, bias=-float(A))
 
     for r in range(3):
         rw, lr, qx, sx = "rw%d" % r, "lr%d" % r, V("qx%d" % r), V("sx%d" % r)
@@ -319,24 +332,27 @@ def rank_program(g, core, T, topo):
         send(r, "codes")
         mm(V("ps0", 0, C), V("qu2"), V("su2"), qx, sx)
         mm(V("ps1", 0, C), V("qu2"), V("su2"), qx, sx)
+        for b in range(4):
+            mm(bank(b, C), *eb(b), qx, sx)
         if r == 0:
-            iota(V("vals", C, 2 * C), [[1, C]], 0, 0, True)
-            iota(V("vals", 0, C), [[1, C]], 0, 0, True)
-            iota(V("val3"), [[1, K]], C, 0, True)
             ts(V("gt"), V("ig"), col("qcol", 1), ALU.is_equal)
-            ts(V("nb"), V("i16"), col("qcol", 0), ALU.subtract, 15.0, ALU.add)
-            ts(BACK, col("qcol", 0), -DROP, ALU.mult, 15 * DROP, ALU.add)
-        else:
-            for b in range(4):
-                mm(bank(b, C), *eb(b), qx, sx)
-            act(V("vals", 0, C), V("vals", C, 2 * C), ACT.Copy)
+            for h in range(2):
+                o = V("et", (h + 2) * EW, (h + 3) * EW)
+                op("g", lambda: g.affine_select(ap(o), ap(V("zero")), [[-1, EW]], ALU.not_equal, -1.0, 2 + h, 4), [V("zero")], [o])
+            iota(V("cols"), [[1, C]], 0, 0, True)
+            iota(V("tab", 0, A), [[0, A]], int(2 * MU), 0, True)
+            iota(V("tab", A, A + K), [[0, K]], int(MU), 0, True)
+            iota(V("tab", A + K, C), [[0, A]], 0, 0, True)
+            iota(V("val3"), [[1, K]], C, 0, True)
         if r == 1:
             quant(V("qv"), V("sv"), V("vt"))
-        for lo, hi in ((256, C), (0, 256)):
-            tt(V("rm", lo, hi), V("ps0", lo, hi), V("mk", lo, hi), ALU.min)
-            if r == 0 and lo == 0:
-                quant(V("qg"), V("sg"), V("gt"))
-            scan(V("wf", lo, hi), V("d0s", lo, hi), V("rm", lo, hi), -BIG, ALU.add, ALU.max)
+
+        def picks():
+            for lo, hi in ((256, C), (0, 256)):
+                tt(V("rm", lo, hi), V("ps0", lo, hi), V("mk", lo, hi), ALU.add)
+                if r == 0 and lo == 0:
+                    quant(V("qg"), V("sg"), V("gt"))
+                scan(V("wf", lo, hi), V("d0s", lo, hi), V("rm", lo, hi), -BIG, ALU.add, ALU.max)
 
         def compare(c):
             ts(slot(c, 0, 16 * c), V("ps0", 0, 16 * c), col("wf", 16 * c + 15), ALU.is_lt)
@@ -350,152 +366,133 @@ def rank_program(g, core, T, topo):
         def sums(c):
             act(slot(c, 0, 16 * c), slot(c, 0, 16 * c), ACT.Relu, acc=col("pa", c))
 
+        packed = []
+
         def pack(k):
             a, b = TOFF[k], TOFF[k + 1]
             quant(V("qt", a, b), V("stp", a, b), V("wt", 4 * a, 4 * b))
+            packed.append(k)
+            if 0 in packed:
+                todo = [k] if k else [0] + packed[:-1]
+                for j in todo:
+                    a, b = TOFF[j], TOFF[j + 1]
+                    mm(V("ps6", 0, b - a), V("qg"), V("sg"), V("qt", a, b), V("stp", a, b), j == 0,
+                       len(packed) == len(TILES) and j == todo[-1])
 
-        sign(NC - 1)
-        for c in range(NC - 1, NV - 1, -1):
-            if c - 1 >= NV:
-                sign(c - 1)
-            sums(c)
-        tt(slot(0, 0, C), V("ps0", 0, C), V("wf"), ALU.is_le)
-        compare(NV - 1)
-        scan(V("eqs"), V("seg"), slot(0, 0, C), 0.0, ALU.mult, ALU.add)
-        for c in range(NV - 1, 6, -1):
-            compare(c - 1)
-            count(c)
-            if c == NV - 1:
-                tt(V("e2"), V("nb"), wrapped("eqs"), ALU.subtract)
-            if c == 9:
-                pack(2)
-            if c == 8:
-                pack(0)
-        for c in (5, 4, 3, 2, 1):
-            compare(c)
-            if c == 4:
-                pack(3)
-        count(6)
-        pack(4)
-        pack(1)
-        for k in (0, 2, 3, 4, 1):
-            a, b = TOFF[k], TOFF[k + 1]
-            mm(V("ps6", 0, b - a), V("qg"), V("sg"), V("qt", a, b), V("stp", a, b), k == 0, k == 1)
-        tt(V("e3", NV, NC), V("e2", NV, NC), V("pa", NV, NC), ALU.subtract)
-        for c in (5, 4, 3, 2, 1):
-            count(c)
-        hold(V("cw"), V("ps6", 0, C))
-        tt(V("e3", 0, NV), V("e2", 0, NV), V("rk", RS - 1, NV * RS, RS), ALU.subtract)
-        tt(V("pd"), V("e3"), wrapped("cw"), ALU.add)
-        ts(V(rw), V("pd"), BACK, ALU.add)
-        send(r, "places")
+        def keep(b):
+            move(TC[b], win(b, 0, C), bank(b, C), None, 64.0)
 
-        if r == 0:
-            for b in range(4):
-                o = EW * (b % 2) + 2 - 2 * (b // 2)
-                quant(*eb(b), V("et", o, o + 512))
-                mm(bank(b, C), *eb(b), qx, sx)
-        for b in range(4):
-            act(win(b, 0, C), bank(b, C), ACT.Copy, scale=64.0)
-        for b in range(4):
-            mm(bank(b, C), *eb(b), V("lq%d" % r), V("ls%d" % r))
-        oo = V("oa", 0, N1)
+        def again(b):
+            mm(bank(b, C), *eb(b), qx, sx, True, False)
 
-        def keep_far(bs):
-            for b in bs:
-                act(V("far", b * C, b * C + C), bank(b, C), ACT.Copy)
-
-        def in_order():
-            ts(oo, wrapped("ox"), BACK, ALU.add)
-            ts(V("oa", N1, 2 * N1), wrapped("ox"), BACK, ALU.add, 1.0, ALU.add)
-
-        def count_s():
-            for c in range(8):
-                act(V("ej", EL * c, EL * c + EL), V("cs", 16 * c, 16 * c + EL), ACT.Sign, bias=col("kb", c), scale=-1.0, acc=col("ea", c))
-
-        def far(q, bs):
-            for b in bs:
-                gather(q, V("ff", b, 512, 4), V("far", b * C, b * C + C), V("eo"), 1.0)
+        def unpack(b):
+            p = V("ps7" if b % 2 == 0 else "ps1", 0, C)
+            mm(p, *eb(b), V("lq%d" % r), V("ls%d" % r))
+            act(V("ff", b, 4 * C, 4), p, ACT.Copy)
 
         def pack_far():
+            if r == 0:
+                for b in range(4, 8):
+                    cut(b)
             quant(V("qf"), V("sf"), V("ff"))
             for b in range(4):
-                mm(bank(b, K), *eb(b), V("qf"), V("sf"))
+                mm(bank(b, C), *eb(4 + b), V("qf"), V("sf"), False, True)
 
-        def near():
-            for b in range(4):
-                gather("s", V("ft", b, 512, 4), win(b, 0, C), V("eo"), 0.015625)
+        def shared(c):
+            e, w, last = V("ej", EL * c, EL * c + EL), V("cs", 16 * c, 16 * c + EL), EH * c + EH - 1
+            if c in COUNT_V:
+                ts(e, w, col("kb", c), ALU.is_lt, 2.0, ALU.mult)
+            else:
+                act(e, w, ACT.Sign, bias=col("kb", c), scale=-1.0, acc=col("er", last))
 
-        def diff():
-            for b in range(4):
-                tt(V("zt", b, 512, 4), V("ft", b, 512, 4), bank(b, K), ALU.subtract)
+        def shared_sum(c):
+            scan(V("er", EH * c, EH * c + EH), V("ej", EL * c, EL * c + EH), V("ej", EL * c + EH, EL * c + EL), -float(EL), ALU.add, ALU.add)
+
+        def counts(c):
+            if c in COUNT_V and c - 1 in COUNT_V:
+                shared(c)
+                shared_sum(c - 1)
+            else:
+                shared(c)
+            if c in COUNT_V and c + 1 not in COUNT_V:
+                shared_sum(c)
+
+        def product():
             quant(V("qz"), V("sz"), V("zt"))
             for b in range(4):
                 mm(bank(b, K), V("qw", 128 * b, 128 * b + 128), V("sw", 128 * b, 128 * b + 128), V("qz"), V("sz"))
 
-        def add(b):
-            tt(win(b, C, WW), bank(b, K), V("f64", b, 512, 4), ALU.add)
+        def near():
+            for b in range(4):
+                move("s", V("f64", b * K, b * K + K), win(b, 0, C), V("eo"))
 
-        def split():
-            ts(V("pi"), wrapped("cx"), BACK, ALU.add)
-            ts(col("tot", 0), col("cm", C), -(512.0 * C + 8192.0), ALU.add)
-            ts(V("xi"), V("pi"), 511, ALU.bitwise_and)
-            ts(V("fi"), V("pi", 0, NC), 9, ALU.arith_shift_right)
+        def whole():
+            ts(V("pi", 0, N2), wrapped("cx", 0, A), BACK, ALU.add, FLAG + 256.0, ALU.add)
+            ts(V("pi", N2, 2 * N2), wrapped("cx", 0, A), BACK, ALU.add, 1.0, ALU.add)
+            ts(V("pi", 2 * N2, NC), wrapped("cx", A, A + K), BACK, ALU.add)
 
-        def copies():
-            tt(V("mw"), V("xi", N1, 2 * N1), V("xi", 0, N1), ALU.subtract)
-            ts(V("r1"), V("xi", 0, NC), -1.0, ALU.mult, col("tot", 0), ALU.add)
-            ts(V("ns", 0, N1), V("mw"), 0.5, ALU.is_ge, -8192.0, ALU.mult)
-            ts(V("ns", N1, NC), V("mw", 0, N2), 1.5, ALU.is_ge, -8192.0, ALU.mult)
-            tt(V("r2"), V("r1"), V("fi"), ALU.add)
-            tt(V("t1"), V("ns"), V("xi", 0, NC), ALU.add)
+        def parts():
+            ts(V("hi"), V("pi"), 8, ALU.arith_shift_right, 1535, ALU.bitwise_and)
+            ts(V("lo"), V("pi"), 255, ALU.bitwise_and)
 
-        def offsets():
-            ts(V("so", 0, N1), V("sl", 0, N1), 8192.0, ALU.add)
-            ts(V("so", N1, NC), V("sl", N1, NC), 8191.0, ALU.add)
+        def name_updated():
+            if r == 2:
+                act(V("nlb"), V("nrow"), ACT.Copy)
+                dma("y", "st", T.nl[:, :], T.nlb[0:128:16, :], [V("nlb")], [])
+            scatter(V("nrow"), V("sko"), V("val3"))
 
         def new():
-            for q, b, lo, hi in LATE:
-                gather(q, V("x1", 64 * lo + b, 64 * hi, 4), win(b, 0, WW), V("no", lo, hi), 0.015625)
+            for q, b in LATE:
+                move(q, V("x1", b, 4 * C, 4), win(b, 0, WW), V("no"), 0.015625)
 
         steps = {
-            "orow": lambda: scatter(V("orow"), V(rw), V("vals", C, 2 * C)),
-            "fr": lambda: cp(V("fr"), V("tab"), V(rw)),
-            "frs": lambda: act(V("fr"), V("tab"), ACT.Copy, off=V(rw)),
-            "f512": lambda: act(V("f512"), V("fr"), ACT.Copy, scale=512.0),
-            "ox": lambda: hold(V("ox"), V("orow", 0, A + K)), "oa": in_order,
-            "tfar": lambda: keep_far((0, 1, 2, 3)), "tfa": lambda: keep_far((0, 1, 2)), "tfb": lambda: keep_far((3,)),
-            "sv2": lambda: act(V("sval", A + K, C), V("orow", 0, A), ACT.Copy),
-            "m": lambda: tt(V("mr"), V("tab"), V("fr"), ALU.min, off=V(lr)),
+            "wf": picks, "in": lambda: tt(slot(0, 0, C), V("ps0", 0, C), V("wf"), ALU.is_le),
+            "eq": lambda: scan(V("eqs"), V("seg"), slot(0, 0, C), 0.0, ALU.mult, ALU.add),
+            "e2": lambda: tt(V("e2"), V("nb"), wrapped("eqs"), ALU.subtract),
+            "e3s": lambda: tt(V("e3", NV, NC), V("e2", NV, NC), V("pa", NV, NC), ALU.subtract),
+            "e3v": lambda: tt(V("e3", 0, NV), V("e2", 0, NV), V("rk", RS - 1, NV * RS, RS), ALU.subtract),
+            "cw": lambda: hold(V("cw"), V("ps6", 0, C)), "pd": lambda: tt(V("pd"), V("e3"), wrapped("cw"), ALU.add),
+            "rw": lambda: ts(V(rw), V("pd"), BACK, ALU.add), "places": lambda: send(r, "places"),
+            "orow": lambda: scatter(V("sval", A, A + C), V(rw), V("cols")),
+            "fq": lambda: act(V("fq"), V("tab"), ACT.Copy, off=V(rw)), "fqv": lambda: cp(V("fq"), V("tab"), V(rw)),
+            "f1": lambda: ts(V("fr"), V("fq"), 1.0 / MU, ALU.mult),
+            "ox": lambda: hold(V("ox"), V("sval", A, 2 * A + K)), "oa": lambda: ts(V("oa"), wrapped("ox"), BACK, ALU.add),
+            "sv": lambda: cp(V("sval", 0, A), V("sval", A, 2 * A)), "qf": pack_far,
+            "m": lambda: tt(V("mr"), V("tab"), V("fq"), ALU.min, off=V(lr)),
             "sh": lambda: ts(V("sh"), V("mr"), 1.0, ALU.min),
             "cs": lambda: scan(V("cs"), V("zero", 0, C), V("sh"), 0.0, ALU.add, ALU.add),
-            "sums": lambda: scan(V("cm", 1, C + 1), V("f512"), V("mr"), 0.0, ALU.add, ALU.add),
-            "count_s": count_s,
-            "e1": lambda: tt(V("ka"), V("ea"), V("kc"), ALU.add), "e2": lambda: ts(V("eo"), V("ka"), 0.5, ALU.mult),
-            "far_s": lambda: far("s", (2, 3)), "far_v": lambda: far("v", (0, 1)), "pack_far": pack_far, "near": near,
-            "named": lambda: scatter(V("vals", 0, C), V("eo"), V("val3")),
-            "values": lambda: act(V("sval", 0, A + K), V("vals", 0, C), ACT.Copy, off=oo),
-            "pick_v": lambda: cp(V("cg"), V("cm", 0, C + 1), V("oa")),
-            "hold": lambda: hold(V("cx"), V("cg")),
-            "near64": lambda: act(V("f64"), V("ft"), ACT.Copy, scale=64.0),
-            "split": split, "copies": copies, "sl": lambda: tt(V("sl"), V("r2"), V("t1"), ALU.min), "so": offsets,
-            "diff": diff, "sc": lambda: scatter(V("nrow"), V("so"), V("sval")), "nx": lambda: hold(V("nx"), V("nrow")),
-            "no": lambda: ts(V("no"), wrapped("nx"), BACK, ALU.add),
-            "a0": lambda: add(0), "a1": lambda: add(1), "a2": lambda: add(2), "a3": lambda: add(3), "new": new,
+            "cm": lambda: scan(V("cm", 1, C + 1), V("fr"), V("mr"), 0.0, ALU.add, ALU.add),
+            "ml": lambda: act(V("ml"), V("mr"), ACT.Identity, bias=2 * FLAG, scale=-FLAG / MU, off=V("oa")),
+            "cg": lambda: tt(V("cg"), V("cm", 0, C), V("ml"), ALU.add, off=V("oa")), "cx": lambda: hold(V("cx"), V("cg")),
+            "pi": whole, "hr": parts,
+            "mq": lambda: ts(col("tot", 0), col("cm", C), MU / 4 - C, ALU.add, 1.0 / MU, ALU.mult),
+            "rr": lambda: ts(V("rr"), V("lo"), col("tot", 0), ALU.add),
+            "sl": lambda: tt(V("sl"), V("rr"), V("hi"), ALU.min), "so": lambda: cp(V("so"), V("sl")),
+            "sc": lambda: scatter(V("nrow"), V("so"), V("sval", 0, C)),
+            "e1": lambda: tt(V("ka"), V("er", EH - 1, 8 * EH, EH), V("kc"), ALU.add), "e2o": lambda: ts(V("eo"), V("ka"), 0.5, ALU.mult),
+            "sk": lambda: act(V("sk"), V("cm", 0, C), ACT.Copy, off=V("eo")), "skv": lambda: cp(V("sk"), V("cm", 0, C), V("eo")),
+            "skh": lambda: hold(V("skx"), V("sk")),
+            "sk1": lambda: ts(V("ski"), wrapped("skx"), col("qcol", 3), ALU.add, 2.0 ** -8, ALU.mult),
+            "sk2": lambda: cp(V("sko"), V("ski")), "fix": name_updated,
+            "near": near, "qz": product, "nx": lambda: hold(V("nx"), V("nrow")),
+            "no": lambda: ts(V("no"), wrapped("nx"), BACK, ALU.add), "new": new,
         }
-        for name in AFTER[r].split():
-            steps[name]()
-            if r == 2 and name == "near64":
-                act(V("ntab", 0, C), V("vals", C, 2 * C), ACT.Copy)
-                act(V("ntab", C, WW), V("vals", C, 2 * C), ACT.Copy, off=V("eo"))
+        each = {"s": sign, "r": sums, "c": compare, "n": count, "p": pack, "t": keep, "d": again, "u": unpack, "k": counts,
+                "z": lambda b: act(V("zw", b * C, b * C + C), bank(b, C), ACT.Copy),
+                "y": lambda b: cp(V("zw", b * C, b * C + C), bank(b, C)),
+                "g": lambda b: move(ZG[b], V("zt", b, 4 * K, 4), V("zw", b * C, b * C + C), V("eo")),
+                "a": lambda b: tt(win(b, C, WW), bank(b, K), V("f64", b * K, b * K + K), ALU.add)}
+        for name in ORDER[r].split():
+            if name in steps:
+                steps[name]()
+            else:
+                each[name[0]](int(name[1:]))
 
-    act(V("nlb"), V("ntab"), ACT.Copy, off=V("no"))
     qx, sx = "qx3", "sx3"
     quant(V(qx), V(sx), V("x1"))
     H = C // 2
     mm(V("ps0", 0, H), V("qv"), V("sv"), V(qx, 0, H), V(sx, 0, H))
     mm(V("ps1", 0, H), V("qv"), V("sv"), V(qx, H, C), V(sx, H, C))
-    dma("s", "st", T.nl[:, :], T.nlb[0:128:16, :], [V("nlb")], [])
     dma("y", "st", T.oc[:], T[qx][:].bitcast(dt.uint8), [V(qx)], [])
     for k in range(4):
         dma("y", "st", T.osc[4 * k:4 * k + 4, :], T[sx][32 * k:32 * k + 4, :], [V(sx)], [])

@@ -6,7 +6,7 @@ C, A, K = 320, 96, 128
 STEP = [1, 2, 4]
 NC = C // 16
 N1, N2 = (A + K) // 16, A // 16
-NV = 14
+NV = 13
 WW = C + K
 BIG = 2.0 ** 83
 DROP = 2.0 ** 19
@@ -19,15 +19,101 @@ TILES = [([0, 19, 18, 17], 320), ([16, 15, 14, 13], 256), ([12, 11, 10, 9], 192)
 TOFF = [sum(n for _, n in TILES[:k]) for k in range(len(TILES) + 1)]
 RS = 128
 EW = 520
-RANK = ("wf s19 s18 r19 s17 r18 s16 r17 s15 r16 s14 r15 r14 in c13 eq c12 n13 e2 c11 n12 c10 n11 c9 n10 c8 n9 p2 c7 n8 p0 c6 n7 c5 c4 p3 "
-        "c3 n6 c2 n5 c1 p1 p4 t0 t1 t3 n4 n3 n2 n1 e3s e3v cw pd rw places ")
-WAIT = "u0 u1 d0 d3 d1 fq u2 u3 t2 orow f1 d2 ox qf oa "
-POST = ("m z0 sv sh ml cm cs cg k0 z2 k6 k3 cx mq pi k1 hr k2 rr k5 k7 k4 sl e1 z1 so z3 e2o g2 sc sk g3 skh sk1 sk2 g0 fix g1 near qz "
-        "nx a0 no a1 a2 a3 new")
-ORDER = [RANK + WAIT + POST] * 3
-COUNT_V = (0, 1, 2)
+ORDER = [
+    "ip zero iu qcol offu b2 et jr dg back mk qu b1 seg ig qu2 one1 d0s gt one0 x1 x3 x0 qx b3 su2 i16 q7 wa q1 b0 q0 b4 val3 cols qg d0g "
+    "small nb s19 x2 wb s18 in r19 c12 s17 eq r18 c11 n12 s16 codes r17 c10 rk s15 r16 s14 n11 w1 c9 w3 r15 n10 c8 n9 s13 c7 tab n8 c6 r14 "
+    "n7 c5 w0 p2 n6 p0 c4 r13 c3 n5 t0 w2 c2 neg1 p3 c1 n3 neg0 p4 t2 p1 n4 e2 n2 n1 t1 e3s e3v cw pd rw x7 u1 x5 u0 places d0 x6 t3 d2 u3 "
+    "orow d1 x4 u2 d3 fq qf sv z0 ox f1 z1 m oa sh cm ml cs cg mq k0 cx pi hr k1 k7 k4 k5 rr k6 k2 sl k3 z2 z3 e1 so e2o sk g2 sc skh g1 "
+    "sk1 g3 g0 j0 fix qz nx j2 a0 j1 no j3 a2 a1 a3 new",
+    "qx q7 q0 wa codes q1 wb s19 w0 s18 r19 s17 in c12 eq c11 w3 n12 c10 n11 r18 e2 w1 s16 c9 r17 n10 c8 n9 p2 s15 c7 n8 c6 r16 s14 n7 r15 "
+    "s13 c5 n6 w2 c4 c3 r14 n5 n4 p0 r13 c2 c1 t1 p3 t2 p4 n2 p1 e3s d1 t0 n1 t3 u1 n3 u0 e3v cw d0 u3 pd rw u2 d2 qv orow fq d3 ox qf "
+    "places sv z1 f1 z2 oa m z3 sh cm ml mq cs k5 cg cx k6 k0 pi hr k4 k3 rr k1 k2 sl k7 e1 so z0 e2o g1 sc g2 sk g0 j1 skh g3 j2 sk1 fix "
+    "j0 j3 qz nx a0 a1 a2 no a3 new",
+    "qx q7 q1 wa s19 s18 r19 q0 s17 r18 s16 r17 wb w1 in c12 s15 eq c11 r16 n12 codes c10 n11 s14 c9 r15 n10 w2 s13 p2 w3 p0 c8 n9 c7 w0 n8 "
+    "c6 n7 c5 r14 n6 r13 c4 c3 t2 n5 t3 c2 e2 c1 u1 u0 p3 p4 p1 n3 n1 n2 n4 t1 e3s e3v cw u3 pd rw places d3 u2 t0 d1 d2 d0 orow qf fq sv "
+    "ox z0 oa f1 z1 m sh cm cs ml cg z2 k6 k2 cx pi mq hr k4 k0 rr k5 k7 k1 k3 sl e1 so z3 e2o sk g2 sc g1 skh g3 sk1 fix g0 qz nx j0 j3 "
+    "a0 no j2 j1 a2 a1 a3 l1 l0 o1 o0 osc"]
+ORDER = [
+    "ip ig zero et rk d0s b3 qcol seg b0 gt jr iu one1 qu dg b2 mk i16 back d0g offu qg x3 su2 one0 x1 b4 qu2 b1 x2 nb qx x0 small q7 "
+    "wa codes cols q0 q1 wb s19 in c13 eq w2 s18 c12 n13 r19 c11 n12 c10 n11 tab s17 r18 s16 c9 n10 r17 c8 w1 s15 n9 c7 p2 e2 n8 w3 c6 "
+    "r16 n7 s14 c5 n6 w0 r15 r14 c4 c3 p0 t3 n5 c2 c1 p3 p4 neg0 p1 neg1 t0 t1 d0 n2 n3 t2 n4 d1 u1 n1 e3s x6 e3v u0 cw x5 pd x4 rw x7 "
+    "u3 u2 fqv d3 places d2 orow f1 ox qf m svg oa sh z0 cm ml z2 cs mqv cg k5 k4 k1 cx v1 pi k2 k7 hr k3 k6 k0 v2 val3 rr v0 z3 sl e1 "
+    "so z1 e2o sk g3 sc skh g0 sk1 g1 fix g2 j0 j2 qz j1 nx j3 a0 no a2 a1 a3 new ",
+    "qx q7 q0 wa q1 codes wb in c13 s19 eq s18 c12 r19 n13 s17 c11 w3 n12 w0 c10 r18 n11 c9 s16 n10 r17 c8 n9 s15 c7 r16 w2 s14 n8 p2 "
+    "r15 c6 n7 c5 n6 c4 c3 r14 n5 p0 c2 c1 p3 p4 t0 p1 w1 t2 t3 d2 d3 n1 t1 n2 d0 n3 e2 n4 e3s cw e3v u0 pd u1 rw d1 orow fqv u2 ox f1 "
+    "qv u3 places oa qf m sh z0 cm ml cs mqv z1 cg k7 k0 k1 cx v1 svg pi v0 k6 hr k2 k5 k4 rr k3 z2 v2 sl e1 z3 so e2o sk sc g2 skh sk1 "
+    "g1 g3 fix g0 j0 j1 qz j2 nx j3 a0 a1 no a2 a3 new ",
+    "qx q7 q0 codes wa q1 wb s19 in c13 s18 eq r19 c12 s17 n13 r18 c11 n12 s16 c10 n11 r17 s15 c9 w1 r16 n10 c8 n9 s14 c7 n8 c6 n7 p2 "
+    "w3 r15 c5 w0 e2 n6 r14 c4 p0 c3 n5 t1 n3 c2 c1 p3 p4 p1 t3 e3s t0 w2 n1 t2 n4 u0 u1 d1 n2 e3v cw u2 pd u3 d0 d2 d3 rw fqv orow qf "
+    "places ox m oa z0 sh f1 z1 cs cm ml svg k1 k4 cg k3 mqv k2 cx k5 k0 k7 pi v1 v2 hr v0 z3 k6 rr e1 sl e2o so z2 g1 sc g2 g0 g3 qz "
+    "sk skh sk1 fix j0 a0 nx j1 a1 j3 j2 a2 no a3 l1 ocb l0 oca i0 i2 o1 i1 i3 o0 yb ya "]
+ORDER = [
+    "zero d0s seg et iu ip ig one0 b0 b2 qcol gt qg offu jr qu x2 b1 qu2 one1 rk x0 dg x3 mk su2 qx q7 x1 wa i16 codes q0 wb q1 tab nb b4 "
+    "back in c13 small eq d0g b3 w1 c12 s19 n13 s18 c11 n12 cols r19 w2 s17 c10 neg1 r18 n11 c9 neg0 n10 w0 c8 s16 n9 r17 c7 p2 p0 n8 c6 "
+    "s15 n7 c5 n6 c4 w3 r16 c3 s14 val3 n5 r15 c2 r14 t2 c1 e2 t1 p3 t3 p4 p1 n4 n1 n3 t0 n2 u0 e3s e3v cw pd u1 rw d1 x6 places u2 orow "
+    "u3 x5 d2 ox x7 d0 x4 d3 fq qf oa m z0 f1 ml sh cm cs cg svg k1 z1 cx k0 pi k2 hr v1 k7 v0 k6 k5 k4 mq rr v2 k3 z2 sl e1 so z3 e2o "
+    "g1 sk g3 sc skh g2 g0 j1 j0 j2 j3 sk1 fix qz nx a0 a1 no a2 a3 new",
+    "qx q7 codes wa q0 wb q1 s19 in c13 eq c12 n13 c11 n12 s18 r19 c10 n11 c9 w1 n10 c8 p2 n9 s17 c7 w2 r18 s16 n8 w0 r17 c6 s15 n7 c5 w3 "
+    "n6 p0 c4 r16 c3 n5 s14 c2 c1 p3 p4 r15 r14 t0 n1 p1 e2 t1 n3 n4 n2 e3s d0 t2 e3v t3 cw d1 d2 pd rw qv fq d3 u0 orow u1 u2 f1 u3 ox "
+    "places oa qf z0 z1 m sh cm ml mq cs cg k1 cx k7 k0 pi k2 hr k6 v1 k3 k4 k5 v2 svg rr z2 v0 sl e1 so e2o z3 sc g2 sk g0 g1 skh g3 j0 "
+    "j1 sk1 fix j2 qz nx a0 no a1 j3 a2 a3 new",
+    "qx q7 codes wa q0 wb in c13 eq c12 q1 n13 s19 c11 n12 c10 w2 n11 s18 r19 s17 c9 n10 c8 n9 w3 r18 c7 p2 s16 w0 n8 r17 c6 w1 n7 s15 "
+    "r16 s14 c5 r15 n6 p0 c4 c3 n5 c2 r14 t3 t1 c1 p3 p4 p1 t2 e2 u0 n4 n1 n2 e3s n3 u1 t0 d1 cw e3v u2 u3 pd d2 rw d3 places fq d0 orow "
+    "ox qf oa z0 f1 m sh z1 cm cs ml cg k2 z2 cx k5 k6 k3 k0 mq svg k1 pi v1 k7 hr k4 v0 rr v2 z3 sl e1 so e2o sk sc skh g0 g2 g1 sk1 "
+    "fix g3 qz nx j0 j3 a0 j1 no j2 a1 a2 a3 last oc i0 i1 i2 i3 o0 o1 y"]
+ORDER = [
+    "et zero ig ip qcol jr iu one0 b1 d0s i16 qu gt b0 b4 dg b2 mk one1 offu x0 x2 su2 qu2 qx x1 q7 q0 q1 x3 back w2 wa neg0 codes wb w3 "
+    "seg w1 qg b3 c11 rk c1 d0g s19 c10 c9 in c12 s17 c4 s18 p2 c8 c2 s13 c6 s15 s14 r15 r18 nb r19 n12 r17 neg1 n9 cols n11 s16 r13 w0 "
+    "eq c5 n10 r16 c3 c7 p0 p3 n8 tab n6 n4 n7 r14 p4 p1 n3 n1 n2 t1 e2 t3 t2 t0 n5 u0 x5 e3s e3v cw u1 small d2 pd u2 rw u3 x7 orow x4 "
+    "d3 d0 places fq sv ox d1 x6 val3 qf oa z0 f1 m sh ml cm cs z1 cg k5 k0 k7 cx k1 pi hr k6 v0 k3 mq k2 rr k4 v1 sl z3 z2 so e1 e2o sk "
+    "g1 sc g0 g2 skh g3 j2 sk1 fix j0 j3 j1 qz nx a0 no a2 a3 a1 new",
+    "qx q7 q0 q1 wa s16 codes s19 w2 s18 s17 wb r19 c3 s13 c12 c1 c5 r17 c8 c7 c2 c9 c11 n1 c4 s15 w0 r16 n3 w3 in c10 n4 n9 r13 c6 r18 "
+    "s14 r15 n2 p2 r14 eq w1 t1 n8 p0 e2 n7 p3 p4 p1 n10 n12 n6 t0 t3 n5 t2 n11 u0 e3s u1 d0 e3v cw u2 pd u3 d2 d3 rw orow ox fq qv d1 "
+    "places qf oa sv f1 z0 m sh cm z2 cs ml cg k2 cx k1 k6 k0 pi hr k5 mq v1 k3 k7 rr k4 z3 v0 z1 sl e1 so e2o sk sc g2 g1 g0 g3 skh sk1 "
+    "fix qz nx j2 j1 j0 a1 j3 a2 no a0 a3 new",
+    "qx q7 q1 q0 wa s18 s16 s19 codes wb c11 s17 w1 c4 c10 s13 c3 c1 s15 s14 c12 n1 c7 w2 r15 r18 c9 c2 r17 c8 w3 in r19 p2 c5 eq r14 n2 "
+    "w0 n9 r13 c6 p0 p3 n3 n7 p4 r16 p1 n8 t0 n12 e2 t1 t3 t2 n11 n10 u0 u1 n5 n4 d0 n6 d2 u2 cw e3v u3 e3s d3 pd rw d1 orow places ox "
+    "qf fq sv oa f1 m z0 sh ml z2 cm cs cg cx k3 mq k6 k0 k2 pi k4 k1 hr k5 k7 rr v1 v0 sl z3 e1 so z1 e2o sc sk g0 skh g2 sk1 fix g1 g3 "
+    "j0 qz nx j2 a0 j3 no j1 a2 a3 a1 last i2 o0 o1 y oc i0 i1 i3"]
+ORDER = [
+    "ip et ig iu zero qcol jr one0 gt b1 offu qu seg qu2 i16 one1 d0s mk dg b3 su2 b0 cols x2 x0 qx val3 d0g q7 x3 wa b2 q1 rk b4 codes qg "
+    "back s18 neg0 s16 neg1 q0 wb s17 nb x1 c2 c4 c9 s19 c5 r17 in c1 c10 c8 c12 s14 w1 s15 c7 s13 c11 tab w0 w2 r14 eq c6 c3 n2 n6 n7 "
+    "r18 r19 w3 r13 r15 p2 r16 p0 n11 p3 n4 small t3 p4 n3 t2 p1 t0 u0 n1 e2 n10 u1 n9 n8 d0 u2 n12 n5 u3 t1 e3v e3s cw pd rw x5 places "
+    "d2 x6 x4 d3 x7 d1 orow qf ox fq oa m f1 sh cm sv cs z0 ml z1 mq k7 cg k3 k2 k1 cx pi k0 k5 k4 hr k6 v0 z3 rr v1 z2 sl e1 so e2o sk "
+    "sc g2 g3 skh sk1 g0 fix g1 j3 j0 j2 qz j1 nx no a0 a3 a2 a1 new",
+    "qx q7 codes q0 q1 wa s17 wb s16 c1 c9 s19 c5 c2 s14 c4 c11 c10 s18 in s13 c6 eq r18 c3 r19 w2 n11 r14 n1 w1 n5 c12 r17 s15 n2 n4 w3 "
+    "c8 r16 w0 r15 n10 r13 c7 t0 p2 t1 n3 p0 t2 p3 n7 n8 n9 t3 p4 p1 n6 u0 u1 n12 e2 e3s d2 u2 u3 d3 e3v cw d0 pd d1 rw orow sv places qv "
+    "ox qf fq oa f1 m sh z0 cs z2 cm ml k5 cg k1 cx k0 k6 k4 mq pi hr k7 k3 k2 v1 rr v0 sl z1 z3 e1 so e2o sk sc g3 skh g1 g0 sk1 fix g2 "
+    "qz nx j3 no j0 a0 a3 j2 j1 a2 a1 new",
+    "qx q7 wa q1 codes s19 q0 wb c8 s18 c1 s17 c3 w3 c10 s14 s15 c2 c11 s16 s13 w0 c9 r16 w2 c7 n10 r17 n3 n8 in c12 w1 c6 r18 c5 c4 r19 "
+    "eq p2 n2 r14 n1 e2 r13 p0 r15 t1 n11 p3 p4 n5 t0 t3 p1 n4 n9 n6 n12 e3s t2 n7 e3v u0 d1 u1 cw pd d2 u2 rw u3 orow d3 fq d0 sv qf z0 "
+    "places ox oa f1 m z1 sh ml cm cs cg z2 k0 cx k1 pi k4 k5 k6 mq v0 k2 hr rr v1 k3 sl k7 so e1 z3 e2o sc sk g1 skh g2 sk1 fix g3 g0 j3 "
+    "qz nx no j0 a0 a3 j2 j1 a2 a1 last o0 oc i2 o1 y i3 i0 i1"]
+ORDER = [
+    "ip zero d0s ig qcol et iu gt jr qu offu b2 one0 qg b3 qu2 seg one1 b1 mk su2 b0 qx dg q7 back neg0 x3 wa i16 q0 codes q1 wb x0 b4 rk "
+    "d0g w3 s18 s17 s19 c12 c9 c10 s15 neg1 s16 x1 c11 c8 c3 c5 in x2 c2 w0 cols r15 eq w1 r18 nb r17 s13 n8 p2 c1 c7 r19 w2 c4 p0 c6 n5 "
+    "tab n9 n3 p3 r13 s14 e2 r16 p4 r14 t2 p1 t3 n1 val3 n12 e3s t1 n7 x4 n6 n11 u0 n4 u1 n2 d1 n10 cw e3v x7 pd x6 rw x5 t0 orow u2 u3 "
+    "d0 fq d2 places d3 sv qf ox m small oa f1 sh z0 cm ml z1 mq cs k5 k2 cg k1 k7 k6 k4 cx k0 pi k3 z2 v0 hr v1 rr sl e1 so e2o sc z3 sk "
+    "skh sk1 g1 g0 g3 g2 j3 fix j1 qz nx j0 no a0 j2 a1 a2 a3 new",
+    "qx q7 wa q0 codes q1 s17 wb c1 w0 c9 c2 s16 c6 c5 c7 s18 w3 n6 s14 c12 n9 s19 w1 c11 c3 s15 n12 r19 w2 c8 r18 n2 n7 qv c10 r17 r16 in "
+    "c4 p2 s13 p0 r14 n8 r13 r15 n3 eq p3 t0 t1 n1 n5 e2 t2 t3 p1 d1 u0 n10 n11 n4 e3v e3s cw u1 u2 u3 d0 d3 pd rw orow ox d2 qf fq places "
+    "oa f1 m sh sv z0 ml cm z2 cs cg k3 k1 k2 cx k0 pi v1 hr mq k7 k6 rr v0 k5 k4 sl e1 so z3 e2o z1 sk sc g0 skh sk1 g1 fix g2 g3 qz nx "
+    "j3 no j1 j0 j2 a0 a1 a2 a3 new",
+    "qx codes q7 q1 wa q0 s16 wb s19 s17 s18 s15 c11 c10 c9 in r18 r19 s14 c6 r17 c12 n9 c7 c5 w1 n7 c3 w0 w3 p2 w2 n11 c1 c8 s13 p0 r14 c4 "
+    "c2 eq r15 n10 r16 r13 n1 p3 t2 t0 p1 n5 n4 n2 n6 t1 n8 n3 u0 e2 n12 u1 e3s t3 e3v cw d0 u2 pd rw u3 orow places fq d1 d2 d3 sv qf ox m "
+    "oa f1 z0 sh cm ml cs z2 mq k3 cg k0 cx k1 pi v0 hr k5 k2 k6 k4 rr v1 k7 z3 sl e1 so z1 e2o sk sc skh g2 sk1 g0 fix g1 g3 qz j3 j0 j2 "
+    "j1 nx a0 no a2 a3 a1 last oc o0 i2 i0 o1 i1 y i3"]
+COUNT_V = (0, 1)
 ZG = "ssss"
 TC = "ssss"
+NG = "ssss"
+YC, YQ, OSQ = "vv", "sy", "yyss"
+FEW, SENDS = 128, "s10"
+UC = ["ssss", "ssss", "ssss"]
+INORDER = False
+EARLY = True
+QX = ((C - K, C), (0, C - K))
+PICKS = ((256, C), (0, 256))
 LATE = (("s", 0), ("s", 1), ("v", 2), ("v", 3))
 
 
@@ -85,6 +171,10 @@ def _helpers(T, topo, src, dst):
     return (near or c)[:2]
 
 
+def _share(j, n):
+    return (0, C) if n == 1 else ((0, FEW), (FEW, C))[j]
+
+
 def _hand_on(g, core, T, topo):
     for r, h in enumerate(STEP):
         for i, src in enumerate(T.cores):
@@ -92,18 +182,22 @@ def _hand_on(g, core, T, topo):
             hs = _helpers(T, topo, src, dst)
             if core not in hs:
                 continue
-            j, w = hs.index(core), C // len(hs)
+            j = hs.index(core)
+            lo, hi = _share(j, len(hs))
             n_in, n, m = len(topo.engines(src, core)), len(topo.engines(core, dst)), topo.mask(core, dst)
             rid, pid = topo.addr(dst, core)
-            g.wait_ge(T.sem.hc, n_in)
-            g.remote_dma(T["lq%d" % r][:, j * w:j * w + w].bitcast(dt.uint8), T.hq[:, 0:w].bitcast(dt.uint8),
-                         T.sem["rf%d" % r], T.sem.sent, pid, rid, m)
-            g.wait_ge(T.sem.hp, n_in)
-            g.remote_dma(T["ls%d" % r][:, j * w:j * w + w], T.hs[:, 0:w], T.sem["rf%d" % r], T.sem.sent, pid, rid, m)
-            if j == 0:
+            for what in SENDS:
+                if what == str(j):
+                    g.wait_ge(T.sem.hc, n_in)
+                    g.remote_dma(T["lq%d" % r][:, lo:hi].bitcast(dt.uint8), T.hq[:, lo:hi].bitcast(dt.uint8),
+                                 T.sem["rf%d" % r], T.sem.sent, pid, rid, m)
+                if what == "s" and j == 0:
+                    g.wait_ge(T.sem.hp, n_in)
+                    g.remote_dma(T["ls%d" % r][:], T.hs[:], T.sem["rf%d" % r], T.sem.sent, pid, rid, m)
+            if j == len(hs) - 1:
                 g.wait_ge(T.sem.ha, n_in)
                 g.remote_dma(T["lr%d" % r][:], T.hr[:], T.sem["ra%d" % r], T.sem.sent, pid, rid, m)
-            g.wait_ge(T.sem.sent, (3 if j == 0 else 2) * n)
+            g.wait_ge(T.sem.sent, (1 + (j == 0) + (j == len(hs) - 1)) * n)
 
 
 def rank_program(g, core, T, topo):
@@ -132,7 +226,7 @@ def rank_program(g, core, T, topo):
             for v in vs:
                 cs_, bank_ = cols(v), v[0].startswith("ps")
                 for (c2, w2, q2, s, n, k) in hist.get(v[0], []):
-                    if adds and wr and q2 == q:
+                    if (adds or INORDER) and wr and q2 == q and s == own.get(q):
                         continue
                     if (wr or w2 or (bank_ and q2 != q)) and know[q].get(s, 0) < n and cs_ & c2:
                         if need.get(s, (0, None))[0] < n:
@@ -238,20 +332,24 @@ def rank_program(g, core, T, topo):
 
         if what == "places":
             order("g", [V("rw%d" % r)], [])
-            write(hs[0] if hs else dst, T["hr" if hs else "lr%d" % r][:], T["rw%d" % r][:], "ha" if hs else "ra%d" % r)
-            note(None, "ra%d" % r, n_in[0], [], [V("lr%d" % r)])
+            write(hs[-1] if hs else dst, T["hr" if hs else "lr%d" % r][:], T["rw%d" % r][:], "ha" if hs else "ra%d" % r)
+            note(None, "ra%d" % r, n_in[-1], [], [V("lr%d" % r)])
             return
         q, s = T["qx%d" % r], T["sx%d" % r]
-        order("g", [V("qx%d" % r), V("sx%d" % r)], [])
         if hs:
-            w = C // len(hs)
-            for j, h in enumerate(hs):
-                write(h, T.hq[:, 0:w].bitcast(dt.uint8), q[:, j * w:j * w + w].bitcast(dt.uint8), "hc")
-                write(h, T.hs[:, 0:w], s[:, j * w:j * w + w], "hp")
+            for j in SENDS:
+                if j == "s":
+                    order("g", [V("sx%d" % r)], [])
+                    write(hs[0], T.hs[:], s[:], "hp")
+                elif int(j) < len(hs):
+                    lo, hi = _share(int(j), len(hs))
+                    order("g", [V("qx%d" % r, lo, hi)], [])
+                    write(hs[int(j)], T.hq[:, lo:hi].bitcast(dt.uint8), q[:, lo:hi].bitcast(dt.uint8), "hc")
         else:
+            order("g", [V("qx%d" % r), V("sx%d" % r)], [])
             write(dst, T["lq%d" % r][:].bitcast(dt.uint8), q[:].bitcast(dt.uint8), "rf%d" % r)
             write(dst, T["ls%d" % r][:], s[:], "rf%d" % r)
-        note(None, "rf%d" % r, 2 * sum(n_in), [], [V("lq%d" % r), V("ls%d" % r)])
+        note(None, "rf%d" % r, sum(n_in) + n_in[0], [], [V("lq%d" % r), V("ls%d" % r)])
 
     def col(name, c):
         return V(name, c, c + 1)
@@ -281,78 +379,79 @@ def rank_program(g, core, T, topo):
 
     BACK = col("qcol", 2)
 
-    dma("y", "ldx", T.x0[:], T.x[:], [], [V("x0")])
+    H = C // 2
     dma("s", "ldu", T.ut[:], T.u[:], [], [V("ut")])
+    dma("y", "ldx", T.x0[:], T.x[:], [], [V("x0")])
     dma("y", "ldw", T.qw[:].bitcast(dt.uint8), T.wc[:], [V("x0"), V("ut")], [V("qw")])
     dma("y", "lds", T.sw[:], T.ws[:], [], [V("sw")])
     dma("y", "ldv", T.vt[:], T.v[:], [], [V("vt")])
 
-    iota(V("iu"), [[16, 8]], 0, 0)
-    iota(col("ipc", 0), [[0, 1]], 0, 1)
-    iota(V("jr"), [[0, NC], [1, 16]], 0, 0, True)
-    iota(V("i16"), [[16, NC]], 0, 0, True)
-    fill(V("zero"), 0.0)
-    fill(V("et", 0, 2 * EW), 0.0)
-    for h in range(2):
-        o, z = V("et", h * EW + 2 + h, h * EW + EW, 4), V("zero", 0, EW // 4)
-        op("g", lambda: g.affine_select(ap(o), ap(z), [[-1, EW // 4]], ALU.not_equal, 1.0, 0, 1), [z], [o])
-    for k, (runs, n) in enumerate(TILES):
-        a, b = 4 * (TOFF[k] + 16 * runs[-1]), 4 * TOFF[k + 1]
+    def select(o, z, n, c, base, cm):
+        op("g", lambda: g.affine_select(ap(o), ap(z), [[-1, n]], ALU.not_equal, c, base, cm), [z], [o])
+
+    def blank(k):
+        a, b = 4 * (TOFF[k] + 16 * TILES[k][0][-1]), 4 * TOFF[k + 1]
         act(V("wt", a, b), V("zero", 0, b - a), ACT.Copy)
-    act(V("seg"), V("zero", 0, C), ACT.Identity, bias=1.0)
-    act(V("d0s"), V("zero", 0, C), ACT.Copy)
-    cp(V("offu"), V("iu"))
-    ts(col("ipc", 1), col("ipc", 0), 15, ALU.bitwise_and)
-    ts(col("ipc", 2), col("ipc", 0), 4, ALU.arith_shift_right)
-    fill(col("rk", RS - 1), 0.0)
-    cp(V("qcol", 0, 2), V("ipc", 1, 3))
-    quant(V("qu"), V("su"), V("ut"))
-    ts(V("mk"), V("jr"), col("qcol", 0), ALU.not_equal, -BIG, ALU.mult)
-    op("v", lambda: g.vector.tensor_copy(T.qu2[:, 0:128].bitcast(dt.uint32), T.qu[:, 0:128].bitcast(dt.uint32).indirect(T.offu[:, 0:8])),
-       [V("qu"), V("offu")], [V("qu2")])
-    act(V("su2"), V("su"), ACT.Copy, off=V("offu"))
-    ts(V("dg"), V("jr"), col("qcol", 0), ALU.is_equal)
-    fill(V("seg", 0, C, 16), 0.0)
-    fill(V("d0s", 0, C, 16), -BIG)
-    iota(V("ig"), [[1, 8], [0, 64]], 0, 0, True)
-    for b in (0, 2, 1, 3):
-        cut(b)
-    ts(V("nb"), V("i16"), col("qcol", 0), ALU.subtract, 15.0, ALU.add)
-    ts(BACK, col("qcol", 0), -DROP, ALU.mult, 15 * DROP, ALU.add)
-    act(V("d0g"), V("dg"), ACT.Identity, bias=-DROP, scale=64 * DROP)
-    act(V("kb"), V("i16", 0, 8), ACT.Identity, bias=col("qcol", 0))
-    act(V("kc"), V("i16", 0, 8), ACT.Identity, bias=float(EL), scale=2.0)
-    act(col("cm", 0), col("zero", 0), ACT.Copy)
-    act(V("kb"), V("kb"), ACT.Identity, bias=0.5)
-    act(col("qcol", 3), BACK, ACT.Identity, bias=-float(A))
+
+    def partitions():
+        ts(col("ipc", 1), col("ipc", 0), 15, ALU.bitwise_and)
+        ts(col("ipc", 2), col("ipc", 0), 4, ALU.arith_shift_right)
+        cp(V("qcol", 0, 2), V("ipc", 1, 3))
+
+    def starts(name, c, c0):
+        act(V(name), V("zero", 0, C), ACT.Identity, bias=c)
+        act(V(name, 0, C, 16), V("zero", 0, NC), ACT.Identity, bias=c0)
+
+    def table():
+        for lo, hi, f in ((0, A, 2), (A, A + K, 1), (A + K, C, 0)):
+            iota(V("tab", lo, hi), [[0, hi - lo]], int(f * MU), 0, True)
+
+    def small():
+        act(V("kb"), V("i16", 0, 8), ACT.Identity, bias=col("qcol", 0))
+        act(V("kc"), V("i16", 0, 8), ACT.Identity, bias=float(EL), scale=2.0)
+        act(col("cm", 0), col("zero", 0), ACT.Copy)
+        act(V("kb"), V("kb"), ACT.Identity, bias=0.5)
+        act(col("qcol", 3), BACK, ACT.Identity, bias=-float(A))
+
+    once = {
+        "iu": lambda: iota(V("iu"), [[16, 8]], 0, 0), "ip": lambda: iota(col("ipc", 0), [[0, 1]], 0, 1),
+        "jr": lambda: iota(V("jr"), [[0, NC], [1, 16]], 0, 0, True), "i16": lambda: iota(V("i16"), [[16, NC]], 0, 0, True),
+        "ig": lambda: iota(V("ig"), [[1, 8], [0, 64]], 0, 0, True), "cols": lambda: iota(V("cols"), [[1, C]], 0, 0, True),
+        "val3": lambda: iota(V("val3"), [[1, K]], C, 0, True), "tab": table,
+        "zero": lambda: fill(V("zero"), 0.0), "et": lambda: fill(V("et", 0, 2 * EW), 0.0),
+        "offu": lambda: cp(V("offu"), V("iu")), "qcol": partitions, "rk": lambda: act(col("rk", RS - 1), col("zero", 0), ACT.Copy),
+        "seg": lambda: starts("seg", 1.0, 0.0), "d0s": lambda: starts("d0s", 0.0, -BIG),
+        "qu": lambda: quant(V("qu"), V("su"), V("ut")), "qv": lambda: quant(V("qv"), V("sv"), V("vt")),
+        "qu2": lambda: op("v", lambda: g.vector.tensor_copy(T.qu2[:, 0:128].bitcast(dt.uint32), T.qu[:, 0:128].bitcast(dt.uint32)
+                                                            .indirect(T.offu[:, 0:8])), [V("qu"), V("offu")], [V("qu2")]),
+        "su2": lambda: act(V("su2"), V("su"), ACT.Copy, off=V("offu")),
+        "mk": lambda: ts(V("mk"), V("jr"), col("qcol", 0), ALU.not_equal, -BIG, ALU.mult),
+        "dg": lambda: ts(V("dg"), V("jr"), col("qcol", 0), ALU.is_equal),
+        "d0g": lambda: act(V("d0g"), V("dg"), ACT.Identity, bias=-DROP, scale=64 * DROP),
+        "nb": lambda: ts(V("nb"), V("i16"), col("qcol", 0), ALU.subtract, 15.0, ALU.add),
+        "back": lambda: act(BACK, col("qcol", 0), ACT.Identity, bias=15 * DROP, scale=-DROP), "small": small,
+        "gt": lambda: ts(V("gt"), V("ig"), col("qcol", 1), ALU.is_equal), "qg": lambda: quant(V("qg"), V("sg"), V("gt")),
+    }
+    for h in range(2):
+        once["one%d" % h] = lambda h=h: select(V("et", h * EW + 2 + h, h * EW + EW, 4), V("zero", 0, EW // 4), EW // 4, 1.0, 0, 1)
+        once["neg%d" % h] = lambda h=h: select(V("et", (h + 2) * EW, (h + 3) * EW), V("zero"), EW, -1.0, 2 + h, 4)
 
     for r in range(3):
         rw, lr, qx, sx = "rw%d" % r, "lr%d" % r, V("qx%d" % r), V("sx%d" % r)
-        quant(qx, sx, V("x0" if r == 0 else "x1"))
-        send(r, "codes")
-        mm(V("ps0", 0, C), V("qu2"), V("su2"), qx, sx)
-        mm(V("ps1", 0, C), V("qu2"), V("su2"), qx, sx)
-        for b in range(4):
-            mm(bank(b, C), *eb(b), qx, sx)
-        if r == 0:
-            ts(V("gt"), V("ig"), col("qcol", 1), ALU.is_equal)
-            for h in range(2):
-                o = V("et", (h + 2) * EW, (h + 3) * EW)
-                op("g", lambda: g.affine_select(ap(o), ap(V("zero")), [[-1, EW]], ALU.not_equal, -1.0, 2 + h, 4), [V("zero")], [o])
-            iota(V("cols"), [[1, C]], 0, 0, True)
-            iota(V("tab", 0, A), [[0, A]], int(2 * MU), 0, True)
-            iota(V("tab", A, A + K), [[0, K]], int(MU), 0, True)
-            iota(V("tab", A + K, C), [[0, A]], 0, 0, True)
-            iota(V("val3"), [[1, K]], C, 0, True)
-        if r == 1:
-            quant(V("qv"), V("sv"), V("vt"))
 
-        def picks():
-            for lo, hi in ((256, C), (0, 256)):
-                tt(V("rm", lo, hi), V("ps0", lo, hi), V("mk", lo, hi), ALU.add)
-                if r == 0 and lo == 0:
-                    quant(V("qg"), V("sg"), V("gt"))
-                scan(V("wf", lo, hi), V("d0s", lo, hi), V("rm", lo, hi), -BIG, ALU.add, ALU.max)
+        def scores():
+            for lo, hi in QX:
+                quant(V(qx[0], lo, hi), V(sx[0], lo, hi), V("x1" if r else "x0", 4 * lo, 4 * hi))
+
+        def score(k):
+            lo = C - K if k == 7 else 0
+            mm(V("ps%d" % k, 0, C - lo), V("qu2"), V("su2"), V(qx[0], lo, C), V(sx[0], lo, C))
+
+        def picks(k):
+            lo, hi = PICKS[k]
+            p = V("ps7", lo - C + K, hi - C + K) if EARLY and k == 0 else V("ps0", lo, hi)
+            tt(V("rm", lo, hi), p, V("mk", lo, hi), ALU.add)
+            scan(V("wf", lo, hi), V("d0s", lo, hi), V("rm", lo, hi), -BIG, ALU.add, ALU.max)
 
         def compare(c):
             ts(slot(c, 0, 16 * c), V("ps0", 0, 16 * c), col("wf", 16 * c + 15), ALU.is_lt)
@@ -370,14 +469,20 @@ def rank_program(g, core, T, topo):
 
         def pack(k):
             a, b = TOFF[k], TOFF[k + 1]
+            both = k == 3 and "p4" not in ORDER[r].split()
+            if both:
+                b += 16 * TILES[4][0][0]
             quant(V("qt", a, b), V("stp", a, b), V("wt", 4 * a, 4 * b))
-            packed.append(k)
+            packed.extend([3, 4] if both else [k])
             if 0 in packed:
-                todo = [k] if k else [0] + packed[:-1]
+                todo = ([3, 4] if both else [k]) if k else [0] + packed[:-1]
                 for j in todo:
                     a, b = TOFF[j], TOFF[j + 1]
                     mm(V("ps6", 0, b - a), V("qg"), V("sg"), V("qt", a, b), V("stp", a, b), j == 0,
                        len(packed) == len(TILES) and j == todo[-1])
+
+        def unpack_own(b):
+            mm(bank(b, C), *eb(b), qx, sx)
 
         def keep(b):
             move(TC[b], win(b, 0, C), bank(b, C), None, 64.0)
@@ -388,12 +493,9 @@ def rank_program(g, core, T, topo):
         def unpack(b):
             p = V("ps7" if b % 2 == 0 else "ps1", 0, C)
             mm(p, *eb(b), V("lq%d" % r), V("ls%d" % r))
-            act(V("ff", b, 4 * C, 4), p, ACT.Copy)
+            move(UC[r][b], V("ff", b, 4 * C, 4), p)
 
         def pack_far():
-            if r == 0:
-                for b in range(4, 8):
-                    cut(b)
             quant(V("qf"), V("sf"), V("ff"))
             for b in range(4):
                 mm(bank(b, C), *eb(4 + b), V("qf"), V("sf"), False, True)
@@ -408,28 +510,21 @@ def rank_program(g, core, T, topo):
         def shared_sum(c):
             scan(V("er", EH * c, EH * c + EH), V("ej", EL * c, EL * c + EH), V("ej", EL * c + EH, EL * c + EL), -float(EL), ALU.add, ALU.add)
 
-        def counts(c):
-            if c in COUNT_V and c - 1 in COUNT_V:
-                shared(c)
-                shared_sum(c - 1)
-            else:
-                shared(c)
-            if c in COUNT_V and c + 1 not in COUNT_V:
-                shared_sum(c)
-
         def product():
             quant(V("qz"), V("sz"), V("zt"))
             for b in range(4):
                 mm(bank(b, K), V("qw", 128 * b, 128 * b + 128), V("sw", 128 * b, 128 * b + 128), V("qz"), V("sz"))
 
-        def near():
-            for b in range(4):
-                move("s", V("f64", b * K, b * K + K), win(b, 0, C), V("eo"))
+        def near(b):
+            move(NG[b], V("f64", b * K, b * K + K), win(b, 0, C), V("eo"))
 
         def whole():
-            ts(V("pi", 0, N2), wrapped("cx", 0, A), BACK, ALU.add, FLAG + 256.0, ALU.add)
-            ts(V("pi", N2, 2 * N2), wrapped("cx", 0, A), BACK, ALU.add, 1.0, ALU.add)
-            ts(V("pi", 2 * N2, NC), wrapped("cx", A, A + K), BACK, ALU.add)
+            ts(V("pi", 0, N2), wrapped("cx", 0, A), BACK, ALU.add, FLAG + 255.0, ALU.add)
+            ts(V("pi", N2, NC), wrapped("cx"), BACK, ALU.add)
+
+        def flags():
+            for lo, hi, c in ((0, N2, 1.0), (N2, N1, 0.0)):
+                act(V("ml", 16 * lo, 16 * hi), V("mr"), ACT.Identity, bias=2 * FLAG + c, scale=-FLAG / MU, off=V("oa", lo, hi))
 
         def parts():
             ts(V("hi"), V("pi"), 8, ALU.arith_shift_right, 1535, ALU.bitwise_and)
@@ -445,8 +540,35 @@ def rank_program(g, core, T, topo):
             for q, b in LATE:
                 move(q, V("x1", b, 4 * C, 4), win(b, 0, WW), V("no"), 0.015625)
 
+        def last(h):
+            lo, hi = h * H, h * H + H
+            for q, b in LATE:
+                move(q, V("x1", 4 * lo + b, 4 * hi, 4), win(b, 0, WW), V("no", lo // 16, hi // 16), 0.015625)
+            quant(V("qx3", lo, hi), V("sx3", lo, hi), V("x1", 4 * lo, 4 * hi))
+            mm(V("ps%d" % h, 0, H), V("qv"), V("sv"), V("qx3", lo, hi), V("sx3", lo, hi))
+
+        def codes_out(lo, hi):
+            dma("y", "st", T.oc[:, 4 * lo:4 * hi], T.qx3[:, lo:hi].bitcast(dt.uint8), [V("qx3", lo, hi)], [])
+
+        def result(h):
+            move(YC[h], V("ysb", h * H, h * H + H), V("ps%d" % h, 0, H))
+
+        def result_out(q, lo, hi):
+            dma(q, "st", T.y[:, lo:hi], T.ysb[:, lo:hi], [V("ysb", lo, hi)], [])
+
+        def scales(k):
+            dma(OSQ[k], "st", T.osc[4 * k:4 * k + 4, :], T.sx3[32 * k:32 * k + 4, :], [V("sx3")], [])
+
+        def whole_last():
+            new()
+            for h in range(2):
+                quant(V("qx3", h * H, h * H + H), V("sx3", h * H, h * H + H), V("x1", 4 * h * H, 4 * h * H + 4 * H))
+                mm(V("ps%d" % h, 0, H), V("qv"), V("sv"), V("qx3", h * H, h * H + H), V("sx3", h * H, h * H + H))
+
         steps = {
-            "wf": picks, "in": lambda: tt(slot(0, 0, C), V("ps0", 0, C), V("wf"), ALU.is_le),
+            "qx": scores, "codes": lambda: send(r, "codes"), "wa": lambda: picks(0), "wb": lambda: picks(1),
+            "shs": lambda: act(V("sh"), V("mr"), ACT.Sign),
+            "in": lambda: tt(slot(0, 0, C), V("ps0", 0, C), V("wf"), ALU.is_le),
             "eq": lambda: scan(V("eqs"), V("seg"), slot(0, 0, C), 0.0, ALU.mult, ALU.add),
             "e2": lambda: tt(V("e2"), V("nb"), wrapped("eqs"), ALU.subtract),
             "e3s": lambda: tt(V("e3", NV, NC), V("e2", NV, NC), V("pa", NV, NC), ALU.subtract),
@@ -457,27 +579,33 @@ def rank_program(g, core, T, topo):
             "fq": lambda: act(V("fq"), V("tab"), ACT.Copy, off=V(rw)), "fqv": lambda: cp(V("fq"), V("tab"), V(rw)),
             "f1": lambda: ts(V("fr"), V("fq"), 1.0 / MU, ALU.mult),
             "ox": lambda: hold(V("ox"), V("sval", A, 2 * A + K)), "oa": lambda: ts(V("oa"), wrapped("ox"), BACK, ALU.add),
-            "sv": lambda: cp(V("sval", 0, A), V("sval", A, 2 * A)), "qf": pack_far,
+            "sv": lambda: act(V("sval", 0, A), V("sval", A, 2 * A), ACT.Copy), "qf": pack_far,
             "m": lambda: tt(V("mr"), V("tab"), V("fq"), ALU.min, off=V(lr)),
             "sh": lambda: ts(V("sh"), V("mr"), 1.0, ALU.min),
             "cs": lambda: scan(V("cs"), V("zero", 0, C), V("sh"), 0.0, ALU.add, ALU.add),
             "cm": lambda: scan(V("cm", 1, C + 1), V("fr"), V("mr"), 0.0, ALU.add, ALU.add),
-            "ml": lambda: act(V("ml"), V("mr"), ACT.Identity, bias=2 * FLAG, scale=-FLAG / MU, off=V("oa")),
+            "ml": flags, "svv": lambda: cp(V("sval", 0, A), V("sval", A, 2 * A)),
+            "svg": lambda: op("g", lambda: g.affine_select(ap(V("sval", 0, A)), ap(V("sval", A, 2 * A)), [[0, A]], ALU.is_ge, 0.0, 0, 0),
+                              [V("sval", A, 2 * A)], [V("sval", 0, A)]),
+            "mqv": lambda: ts(col("tot", 0), col("cm", C), MU / 4 - C, ALU.add, 1.0 / MU, ALU.mult),
             "cg": lambda: tt(V("cg"), V("cm", 0, C), V("ml"), ALU.add, off=V("oa")), "cx": lambda: hold(V("cx"), V("cg")),
             "pi": whole, "hr": parts,
-            "mq": lambda: ts(col("tot", 0), col("cm", C), MU / 4 - C, ALU.add, 1.0 / MU, ALU.mult),
+            "mq": lambda: act(col("tot", 0), col("cm", C), ACT.Identity, bias=0.25 - C / MU, scale=1.0 / MU),
             "rr": lambda: ts(V("rr"), V("lo"), col("tot", 0), ALU.add),
             "sl": lambda: tt(V("sl"), V("rr"), V("hi"), ALU.min), "so": lambda: cp(V("so"), V("sl")),
             "sc": lambda: scatter(V("nrow"), V("so"), V("sval", 0, C)),
             "e1": lambda: tt(V("ka"), V("er", EH - 1, 8 * EH, EH), V("kc"), ALU.add), "e2o": lambda: ts(V("eo"), V("ka"), 0.5, ALU.mult),
             "sk": lambda: act(V("sk"), V("cm", 0, C), ACT.Copy, off=V("eo")), "skv": lambda: cp(V("sk"), V("cm", 0, C), V("eo")),
             "skh": lambda: hold(V("skx"), V("sk")),
-            "sk1": lambda: ts(V("ski"), wrapped("skx"), col("qcol", 3), ALU.add, 2.0 ** -8, ALU.mult),
-            "sk2": lambda: cp(V("sko"), V("ski")), "fix": name_updated,
-            "near": near, "qz": product, "nx": lambda: hold(V("nx"), V("nrow")),
-            "no": lambda: ts(V("no"), wrapped("nx"), BACK, ALU.add), "new": new,
+            "sk1": lambda: ts(V("sko"), wrapped("skx"), col("qcol", 3), ALU.add, 2.0 ** -8, ALU.mult),
+            "fix": name_updated,
+            "qz": product, "nx": lambda: hold(V("nx"), V("nrow")),
+            "no": lambda: ts(V("no"), wrapped("nx"), BACK, ALU.add), "new": new, "last": whole_last,
+            "oc": lambda: codes_out(0, C), "oca": lambda: codes_out(0, H), "ocb": lambda: codes_out(H, C),
+            "y": lambda: result_out("s", 0, C), "ya": lambda: result_out(YQ[0], 0, H), "yb": lambda: result_out(YQ[1], H, C),
         }
-        each = {"s": sign, "r": sums, "c": compare, "n": count, "p": pack, "t": keep, "d": again, "u": unpack, "k": counts,
+        each = {"i": scales, "l": last, "o": result, "x": cut, "j": near, "w": unpack_own, "q": score, "b": blank,
+                "s": sign, "r": sums, "c": compare, "n": count, "p": pack, "t": keep, "d": again, "u": unpack, "k": shared, "v": shared_sum,
                 "z": lambda b: act(V("zw", b * C, b * C + C), bank(b, C), ACT.Copy),
                 "y": lambda b: cp(V("zw", b * C, b * C + C), bank(b, C)),
                 "g": lambda b: move(ZG[b], V("zt", b, 4 * K, 4), V("zw", b * C, b * C + C), V("eo")),
@@ -485,20 +613,11 @@ def rank_program(g, core, T, topo):
         for name in ORDER[r].split():
             if name in steps:
                 steps[name]()
+            elif name in once:
+                once[name]()
             else:
                 each[name[0]](int(name[1:]))
 
-    qx, sx = "qx3", "sx3"
-    quant(V(qx), V(sx), V("x1"))
-    H = C // 2
-    mm(V("ps0", 0, H), V("qv"), V("sv"), V(qx, 0, H), V(sx, 0, H))
-    mm(V("ps1", 0, H), V("qv"), V("sv"), V(qx, H, C), V(sx, H, C))
-    dma("y", "st", T.oc[:], T[qx][:].bitcast(dt.uint8), [V(qx)], [])
-    for k in range(4):
-        dma("y", "st", T.osc[4 * k:4 * k + 4, :], T[sx][32 * k:32 * k + 4, :], [V(sx)], [])
-    cp(V("ysb", 0, H), V("ps0", 0, H))
-    act(V("ysb", H, C), V("ps1", 0, H), ACT.Copy)
-    dma("s", "st", T.y[:], T.ysb[:], [V("ysb")], [])
     for s in SEMAPHORES:
         if total.get(s, 0):
             g.wait_ge(T.sem[s], total[s])

@@ -5,116 +5,46 @@ ACT = ActivationFunctionType
 C, A, K = 320, 96, 128
 STEP = [1, 2, 4]
 NC = C // 16
-N1, N2 = (A + K) // 16, A // 16
-NV = 13
+KEPT = A + K
+N1, N2 = KEPT // 16, A // 16
 WW = C + K
 BIG = 2.0 ** 83
 DROP = 2.0 ** 19
-EL = 2 * A + 16
-EH = EL // 2
+XW = KEPT + K
+MID = 160.0
 MU = 255.0
 FLAG = 2.0 ** 17
+EL = 2 * A + 16
+EH = EL // 2
 CODE = "float8_e4m3fn_x4"
 TILES = [([0, 19, 18, 17], 320), ([16, 15, 14, 13], 256), ([12, 11, 10, 9], 192), ([8, 7, 6, 5], 128), ([4, 3, 2, 1], 128)]
 TOFF = [sum(n for _, n in TILES[:k]) for k in range(len(TILES) + 1)]
-RS = 128
+RS = C
 EW = 520
 ORDER = [
-    "ip zero iu qcol offu b2 et jr dg back mk qu b1 seg ig qu2 one1 d0s gt one0 x1 x3 x0 qx b3 su2 i16 q7 wa q1 b0 q0 b4 val3 cols qg d0g "
-    "small nb s19 x2 wb s18 in r19 c12 s17 eq r18 c11 n12 s16 codes r17 c10 rk s15 r16 s14 n11 w1 c9 w3 r15 n10 c8 n9 s13 c7 tab n8 c6 r14 "
-    "n7 c5 w0 p2 n6 p0 c4 r13 c3 n5 t0 w2 c2 neg1 p3 c1 n3 neg0 p4 t2 p1 n4 e2 n2 n1 t1 e3s e3v cw pd rw x7 u1 x5 u0 places d0 x6 t3 d2 u3 "
-    "orow d1 x4 u2 d3 fq qf sv z0 ox f1 z1 m oa sh cm ml cs cg mq k0 cx pi hr k1 k7 k4 k5 rr k6 k2 sl k3 z2 z3 e1 so e2o sk g2 sc skh g1 "
-    "sk1 g3 g0 j0 fix qz nx j2 a0 j1 no j3 a2 a1 a3 new",
-    "qx q7 q0 wa codes q1 wb s19 w0 s18 r19 s17 in c12 eq c11 w3 n12 c10 n11 r18 e2 w1 s16 c9 r17 n10 c8 n9 p2 s15 c7 n8 c6 r16 s14 n7 r15 "
-    "s13 c5 n6 w2 c4 c3 r14 n5 n4 p0 r13 c2 c1 t1 p3 t2 p4 n2 p1 e3s d1 t0 n1 t3 u1 n3 u0 e3v cw d0 u3 pd rw u2 d2 qv orow fq d3 ox qf "
-    "places sv z1 f1 z2 oa m z3 sh cm ml mq cs k5 cg cx k6 k0 pi hr k4 k3 rr k1 k2 sl k7 e1 so z0 e2o g1 sc g2 sk g0 j1 skh g3 j2 sk1 fix "
-    "j0 j3 qz nx a0 a1 a2 no a3 new",
-    "qx q7 q1 wa s19 s18 r19 q0 s17 r18 s16 r17 wb w1 in c12 s15 eq c11 r16 n12 codes c10 n11 s14 c9 r15 n10 w2 s13 p2 w3 p0 c8 n9 c7 w0 n8 "
-    "c6 n7 c5 r14 n6 r13 c4 c3 t2 n5 t3 c2 e2 c1 u1 u0 p3 p4 p1 n3 n1 n2 n4 t1 e3s e3v cw u3 pd rw places d3 u2 t0 d1 d2 d0 orow qf fq sv "
-    "ox z0 oa f1 z1 m sh cm cs ml cg z2 k6 k2 cx pi mq hr k4 k0 rr k5 k7 k1 k3 sl e1 so z3 e2o sk g2 sc g1 skh g3 sk1 fix g0 qz nx j0 j3 "
-    "a0 no j2 j1 a2 a1 a3 l1 l0 o1 o0 osc"]
-ORDER = [
-    "ip ig zero et rk d0s b3 qcol seg b0 gt jr iu one1 qu dg b2 mk i16 back d0g offu qg x3 su2 one0 x1 b4 qu2 b1 x2 nb qx x0 small q7 "
-    "wa codes cols q0 q1 wb s19 in c13 eq w2 s18 c12 n13 r19 c11 n12 c10 n11 tab s17 r18 s16 c9 n10 r17 c8 w1 s15 n9 c7 p2 e2 n8 w3 c6 "
-    "r16 n7 s14 c5 n6 w0 r15 r14 c4 c3 p0 t3 n5 c2 c1 p3 p4 neg0 p1 neg1 t0 t1 d0 n2 n3 t2 n4 d1 u1 n1 e3s x6 e3v u0 cw x5 pd x4 rw x7 "
-    "u3 u2 fqv d3 places d2 orow f1 ox qf m svg oa sh z0 cm ml z2 cs mqv cg k5 k4 k1 cx v1 pi k2 k7 hr k3 k6 k0 v2 val3 rr v0 z3 sl e1 "
-    "so z1 e2o sk g3 sc skh g0 sk1 g1 fix g2 j0 j2 qz j1 nx j3 a0 no a2 a1 a3 new ",
-    "qx q7 q0 wa q1 codes wb in c13 s19 eq s18 c12 r19 n13 s17 c11 w3 n12 w0 c10 r18 n11 c9 s16 n10 r17 c8 n9 s15 c7 r16 w2 s14 n8 p2 "
-    "r15 c6 n7 c5 n6 c4 c3 r14 n5 p0 c2 c1 p3 p4 t0 p1 w1 t2 t3 d2 d3 n1 t1 n2 d0 n3 e2 n4 e3s cw e3v u0 pd u1 rw d1 orow fqv u2 ox f1 "
-    "qv u3 places oa qf m sh z0 cm ml cs mqv z1 cg k7 k0 k1 cx v1 svg pi v0 k6 hr k2 k5 k4 rr k3 z2 v2 sl e1 z3 so e2o sk sc g2 skh sk1 "
-    "g1 g3 fix g0 j0 j1 qz j2 nx j3 a0 a1 no a2 a3 new ",
-    "qx q7 q0 codes wa q1 wb s19 in c13 s18 eq r19 c12 s17 n13 r18 c11 n12 s16 c10 n11 r17 s15 c9 w1 r16 n10 c8 n9 s14 c7 n8 c6 n7 p2 "
-    "w3 r15 c5 w0 e2 n6 r14 c4 p0 c3 n5 t1 n3 c2 c1 p3 p4 p1 t3 e3s t0 w2 n1 t2 n4 u0 u1 d1 n2 e3v cw u2 pd u3 d0 d2 d3 rw fqv orow qf "
-    "places ox m oa z0 sh f1 z1 cs cm ml svg k1 k4 cg k3 mqv k2 cx k5 k0 k7 pi v1 v2 hr v0 z3 k6 rr e1 sl e2o so z2 g1 sc g2 g0 g3 qz "
-    "sk skh sk1 fix j0 a0 nx j1 a1 j3 j2 a2 no a3 l1 ocb l0 oca i0 i2 o1 i1 i3 o0 yb ya "]
-ORDER = [
-    "zero d0s seg et iu ip ig one0 b0 b2 qcol gt qg offu jr qu x2 b1 qu2 one1 rk x0 dg x3 mk su2 qx q7 x1 wa i16 codes q0 wb q1 tab nb b4 "
-    "back in c13 small eq d0g b3 w1 c12 s19 n13 s18 c11 n12 cols r19 w2 s17 c10 neg1 r18 n11 c9 neg0 n10 w0 c8 s16 n9 r17 c7 p2 p0 n8 c6 "
-    "s15 n7 c5 n6 c4 w3 r16 c3 s14 val3 n5 r15 c2 r14 t2 c1 e2 t1 p3 t3 p4 p1 n4 n1 n3 t0 n2 u0 e3s e3v cw pd u1 rw d1 x6 places u2 orow "
-    "u3 x5 d2 ox x7 d0 x4 d3 fq qf oa m z0 f1 ml sh cm cs cg svg k1 z1 cx k0 pi k2 hr v1 k7 v0 k6 k5 k4 mq rr v2 k3 z2 sl e1 so z3 e2o "
-    "g1 sk g3 sc skh g2 g0 j1 j0 j2 j3 sk1 fix qz nx a0 a1 no a2 a3 new",
-    "qx q7 codes wa q0 wb q1 s19 in c13 eq c12 n13 c11 n12 s18 r19 c10 n11 c9 w1 n10 c8 p2 n9 s17 c7 w2 r18 s16 n8 w0 r17 c6 s15 n7 c5 w3 "
-    "n6 p0 c4 r16 c3 n5 s14 c2 c1 p3 p4 r15 r14 t0 n1 p1 e2 t1 n3 n4 n2 e3s d0 t2 e3v t3 cw d1 d2 pd rw qv fq d3 u0 orow u1 u2 f1 u3 ox "
-    "places oa qf z0 z1 m sh cm ml mq cs cg k1 cx k7 k0 pi k2 hr k6 v1 k3 k4 k5 v2 svg rr z2 v0 sl e1 so e2o z3 sc g2 sk g0 g1 skh g3 j0 "
-    "j1 sk1 fix j2 qz nx a0 no a1 j3 a2 a3 new",
-    "qx q7 codes wa q0 wb in c13 eq c12 q1 n13 s19 c11 n12 c10 w2 n11 s18 r19 s17 c9 n10 c8 n9 w3 r18 c7 p2 s16 w0 n8 r17 c6 w1 n7 s15 "
-    "r16 s14 c5 r15 n6 p0 c4 c3 n5 c2 r14 t3 t1 c1 p3 p4 p1 t2 e2 u0 n4 n1 n2 e3s n3 u1 t0 d1 cw e3v u2 u3 pd d2 rw d3 places fq d0 orow "
-    "ox qf oa z0 f1 m sh z1 cm cs ml cg k2 z2 cx k5 k6 k3 k0 mq svg k1 pi v1 k7 hr k4 v0 rr v2 z3 sl e1 so e2o sk sc skh g0 g2 g1 sk1 "
-    "fix g3 qz nx j0 j3 a0 j1 no j2 a1 a2 a3 last oc i0 i1 i2 i3 o0 o1 y"]
-ORDER = [
-    "et zero ig ip qcol jr iu one0 b1 d0s i16 qu gt b0 b4 dg b2 mk one1 offu x0 x2 su2 qu2 qx x1 q7 q0 q1 x3 back w2 wa neg0 codes wb w3 "
-    "seg w1 qg b3 c11 rk c1 d0g s19 c10 c9 in c12 s17 c4 s18 p2 c8 c2 s13 c6 s15 s14 r15 r18 nb r19 n12 r17 neg1 n9 cols n11 s16 r13 w0 "
-    "eq c5 n10 r16 c3 c7 p0 p3 n8 tab n6 n4 n7 r14 p4 p1 n3 n1 n2 t1 e2 t3 t2 t0 n5 u0 x5 e3s e3v cw u1 small d2 pd u2 rw u3 x7 orow x4 "
-    "d3 d0 places fq sv ox d1 x6 val3 qf oa z0 f1 m sh ml cm cs z1 cg k5 k0 k7 cx k1 pi hr k6 v0 k3 mq k2 rr k4 v1 sl z3 z2 so e1 e2o sk "
-    "g1 sc g0 g2 skh g3 j2 sk1 fix j0 j3 j1 qz nx a0 no a2 a3 a1 new",
-    "qx q7 q0 q1 wa s16 codes s19 w2 s18 s17 wb r19 c3 s13 c12 c1 c5 r17 c8 c7 c2 c9 c11 n1 c4 s15 w0 r16 n3 w3 in c10 n4 n9 r13 c6 r18 "
-    "s14 r15 n2 p2 r14 eq w1 t1 n8 p0 e2 n7 p3 p4 p1 n10 n12 n6 t0 t3 n5 t2 n11 u0 e3s u1 d0 e3v cw u2 pd u3 d2 d3 rw orow ox fq qv d1 "
-    "places qf oa sv f1 z0 m sh cm z2 cs ml cg k2 cx k1 k6 k0 pi hr k5 mq v1 k3 k7 rr k4 z3 v0 z1 sl e1 so e2o sk sc g2 g1 g0 g3 skh sk1 "
-    "fix qz nx j2 j1 j0 a1 j3 a2 no a0 a3 new",
-    "qx q7 q1 q0 wa s18 s16 s19 codes wb c11 s17 w1 c4 c10 s13 c3 c1 s15 s14 c12 n1 c7 w2 r15 r18 c9 c2 r17 c8 w3 in r19 p2 c5 eq r14 n2 "
-    "w0 n9 r13 c6 p0 p3 n3 n7 p4 r16 p1 n8 t0 n12 e2 t1 t3 t2 n11 n10 u0 u1 n5 n4 d0 n6 d2 u2 cw e3v u3 e3s d3 pd rw d1 orow places ox "
-    "qf fq sv oa f1 m z0 sh ml z2 cm cs cg cx k3 mq k6 k0 k2 pi k4 k1 hr k5 k7 rr v1 v0 sl z3 e1 so z1 e2o sc sk g0 skh g2 sk1 fix g1 g3 "
-    "j0 qz nx j2 a0 j3 no j1 a2 a3 a1 last i2 o0 o1 y oc i0 i1 i3"]
-ORDER = [
-    "ip et ig iu zero qcol jr one0 gt b1 offu qu seg qu2 i16 one1 d0s mk dg b3 su2 b0 cols x2 x0 qx val3 d0g q7 x3 wa b2 q1 rk b4 codes qg "
-    "back s18 neg0 s16 neg1 q0 wb s17 nb x1 c2 c4 c9 s19 c5 r17 in c1 c10 c8 c12 s14 w1 s15 c7 s13 c11 tab w0 w2 r14 eq c6 c3 n2 n6 n7 "
-    "r18 r19 w3 r13 r15 p2 r16 p0 n11 p3 n4 small t3 p4 n3 t2 p1 t0 u0 n1 e2 n10 u1 n9 n8 d0 u2 n12 n5 u3 t1 e3v e3s cw pd rw x5 places "
-    "d2 x6 x4 d3 x7 d1 orow qf ox fq oa m f1 sh cm sv cs z0 ml z1 mq k7 cg k3 k2 k1 cx pi k0 k5 k4 hr k6 v0 z3 rr v1 z2 sl e1 so e2o sk "
-    "sc g2 g3 skh sk1 g0 fix g1 j3 j0 j2 qz j1 nx no a0 a3 a2 a1 new",
-    "qx q7 codes q0 q1 wa s17 wb s16 c1 c9 s19 c5 c2 s14 c4 c11 c10 s18 in s13 c6 eq r18 c3 r19 w2 n11 r14 n1 w1 n5 c12 r17 s15 n2 n4 w3 "
-    "c8 r16 w0 r15 n10 r13 c7 t0 p2 t1 n3 p0 t2 p3 n7 n8 n9 t3 p4 p1 n6 u0 u1 n12 e2 e3s d2 u2 u3 d3 e3v cw d0 pd d1 rw orow sv places qv "
-    "ox qf fq oa f1 m sh z0 cs z2 cm ml k5 cg k1 cx k0 k6 k4 mq pi hr k7 k3 k2 v1 rr v0 sl z1 z3 e1 so e2o sk sc g3 skh g1 g0 sk1 fix g2 "
-    "qz nx j3 no j0 a0 a3 j2 j1 a2 a1 new",
-    "qx q7 wa q1 codes s19 q0 wb c8 s18 c1 s17 c3 w3 c10 s14 s15 c2 c11 s16 s13 w0 c9 r16 w2 c7 n10 r17 n3 n8 in c12 w1 c6 r18 c5 c4 r19 "
-    "eq p2 n2 r14 n1 e2 r13 p0 r15 t1 n11 p3 p4 n5 t0 t3 p1 n4 n9 n6 n12 e3s t2 n7 e3v u0 d1 u1 cw pd d2 u2 rw u3 orow d3 fq d0 sv qf z0 "
-    "places ox oa f1 m z1 sh ml cm cs cg z2 k0 cx k1 pi k4 k5 k6 mq v0 k2 hr rr v1 k3 sl k7 so e1 z3 e2o sc sk g1 skh g2 sk1 fix g3 g0 j3 "
-    "qz nx no j0 a0 a3 j2 j1 a2 a1 last o0 oc i2 o1 y i3 i0 i1"]
-ORDER = [
-    "ip zero d0s ig qcol et iu gt jr qu offu b2 one0 qg b3 qu2 seg one1 b1 mk su2 b0 qx dg q7 back neg0 x3 wa i16 q0 codes q1 wb x0 b4 rk "
-    "d0g w3 s18 s17 s19 c12 c9 c10 s15 neg1 s16 x1 c11 c8 c3 c5 in x2 c2 w0 cols r15 eq w1 r18 nb r17 s13 n8 p2 c1 c7 r19 w2 c4 p0 c6 n5 "
-    "tab n9 n3 p3 r13 s14 e2 r16 p4 r14 t2 p1 t3 n1 val3 n12 e3s t1 n7 x4 n6 n11 u0 n4 u1 n2 d1 n10 cw e3v x7 pd x6 rw x5 t0 orow u2 u3 "
-    "d0 fq d2 places d3 sv qf ox m small oa f1 sh z0 cm ml z1 mq cs k5 k2 cg k1 k7 k6 k4 cx k0 pi k3 z2 v0 hr v1 rr sl e1 so e2o sc z3 sk "
-    "skh sk1 g1 g0 g3 g2 j3 fix j1 qz nx j0 no a0 j2 a1 a2 a3 new",
-    "qx q7 wa q0 codes q1 s17 wb c1 w0 c9 c2 s16 c6 c5 c7 s18 w3 n6 s14 c12 n9 s19 w1 c11 c3 s15 n12 r19 w2 c8 r18 n2 n7 qv c10 r17 r16 in "
-    "c4 p2 s13 p0 r14 n8 r13 r15 n3 eq p3 t0 t1 n1 n5 e2 t2 t3 p1 d1 u0 n10 n11 n4 e3v e3s cw u1 u2 u3 d0 d3 pd rw orow ox d2 qf fq places "
-    "oa f1 m sh sv z0 ml cm z2 cs cg k3 k1 k2 cx k0 pi v1 hr mq k7 k6 rr v0 k5 k4 sl e1 so z3 e2o z1 sk sc g0 skh sk1 g1 fix g2 g3 qz nx "
-    "j3 no j1 j0 j2 a0 a1 a2 a3 new",
-    "qx codes q7 q1 wa q0 s16 wb s19 s17 s18 s15 c11 c10 c9 in r18 r19 s14 c6 r17 c12 n9 c7 c5 w1 n7 c3 w0 w3 p2 w2 n11 c1 c8 s13 p0 r14 c4 "
-    "c2 eq r15 n10 r16 r13 n1 p3 t2 t0 p1 n5 n4 n2 n6 t1 n8 n3 u0 e2 n12 u1 e3s t3 e3v cw d0 u2 pd rw u3 orow places fq d1 d2 d3 sv qf ox m "
-    "oa f1 z0 sh cm ml cs z2 mq k3 cg k0 cx k1 pi v0 hr k5 k2 k6 k4 rr v1 k7 z3 sl e1 so z1 e2o sk sc skh g2 sk1 g0 fix g1 g3 qz j3 j0 j2 "
-    "j1 nx a0 no a2 a3 a1 last oc o0 i2 i0 o1 i1 y i3"]
-COUNT_V = (0, 1)
-ZG = "ssss"
-TC = "ssss"
-NG = "ssss"
-YC, YQ, OSQ = "vv", "sy", "yyss"
+    "zero et b1 iu b2 ip d0s jr qcol offu b0 one1 d0t qu small su2 mk qu2 x1 one0 b3 seg qa qb i16 q7 q0 x2 q1 ma codes x0 w1 wa b4 mb "
+    "seh ia c16 wb c14 in c10 c2 s19 s17 ig eq c3 c5 gt c6 c4 c8 c15 s18 n16 s12 r17 w0 r18 r19 s13 c9 s11 c1 n10 c7 r12 n2 qg r13 p0 n3 "
+    "r11 p1 p2 p3 p4 n4 n1 n15 n7 n8 f0 cols n9 f1 n6 f2 n5 t0 d0g n14 f3 t1 e3s f4 tab pad h2 cw h0 u2 x3 u0 w2 w3 h3 pd kb rw orow fq "
+    "t2 places m t3 ox h1 sh fp oa cm u1 d2 d1 u3 d3 cs ml mq qf cg E7 E5 E0 cx v1 d0 E1 pi v3 E4 E6 E3 v0 E2 F0 F1 v2 hr z3 rr eo z1 z2 "
+    "sl so g1 g2 z0 g3 sv g0 sk sc skh j3 ny sko qz ne k1 j0 j2 k2 e1 fix e0 k0 e2 e3 nx a2 j1 no +qa a0 k3 l2 +q7 a1 a3 +ma l3 +wa +ia "
+    "l0 l1 ",
+    "qb q0 mb c14 q1 s18 w0 codes wb s17 r18 c16 c5 c6 s12 in s13 s19 c3 c15 r17 eq c8 c2 c9 r19 n16 w3 c1 c10 w2 n3 n1 c7 s11 p0 r13 w1 "
+    "n10 r12 f0 p1 c4 n2 r11 p2 p3 f1 n5 n4 f2 f3 n14 n15 n8 n6 n7 n9 e3s f4 cw qv pd rw places t1 t0 t2 t3 h0 u0 h1 h2 h3 orow u1 u2 d1 "
+    "d2 u3 qf v2 fq ox d0 m v1 oa sh fp cm ml cs cg z2 d3 E0 cx E1 mq E4 v0 E2 pi F0 hr E7 sv v3 E5 E3 E6 F1 rr sl z3 eo z1 so z0 sk sc "
+    "g3 skh g1 g2 ny g0 j3 j1 j0 sko qz ne k2 fix k3 e3 e2 k1 e1 k0 nx a3 e0 no j2 +qa a0 a1 l3 +q7 a2 +ma l0 l2 l1 +wa +ia ",
+    "qb q0 mb q1 c15 wb s18 c14 c9 s19 s17 c3 c2 r18 w1 c8 in r17 w0 c6 s13 c7 c5 w2 eq r19 s12 c16 n8 c4 s11 n5 r13 c1 p0 r11 p3 c10 p1 "
+    "r12 p2 f0 e3s n10 n14 w3 n9 t2 f1 n4 f2 n6 n15 n1 t0 f3 f4 n16 n3 n2 codes h0 n7 cw pd h1 rw h2 t1 u0 d2 orow places h3 u2 d0 u1 u3 "
+    "fq d1 t3 qf ox m fp oa sh cm v2 z2 ml cs v1 z1 d3 E5 cg v0 E3 E0 E6 cx sv E4 E1 mq pi E2 F0 hr E7 v3 z3 F1 rr sl eo z0 g1 sk g3 so "
+    "sc skh g0 ny g2 nc sko qz j2 ne nl j0 fix j1 e2 k2 nx e3 e1 a2 k0 e0 a0 k3 j3 no k1 a1 l0 la oe l1 ya o1 a3 l2 l3 ye lb i2 oc yb i3 "
+    "i1 i0 o0 yo "]
+WHO = {k: ["ssss"] * 3 for k in "tuzgjelo"}
+WHO.update({"z": ["ssss", "vsss", "ssss"], "g": ["ssss", "ssss", "vsss"], "j": ["ssss", "ssss", "svss"], "e": ["ssvs", "svss", "ssss"],
+            "l": ["sssv", "svss", "ssvv"], "fq": "sss", "fp": "sss", "sh": "vvv", "sk": "vss"})
+ON_S = (11, 12, 13, 17, 18, 19)
+COUNT_V = 2
+OSQ = "yyss"
 FEW, SENDS = 128, "s10"
-UC = ["ssss", "ssss", "ssss"]
-INORDER = False
-EARLY = True
-QX = ((C - K, C), (0, C - K))
-PICKS = ((256, C), (0, 256))
-LATE = (("s", 0), ("s", 1), ("v", 2), ("v", 3))
+PICK = (KEPT, KEPT, KEPT)
 
 
 def _sb(n, d):
@@ -122,35 +52,34 @@ def _sb(n, d):
 
 
 SCRATCH = {
-    "x0": _sb(4 * C, "bfloat16"), "x1": _sb(4 * C, "bfloat16"), "ut": _sb(512, "bfloat16"), "vt": _sb(512, "bfloat16"),
+    "x0": _sb(4 * C, "bfloat16"), "x1": _sb(4 * XW, "bfloat16"), "ut": _sb(512, "bfloat16"), "vt": _sb(512, "bfloat16"),
     "qu": _sb(128, CODE), "su": _sb(128, "uint8"),
     "qu2": _sb(128, CODE), "su2": _sb(128, "uint8"), "qv": _sb(128, CODE), "sv": _sb(128, "uint8"),
-    "qw": _sb(512, CODE), "sw": _sb(512, "uint8"), "et": _sb(4 * EW, "bfloat16"),
-    "qe": _sb(1024, CODE), "se": _sb(1024, "uint8"), "qf": _sb(C, CODE), "sf": _sb(C, "uint8"),
+    "qw": _sb(512, CODE), "sw": _sb(512, "uint8"), "et": _sb(2 * EW, "bfloat16"),
+    "qe": _sb(512, CODE), "se": _sb(512, "uint8"), "qf": _sb(C, CODE), "sf": _sb(C, "uint8"),
     "qz": _sb(K, CODE), "sz": _sb(K, "uint8"), "zt": _sb(4 * K, "bfloat16"), "ff": _sb(4 * C, "bfloat16"),
     "f64": _sb(4 * K, "bfloat16"), "win": _sb(4 * WW, "bfloat16"), "zw": _sb(4 * C, "bfloat16"), "ysb": _sb(C, "float32"),
     "wt": _sb(4 * TOFF[-1], "bfloat16"), "qt": _sb(TOFF[-1], CODE), "stp": _sb(TOFF[-1], "uint8"),
     "ig": _sb(512, "bfloat16"), "gt": _sb(512, "bfloat16"), "qg": _sb(128, CODE), "sg": _sb(128, "uint8"),
     "iu": _sb(8, "int32"), "offu": _sb(8, "uint16"), "jr": _sb(C, "bfloat16"),
-    "ipc": _sb(4, "int32"), "i16": _sb(NC, "float32"), "qcol": _sb(4, "float32"), "ka": _sb(8, "float32"), "kc": _sb(8, "float32"),
-    "kb": _sb(8, "bfloat16"), "cols": _sb(C, "float32"), "val3": _sb(K, "float32"),
-    "dg": _sb(C, "bfloat16"), "mk": _sb(C, "bfloat16"), "d0s": _sb(C, "bfloat16"), "seg": _sb(C, "bfloat16"),
-    "d0g": _sb(C, "bfloat16"), "nb": _sb(NC, "float32"), "tab": _sb(C, "bfloat16"), "zero": _sb(EW, "bfloat16"),
-    "rm": _sb(C, "float32"), "wf": _sb(C, "float32"), "eqs": _sb(C, "bfloat16"), "e2": _sb(NC, "float32"), "e3": _sb(NC, "float32"),
-    "rk": _sb(16 * RS, "bfloat16"), "pa": _sb(NC, "float32"), "cw": _sb(C, "float32"), "pd": _sb(NC, "float32"),
-    "fq": _sb(C, "bfloat16"), "fr": _sb(C, "bfloat16"), "sval": _sb(A + C, "float32"), "ox": _sb(A + K, "float32"),
+    "ipc": _sb(4, "int32"), "i16": _sb(NC, "float32"), "qcol": _sb(8, "float32"), "cols": _sb(WW, "float32"), "kb": _sb(8, "float32"),
+    "mk": _sb(C, "bfloat16"), "d0s": _sb(C, "bfloat16"), "seg": _sb(C, "bfloat16"),
+    "d0g": _sb(C, "bfloat16"), "tab": _sb(C, "bfloat16"), "zero": _sb(EW, "bfloat16"),
+    "rm": _sb(C, "float32"), "wf": _sb(C, "float32"),
+    "rk": _sb(NC * RS, "bfloat16"), "pa": _sb(NC, "float32"), "cw": _sb(C, "float32"), "pd": _sb(NC, "float32"),
+    "fq": _sb(C, "bfloat16"), "fr": _sb(C, "bfloat16"),
+    "sval": _sb(A + C, "float32"), "ox": _sb(KEPT, "float32"), "oa": _sb(N1, "uint16"),
+    "mr": _sb(C, "bfloat16"), "cm": _sb(C + 16, "float32"), "ml": _sb(KEPT, "float32"), "cg": _sb(KEPT, "float32"), "cx": _sb(KEPT, "float32"),
     "pi": _sb(NC, "int32"), "hi": _sb(NC, "int32"), "lo": _sb(NC, "int32"), "tot": _sb(2, "float32"),
-    "sh": _sb(C, "bfloat16"), "cs": _sb(C, "bfloat16"), "ej": _sb(8 * EL, "bfloat16"), "er": _sb(8 * EH, "float32"),
-    "eo": _sb(8, "uint16"), "mr": _sb(C, "bfloat16"), "cm": _sb(C + 16, "float32"), "ml": _sb(A + K, "float32"),
-    "cg": _sb(A + K, "float32"), "cx": _sb(A + K, "float32"), "oa": _sb(N1, "uint16"), "rr": _sb(NC, "float32"),
-    "sl": _sb(NC, "float32"), "so": _sb(NC, "uint16"), "nrow": _sb(C, "float32"), "nlb": _sb(C, "float32"),
-    "sk": _sb(K, "float32"), "skx": _sb(K, "float32"), "ski": _sb(8, "int32"), "sko": _sb(8, "uint16"),
-    "nx": _sb(C, "float32"), "no": _sb(NC, "uint16"),
+    "rr": _sb(NC, "float32"), "sl": _sb(NC, "float32"), "so": _sb(NC, "uint16"),
+    "sh": _sb(C, "bfloat16"), "cs": _sb(C, "bfloat16"), "ej": _sb(8 * EL, "bfloat16"), "er": _sb(8 * EH, "float32"), "eo": _sb(8, "uint16"),
+    "sk": _sb(K, "float32"), "skx": _sb(K, "float32"), "sko": _sb(8, "uint16"),
+    "nrow": _sb(C, "float32"), "nlb": _sb(C, "float32"), "nx": _sb(C, "float32"), "no": _sb(NC, "uint16"),
     "hr": _sb(NC, "uint16"), "hq": _sb(C, CODE), "hs": _sb(C, "uint8"),
 }
 for _r in range(4):
-    SCRATCH["qx%d" % _r] = _sb(C, CODE)
-    SCRATCH["sx%d" % _r] = _sb(C, "uint8")
+    SCRATCH["qx%d" % _r] = _sb(XW, CODE)
+    SCRATCH["sx%d" % _r] = _sb(XW, "uint8")
 for _r in range(3):
     SCRATCH["rw%d" % _r] = _sb(NC, "uint16")
     SCRATCH["lr%d" % _r] = _sb(NC, "uint16")
@@ -226,7 +155,7 @@ def rank_program(g, core, T, topo):
             for v in vs:
                 cs_, bank_ = cols(v), v[0].startswith("ps")
                 for (c2, w2, q2, s, n, k) in hist.get(v[0], []):
-                    if (adds or INORDER) and wr and q2 == q and s == own.get(q):
+                    if adds and wr and q2 == q and s == own.get(q):
                         continue
                     if (wr or w2 or (bank_ and q2 != q)) and know[q].get(s, 0) < n and cs_ & c2:
                         if need.get(s, (0, None))[0] < n:
@@ -339,16 +268,16 @@ def rank_program(g, core, T, topo):
         if hs:
             for j in SENDS:
                 if j == "s":
-                    order("g", [V("sx%d" % r)], [])
-                    write(hs[0], T.hs[:], s[:], "hp")
+                    order("g", [V("sx%d" % r, 0, C)], [])
+                    write(hs[0], T.hs[:], s[:, 0:C], "hp")
                 elif int(j) < len(hs):
                     lo, hi = _share(int(j), len(hs))
                     order("g", [V("qx%d" % r, lo, hi)], [])
                     write(hs[int(j)], T.hq[:, lo:hi].bitcast(dt.uint8), q[:, lo:hi].bitcast(dt.uint8), "hc")
         else:
-            order("g", [V("qx%d" % r), V("sx%d" % r)], [])
-            write(dst, T["lq%d" % r][:].bitcast(dt.uint8), q[:].bitcast(dt.uint8), "rf%d" % r)
-            write(dst, T["ls%d" % r][:], s[:], "rf%d" % r)
+            order("g", [V("qx%d" % r, 0, C), V("sx%d" % r, 0, C)], [])
+            write(dst, T["lq%d" % r][:].bitcast(dt.uint8), q[:, 0:C].bitcast(dt.uint8), "rf%d" % r)
+            write(dst, T["ls%d" % r][:], s[:, 0:C], "rf%d" % r)
         note(None, "rf%d" % r, sum(n_in) + n_in[0], [], [V("lq%d" % r), V("ls%d" % r)])
 
     def col(name, c):
@@ -357,9 +286,6 @@ def rank_program(g, core, T, topo):
     def wrapped(name, lo=0, hi=None):
         v = V(name, lo, hi)
         return (name, lo + 15, v[2], 16)
-
-    def win(b, lo, hi):
-        return V("win", b * WW + lo, b * WW + hi)
 
     def slot(c, lo, hi):
         for k, (runs, n) in enumerate(TILES):
@@ -371,15 +297,18 @@ def rank_program(g, core, T, topo):
         return V("qe", 128 * b, 128 * b + 128), V("se", 128 * b, 128 * b + 128)
 
     def cut(b):
-        o = EW * (2 * (b // 4) + b % 2) + 2 - 2 * (b % 4 // 2)
+        o = EW * (b % 2) + 2 - 2 * (b // 2)
         quant(*eb(b), V("et", o, o + 512))
 
     def bank(b, n):
         return V("ps%d" % (2 + b), 0, n)
 
-    BACK = col("qcol", 2)
+    def win(b, lo, hi):
+        return V("win", b * WW + lo, b * WW + hi)
 
-    H = C // 2
+    BACK = col("qcol", 2)
+    INRUN = RS - 16
+
     dma("s", "ldu", T.ut[:], T.u[:], [], [V("ut")])
     dma("y", "ldx", T.x0[:], T.x[:], [], [V("x0")])
     dma("y", "ldw", T.qw[:].bitcast(dt.uint8), T.wc[:], [V("x0"), V("ut")], [V("qw")])
@@ -389,75 +318,74 @@ def rank_program(g, core, T, topo):
     def select(o, z, n, c, base, cm):
         op("g", lambda: g.affine_select(ap(o), ap(z), [[-1, n]], ALU.not_equal, c, base, cm), [z], [o])
 
+    def band(o, z, step, c, base, cm):
+        op("g", lambda: g.affine_select(ap(o), ap(z), [[step, 8], [0, 64]], ALU.is_ge, c, base, cm), [z], [o])
+
+    def const(out, c):
+        act(out, V("zero", 0, len(range(out[1], out[2], out[3]))), ACT.Identity, bias=c)
+
     def blank(k):
-        a, b = 4 * (TOFF[k] + 16 * TILES[k][0][-1]), 4 * TOFF[k + 1]
-        act(V("wt", a, b), V("zero", 0, b - a), ACT.Copy)
+        act(V("wt", 4 * (TOFF[k] + 16 * TILES[k][0][-1]), 4 * TOFF[k + 1]), V("zero", 0, 4 * TILES[k][1] - 64 * TILES[k][0][-1]), ACT.Copy)
 
     def partitions():
         ts(col("ipc", 1), col("ipc", 0), 15, ALU.bitwise_and)
-        ts(col("ipc", 2), col("ipc", 0), 4, ALU.arith_shift_right)
-        cp(V("qcol", 0, 2), V("ipc", 1, 3))
-
-    def starts(name, c, c0):
-        act(V(name), V("zero", 0, C), ACT.Identity, bias=c)
-        act(V(name, 0, C, 16), V("zero", 0, NC), ACT.Identity, bias=c0)
+        cp(col("qcol", 0), col("ipc", 1))
 
     def table():
-        for lo, hi, f in ((0, A, 2), (A, A + K, 1), (A + K, C, 0)):
+        for lo, hi, f in ((0, A, 2.0), (A, KEPT, 1.0), (KEPT, C, 0.0)):
             iota(V("tab", lo, hi), [[0, hi - lo]], int(f * MU), 0, True)
 
     def small():
-        act(V("kb"), V("i16", 0, 8), ACT.Identity, bias=col("qcol", 0))
-        act(V("kc"), V("i16", 0, 8), ACT.Identity, bias=float(EL), scale=2.0)
-        act(col("cm", 0), col("zero", 0), ACT.Copy)
-        act(V("kb"), V("kb"), ACT.Identity, bias=0.5)
-        act(col("qcol", 3), BACK, ACT.Identity, bias=-float(A))
+        for c, a, b in ((2, 15 * DROP, -DROP), (3, MID - 15, 1.0), (4, 15 * DROP - A, -DROP), (6, 0.5, 1.0)):
+            act(col("qcol", c), col("qcol", 0), ACT.Identity, bias=a, scale=b)
+        const(col("cm", 0), 0.0)
 
     once = {
         "iu": lambda: iota(V("iu"), [[16, 8]], 0, 0), "ip": lambda: iota(col("ipc", 0), [[0, 1]], 0, 1),
         "jr": lambda: iota(V("jr"), [[0, NC], [1, 16]], 0, 0, True), "i16": lambda: iota(V("i16"), [[16, NC]], 0, 0, True),
-        "ig": lambda: iota(V("ig"), [[1, 8], [0, 64]], 0, 0, True), "cols": lambda: iota(V("cols"), [[1, C]], 0, 0, True),
-        "val3": lambda: iota(V("val3"), [[1, K]], C, 0, True), "tab": table,
-        "zero": lambda: fill(V("zero"), 0.0), "et": lambda: fill(V("et", 0, 2 * EW), 0.0),
-        "offu": lambda: cp(V("offu"), V("iu")), "qcol": partitions, "rk": lambda: act(col("rk", RS - 1), col("zero", 0), ACT.Copy),
-        "seg": lambda: starts("seg", 1.0, 0.0), "d0s": lambda: starts("d0s", 0.0, -BIG),
+        "ig": lambda: band(V("ig"), V("zero", 0, 512), 16, 1.0, -1, -1), "cols": lambda: iota(V("cols"), [[1, WW]], 0, 0, True),
+        "tab": table, "zero": lambda: fill(V("zero"), 0.0), "et": lambda: fill(V("et"), 0.0),
+        "offu": lambda: cp(V("offu"), V("iu")), "qcol": partitions,
+        "d0s": lambda: const(V("d0s"), 0.0), "d0t": lambda: const(V("d0s", 0, C, 16), -BIG), "seg": lambda: const(V("seg"), 2 * MID),
+        "seh": lambda: act(V("seg", 0, C, 16), V("i16"), ACT.Identity, bias=col("qcol", 3), scale=-1.0),
+        "kb": lambda: act(V("kb"), V("i16", 0, 8), ACT.Identity, bias=col("qcol", 6)),
         "qu": lambda: quant(V("qu"), V("su"), V("ut")), "qv": lambda: quant(V("qv"), V("sv"), V("vt")),
         "qu2": lambda: op("v", lambda: g.vector.tensor_copy(T.qu2[:, 0:128].bitcast(dt.uint32), T.qu[:, 0:128].bitcast(dt.uint32)
                                                             .indirect(T.offu[:, 0:8])), [V("qu"), V("offu")], [V("qu2")]),
         "su2": lambda: act(V("su2"), V("su"), ACT.Copy, off=V("offu")),
         "mk": lambda: ts(V("mk"), V("jr"), col("qcol", 0), ALU.not_equal, -BIG, ALU.mult),
-        "dg": lambda: ts(V("dg"), V("jr"), col("qcol", 0), ALU.is_equal),
-        "d0g": lambda: act(V("d0g"), V("dg"), ACT.Identity, bias=-DROP, scale=64 * DROP),
-        "nb": lambda: ts(V("nb"), V("i16"), col("qcol", 0), ALU.subtract, 15.0, ALU.add),
-        "back": lambda: act(BACK, col("qcol", 0), ACT.Identity, bias=15 * DROP, scale=-DROP), "small": small,
-        "gt": lambda: ts(V("gt"), V("ig"), col("qcol", 1), ALU.is_equal), "qg": lambda: quant(V("qg"), V("sg"), V("gt")),
+        "d0g": lambda: act(V("d0g"), V("mk"), ACT.Identity, bias=63 * DROP, scale=64 * DROP / BIG),
+        "pad": lambda: iota(V("x1", 4 * C), [[0, 4 * (XW - C)]], 0, 0, True), "small": small,
+        "gt": lambda: band(V("gt"), V("ig"), 16, 0.0, 15, -1), "qg": lambda: quant(V("qg"), V("sg"), V("gt")),
     }
     for h in range(2):
         once["one%d" % h] = lambda h=h: select(V("et", h * EW + 2 + h, h * EW + EW, 4), V("zero", 0, EW // 4), EW // 4, 1.0, 0, 1)
-        once["neg%d" % h] = lambda h=h: select(V("et", (h + 2) * EW, (h + 3) * EW), V("zero"), EW, -1.0, 2 + h, 4)
 
-    for r in range(3):
-        rw, lr, qx, sx = "rw%d" % r, "lr%d" % r, V("qx%d" % r), V("sx%d" % r)
+    def round_steps(r):
+        rw, lr, qx, sx = "rw%d" % r, "lr%d" % r, V("qx%d" % r, 0, C), V("sx%d" % r, 0, C)
 
-        def scores():
-            for lo, hi in QX:
-                quant(V(qx[0], lo, hi), V(sx[0], lo, hi), V("x1" if r else "x0", 4 * lo, 4 * hi))
+        cut_at = KEPT if r else C - K
+
+        def pack_x(n, lo, hi):
+            quant(V("qx%d" % n, lo, hi), V("sx%d" % n, lo, hi), V("x1" if n else "x0", 4 * lo, 4 * hi))
 
         def score(k):
-            lo = C - K if k == 7 else 0
-            mm(V("ps%d" % k, 0, C - lo), V("qu2"), V("su2"), V(qx[0], lo, C), V(sx[0], lo, C))
+            lo, hi = (cut_at, cut_at + K) if k == 7 else (0, C)
+            mm(V("ps%d" % k, 0, hi - lo), V("qu2"), V("su2"), V(qx[0], lo, hi), V(sx[0], lo, hi))
 
-        def picks(k):
-            lo, hi = PICKS[k]
-            p = V("ps7", lo - C + K, hi - C + K) if EARLY and k == 0 else V("ps0", lo, hi)
+        def masked(lo, hi):
+            p = V("ps7", lo - cut_at, hi - cut_at) if lo else V("ps0", lo, hi)
             tt(V("rm", lo, hi), p, V("mk", lo, hi), ALU.add)
+
+        def picks(lo, hi):
             scan(V("wf", lo, hi), V("d0s", lo, hi), V("rm", lo, hi), -BIG, ALU.add, ALU.max)
 
         def compare(c):
             ts(slot(c, 0, 16 * c), V("ps0", 0, 16 * c), col("wf", 16 * c + 15), ALU.is_lt)
 
         def count(c):
-            scan(V("rk", RS * (c + 1) - 8 * c, RS * (c + 1)), slot(c, 0, 8 * c), slot(c, 8 * c, 16 * c), 0.0, ALU.add, ALU.add)
+            scan(V("rk", RS * (c + 1) - 8 * c, RS * (c + 1)), slot(c, 0, 8 * c), slot(c, 8 * c, 16 * c),
+                 col("rk", INRUN + 16 * c + 15), ALU.add, ALU.add)
 
         def sign(c):
             act(slot(c, 0, 16 * c), V("ps1", 0, 16 * c), ACT.Sign, bias=col("wf", 16 * c + 15), scale=-1.0)
@@ -465,158 +393,150 @@ def rank_program(g, core, T, topo):
         def sums(c):
             act(slot(c, 0, 16 * c), slot(c, 0, 16 * c), ACT.Relu, acc=col("pa", c))
 
-        packed = []
-
         def pack(k):
             a, b = TOFF[k], TOFF[k + 1]
-            both = k == 3 and "p4" not in ORDER[r].split()
-            if both:
+            if k == 3 and r:
                 b += 16 * TILES[4][0][0]
             quant(V("qt", a, b), V("stp", a, b), V("wt", 4 * a, 4 * b))
-            packed.extend([3, 4] if both else [k])
-            if 0 in packed:
-                todo = ([3, 4] if both else [k]) if k else [0] + packed[:-1]
-                for j in todo:
-                    a, b = TOFF[j], TOFF[j + 1]
-                    mm(V("ps6", 0, b - a), V("qg"), V("sg"), V("qt", a, b), V("stp", a, b), j == 0,
-                       len(packed) == len(TILES) and j == todo[-1])
+
+        summed = []
+
+        def over_partitions(k):
+            a, b = TOFF[k], TOFF[k + 1]
+            summed.append(k)
+            mm(V("ps6", 0, b - a), V("qg"), V("sg"), V("qt", a, b), V("stp", a, b), k == 0, len(summed) == len(TILES))
 
         def unpack_own(b):
             mm(bank(b, C), *eb(b), qx, sx)
 
         def keep(b):
-            move(TC[b], win(b, 0, C), bank(b, C), None, 64.0)
+            move(WHO["t"][r][b], win(b, 0, C), bank(b, C), None, 64.0)
 
         def again(b):
             mm(bank(b, C), *eb(b), qx, sx, True, False)
 
-        def unpack(b):
-            p = V("ps7" if b % 2 == 0 else "ps1", 0, C)
-            mm(p, *eb(b), V("lq%d" % r), V("ls%d" % r))
-            move(UC[r][b], V("ff", b, 4 * C, 4), p)
+        def far(b):
+            return V(("ps7", "ps1", "ps0", "ps7")[b], 0, C)
 
-        def pack_far():
-            quant(V("qf"), V("sf"), V("ff"))
-            for b in range(4):
-                mm(bank(b, C), *eb(4 + b), V("qf"), V("sf"), False, True)
+        def unpack(b):
+            mm(far(b), *eb(b), V("lq%d" % r), V("ls%d" % r))
+
+        def product(b):
+            mm(bank(b, K), V("qw", 128 * b, 128 * b + 128), V("sw", 128 * b, 128 * b + 128), V("qz"), V("sz"))
+
+        def sums_on_s():
+            for c in ON_S:
+                if c - 1 not in ON_S:
+                    e = min(k for k in range(c, NC + 1) if k not in ON_S)
+                    tt(V("rk", RS * c + RS - 1, RS * e, RS), wrapped("rk", INRUN + 16 * c, INRUN + 16 * e), V("pa", c, e), ALU.add)
 
         def shared(c):
-            e, w, last = V("ej", EL * c, EL * c + EL), V("cs", 16 * c, 16 * c + EL), EH * c + EH - 1
-            if c in COUNT_V:
-                ts(e, w, col("kb", c), ALU.is_lt, 2.0, ALU.mult)
+            e, w = V("ej", EL * c, EL * c + EL), V("cs", 16 * c, 16 * c + EL)
+            if c < COUNT_V:
+                ts(e, w, col("kb", c), ALU.is_lt)
             else:
-                act(e, w, ACT.Sign, bias=col("kb", c), scale=-1.0, acc=col("er", last))
+                act(e, w, ACT.Sign, bias=col("kb", c), scale=-1.0, acc=col("er", EH * c + EH - 1))
 
         def shared_sum(c):
-            scan(V("er", EH * c, EH * c + EH), V("ej", EL * c, EL * c + EH), V("ej", EL * c + EH, EL * c + EL), -float(EL), ALU.add, ALU.add)
+            scan(V("er", EH * c, EH * c + EH), V("ej", EL * c, EL * c + EH), V("ej", EL * c + EH, EL * c + EL), 16.0 * c, ALU.add, ALU.add)
 
-        def product():
-            quant(V("qz"), V("sz"), V("zt"))
-            for b in range(4):
-                mm(bank(b, K), V("qw", 128 * b, 128 * b + 128), V("sw", 128 * b, 128 * b + 128), V("qz"), V("sz"))
-
-        def near(b):
-            move(NG[b], V("f64", b * K, b * K + K), win(b, 0, C), V("eo"))
-
-        def whole():
-            ts(V("pi", 0, N2), wrapped("cx", 0, A), BACK, ALU.add, FLAG + 255.0, ALU.add)
-            ts(V("pi", N2, NC), wrapped("cx"), BACK, ALU.add)
+        def list_e():
+            cp(V("eo", 0, COUNT_V), V("er", EH - 1, EH * COUNT_V, EH))
+            for c in range(COUNT_V, 8):
+                ts(col("eo", c), col("er", EH * c + EH - 1), 0.5, ALU.mult, 16.0 * c + EH, ALU.add)
 
         def flags():
             for lo, hi, c in ((0, N2, 1.0), (N2, N1, 0.0)):
                 act(V("ml", 16 * lo, 16 * hi), V("mr"), ACT.Identity, bias=2 * FLAG + c, scale=-FLAG / MU, off=V("oa", lo, hi))
 
+        def whole():
+            ts(V("pi", 0, N2), wrapped("cx", 0, A), BACK, ALU.add, FLAG + 255.0, ALU.add)
+            ts(V("pi", N2, NC), wrapped("cx"), BACK, ALU.add)
+
         def parts():
             ts(V("hi"), V("pi"), 8, ALU.arith_shift_right, 1535, ALU.bitwise_and)
             ts(V("lo"), V("pi"), 255, ALU.bitwise_and)
 
-        def name_updated():
-            if r == 2:
-                act(V("nlb"), V("nrow"), ACT.Copy)
-                dma("y", "st", T.nl[:, :], T.nlb[0:128:16, :], [V("nlb")], [])
-            scatter(V("nrow"), V("sko"), V("val3"))
-
-        def new():
-            for q, b in LATE:
-                move(q, V("x1", b, 4 * C, 4), win(b, 0, WW), V("no"), 0.015625)
-
-        def last(h):
-            lo, hi = h * H, h * H + H
-            for q, b in LATE:
-                move(q, V("x1", 4 * lo + b, 4 * hi, 4), win(b, 0, WW), V("no", lo // 16, hi // 16), 0.015625)
-            quant(V("qx3", lo, hi), V("sx3", lo, hi), V("x1", 4 * lo, 4 * hi))
-            mm(V("ps%d" % h, 0, H), V("qv"), V("sv"), V("qx3", lo, hi), V("sx3", lo, hi))
-
-        def codes_out(lo, hi):
-            dma("y", "st", T.oc[:, 4 * lo:4 * hi], T.qx3[:, lo:hi].bitcast(dt.uint8), [V("qx3", lo, hi)], [])
+        def gather_new(q, b, lo, hi, w):
+            move(q, V("x1", 4 * lo + b, 4 * hi, 4), win(b, 0, w), V("no", lo // 16, hi // 16), 0.015625)
 
         def result(h):
-            move(YC[h], V("ysb", h * H, h * H + H), V("ps%d" % h, 0, H))
+            lo, hi = ((0, KEPT), (KEPT, C))[h]
+            move(WHO["o"][r][h], V("ysb", lo, hi), V("ps%d" % h, 0, hi - lo))
 
         def result_out(q, lo, hi):
             dma(q, "st", T.y[:, lo:hi], T.ysb[:, lo:hi], [V("ysb", lo, hi)], [])
 
-        def scales(k):
-            dma(OSQ[k], "st", T.osc[4 * k:4 * k + 4, :], T.sx3[32 * k:32 * k + 4, :], [V("sx3")], [])
+        def codes_out(lo, hi):
+            dma("y", "st", T.oc[:, 4 * lo:4 * hi], T.qx3[:, lo:hi].bitcast(dt.uint8), [V("qx3", lo, hi)], [])
 
-        def whole_last():
-            new()
-            for h in range(2):
-                quant(V("qx3", h * H, h * H + H), V("sx3", h * H, h * H + H), V("x1", 4 * h * H, 4 * h * H + 4 * H))
-                mm(V("ps%d" % h, 0, H), V("qv"), V("sv"), V("qx3", h * H, h * H + H), V("sx3", h * H, h * H + H))
+        def scales(k):
+            dma(OSQ[k], "st", T.osc[4 * k:4 * k + 4, :], T.sx3[32 * k:32 * k + 4, 0:C], [V("sx3", 0, C)], [])
+
+        def last(h):
+            lo, hi = ((0, KEPT), (KEPT, KEPT + K))[h]
+            mm(V("ps%d" % h, 0, hi - lo), V("qv"), V("sv"), V("qx3", lo, hi), V("sx3", lo, hi))
 
         steps = {
-            "qx": scores, "codes": lambda: send(r, "codes"), "wa": lambda: picks(0), "wb": lambda: picks(1),
-            "shs": lambda: act(V("sh"), V("mr"), ACT.Sign),
-            "in": lambda: tt(slot(0, 0, C), V("ps0", 0, C), V("wf"), ALU.is_le),
-            "eq": lambda: scan(V("eqs"), V("seg"), slot(0, 0, C), 0.0, ALU.mult, ALU.add),
-            "e2": lambda: tt(V("e2"), V("nb"), wrapped("eqs"), ALU.subtract),
-            "e3s": lambda: tt(V("e3", NV, NC), V("e2", NV, NC), V("pa", NV, NC), ALU.subtract),
-            "e3v": lambda: tt(V("e3", 0, NV), V("e2", 0, NV), V("rk", RS - 1, NV * RS, RS), ALU.subtract),
-            "cw": lambda: hold(V("cw"), V("ps6", 0, C)), "pd": lambda: tt(V("pd"), V("e3"), wrapped("cw"), ALU.add),
-            "rw": lambda: ts(V(rw), V("pd"), BACK, ALU.add), "places": lambda: send(r, "places"),
-            "orow": lambda: scatter(V("sval", A, A + C), V(rw), V("cols")),
-            "fq": lambda: act(V("fq"), V("tab"), ACT.Copy, off=V(rw)), "fqv": lambda: cp(V("fq"), V("tab"), V(rw)),
-            "f1": lambda: ts(V("fr"), V("fq"), 1.0 / MU, ALU.mult),
-            "ox": lambda: hold(V("ox"), V("sval", A, 2 * A + K)), "oa": lambda: ts(V("oa"), wrapped("ox"), BACK, ALU.add),
-            "sv": lambda: act(V("sval", 0, A), V("sval", A, 2 * A), ACT.Copy), "qf": pack_far,
+            "qa": lambda: pack_x(r, cut_at, cut_at + K), "qb": lambda: pack_x(r, 0, cut_at),
+            "la": lambda: pack_x(3, KEPT, KEPT + K), "lb": lambda: pack_x(3, 0, KEPT), "ya": lambda: last(1), "yb": lambda: last(0),
+            "codes": lambda: send(r, "codes"), "ma": lambda: masked(PICK[r], C), "mb": lambda: masked(0, PICK[r]),
+            "wa": lambda: picks(PICK[r], C), "wb": lambda: picks(0, PICK[r]),
+            "ia": lambda: tt(slot(0, PICK[r], C), V("ps7", PICK[r] - cut_at, C - cut_at), V("wf", PICK[r], C), ALU.is_le),
+            "in": lambda: tt(slot(0, 0, PICK[r]), V("ps0", 0, PICK[r]), V("wf", 0, PICK[r]), ALU.is_le),
+            "eq": lambda: scan(V("rk", INRUN, INRUN + C), V("seg"), slot(0, 0, C), 2 * MID, ALU.min, ALU.add),
+            "e3s": sums_on_s, "cw": lambda: hold(V("cw"), V("ps6", 0, C)),
+            "pd": lambda: tt(V("pd"), wrapped("cw"), V("rk", RS - 1, RS * NC, RS), ALU.subtract),
+            "rw": lambda: ts(V(rw), V("pd"), BACK, ALU.add, MID, ALU.add), "places": lambda: send(r, "places"),
+            "orow": lambda: scatter(V("sval", A, A + C), V(rw), V("cols", 0, C)),
+            "sv": lambda: select(V("sval", 0, A), V("sval", A, 2 * A), A, 0.0, -1, 0),
+            "fq": lambda: move(WHO["fq"][r], V("fq"), V("tab"), V(rw)),
+            "fp": lambda: move(WHO["fp"][r], V("fr"), V("fq"), None, 1.0 / MU),
+            "ox": lambda: hold(V("ox"), V("sval", A, A + KEPT)), "oa": lambda: ts(V("oa"), wrapped("ox"), BACK, ALU.add),
+            "qf": lambda: quant(V("qf"), V("sf"), V("ff")),
             "m": lambda: tt(V("mr"), V("tab"), V("fq"), ALU.min, off=V(lr)),
-            "sh": lambda: ts(V("sh"), V("mr"), 1.0, ALU.min),
-            "cs": lambda: scan(V("cs"), V("zero", 0, C), V("sh"), 0.0, ALU.add, ALU.add),
-            "cm": lambda: scan(V("cm", 1, C + 1), V("fr"), V("mr"), 0.0, ALU.add, ALU.add),
-            "ml": flags, "svv": lambda: cp(V("sval", 0, A), V("sval", A, 2 * A)),
-            "svg": lambda: op("g", lambda: g.affine_select(ap(V("sval", 0, A)), ap(V("sval", A, 2 * A)), [[0, A]], ALU.is_ge, 0.0, 0, 0),
-                              [V("sval", A, 2 * A)], [V("sval", 0, A)]),
-            "mqv": lambda: ts(col("tot", 0), col("cm", C), MU / 4 - C, ALU.add, 1.0 / MU, ALU.mult),
+            "sh": lambda: ts(V("sh"), V("mr"), 1.0, ALU.min) if WHO["sh"][r] == "v" else act(V("sh"), V("mr"), ACT.Sign),
+            "cs": lambda: scan(V("cs"), V("zero", 0, C), V("sh"), 0.0, ALU.add, ALU.add), "eo": list_e,
+            "cm": lambda: scan(V("cm", 1, C + 1), V("fr"), V("mr"), 0.0, ALU.add, ALU.add), "ml": flags,
             "cg": lambda: tt(V("cg"), V("cm", 0, C), V("ml"), ALU.add, off=V("oa")), "cx": lambda: hold(V("cx"), V("cg")),
             "pi": whole, "hr": parts,
             "mq": lambda: act(col("tot", 0), col("cm", C), ACT.Identity, bias=0.25 - C / MU, scale=1.0 / MU),
             "rr": lambda: ts(V("rr"), V("lo"), col("tot", 0), ALU.add),
             "sl": lambda: tt(V("sl"), V("rr"), V("hi"), ALU.min), "so": lambda: cp(V("so"), V("sl")),
             "sc": lambda: scatter(V("nrow"), V("so"), V("sval", 0, C)),
-            "e1": lambda: tt(V("ka"), V("er", EH - 1, 8 * EH, EH), V("kc"), ALU.add), "e2o": lambda: ts(V("eo"), V("ka"), 0.5, ALU.mult),
-            "sk": lambda: act(V("sk"), V("cm", 0, C), ACT.Copy, off=V("eo")), "skv": lambda: cp(V("sk"), V("cm", 0, C), V("eo")),
-            "skh": lambda: hold(V("skx"), V("sk")),
-            "sk1": lambda: ts(V("sko"), wrapped("skx"), col("qcol", 3), ALU.add, 2.0 ** -8, ALU.mult),
-            "fix": name_updated,
-            "qz": product, "nx": lambda: hold(V("nx"), V("nrow")),
-            "no": lambda: ts(V("no"), wrapped("nx"), BACK, ALU.add), "new": new, "last": whole_last,
-            "oc": lambda: codes_out(0, C), "oca": lambda: codes_out(0, H), "ocb": lambda: codes_out(H, C),
-            "y": lambda: result_out("s", 0, C), "ya": lambda: result_out(YQ[0], 0, H), "yb": lambda: result_out(YQ[1], H, C),
+            "ny": lambda: hold(V("nx", KEPT, C), V("nrow", KEPT, C)), "ne": lambda: ts(V("no", N1, NC), wrapped("nx", KEPT, C), BACK, ALU.add),
+            "sk": lambda: move(WHO["sk"][r], V("sk"), V("cm", 0, C), V("eo")), "skh": lambda: hold(V("skx"), V("sk")),
+            "sko": lambda: ts(V("sko"), wrapped("skx"), col("qcol", 4), ALU.add, 2.0 ** -8, ALU.mult),
+            "fix": lambda: scatter(V("nrow", 0, KEPT), V("sko"), V("cols", C)),
+            "nx": lambda: hold(V("nx", 0, KEPT), V("nrow", 0, KEPT)), "no": lambda: ts(V("no", 0, N1), wrapped("nx", 0, KEPT), BACK, ALU.add),
+            "qz": lambda: quant(V("qz"), V("sz"), V("zt")), "nc": lambda: act(V("nlb"), V("nrow"), ACT.Copy),
+            "nl": lambda: dma("y", "st", T.nl[:, :], T.nlb[0:128:16, :], [V("nlb")], []),
+            "yo": lambda: result_out("s", 0, KEPT), "ye": lambda: result_out("y", KEPT, C),
+            "oc": lambda: codes_out(0, KEPT), "oe": lambda: codes_out(KEPT, C),
         }
-        each = {"i": scales, "l": last, "o": result, "x": cut, "j": near, "w": unpack_own, "q": score, "b": blank,
-                "s": sign, "r": sums, "c": compare, "n": count, "p": pack, "t": keep, "d": again, "u": unpack, "k": shared, "v": shared_sum,
-                "z": lambda b: act(V("zw", b * C, b * C + C), bank(b, C), ACT.Copy),
-                "y": lambda b: cp(V("zw", b * C, b * C + C), bank(b, C)),
-                "g": lambda b: move(ZG[b], V("zt", b, 4 * K, 4), V("zw", b * C, b * C + C), V("eo")),
-                "a": lambda b: tt(win(b, C, WW), bank(b, K), V("f64", b * K, b * K + K), ALU.add)}
-        for name in ORDER[r].split():
+        each = {"i": scales, "o": result, "x": cut, "w": unpack_own, "q": score, "b": blank,
+                "s": sign, "r": sums, "c": compare, "n": count, "p": pack, "t": keep, "d": again, "h": unpack, "f": over_partitions, "k": product,
+                "u": lambda b: move(WHO["u"][r][b], V("ff", b, 4 * C, 4), far(b), None, -1.0),
+                "v": lambda b: mm(bank(b, C), *eb(b), V("qf"), V("sf"), False, True),
+                "z": lambda b: move(WHO["z"][r][b], V("zw", b * C, b * C + C), bank(b, C)), "E": shared, "F": shared_sum,
+                "g": lambda b: move(WHO["g"][r][b], V("zt", b, 4 * K, 4), V("zw", b * C, b * C + C), V("eo")),
+                "j": lambda b: move(WHO["j"][r][b], V("f64", b * K, b * K + K), win(b, 0, C), V("eo")),
+                "a": lambda b: tt(win(b, C, WW), bank(b, K), V("f64", b * K, b * K + K), ALU.add),
+                "e": lambda b: gather_new(WHO["e"][r][b], b, KEPT, C, C), "l": lambda b: gather_new(WHO["l"][r][b], b, 0, KEPT, WW)}
+
+        def do(name):
             if name in steps:
                 steps[name]()
             elif name in once:
                 once[name]()
             else:
                 each[name[0]](int(name[1:]))
+        return do
+
+    rounds = [round_steps(r) for r in range(3)]
+    for r in range(3):
+        for name in ORDER[r].split():
+            rounds[r + name.startswith("+")](name.lstrip("+"))
 
     for s in SEMAPHORES:
         if total.get(s, 0):

from concourse.mybir import dt, AluOpType, ActivationFunctionType

ALU = AluOpType
ACT = ActivationFunctionType
C, A, K = 320, 96, 128
STEP = [1, 2, 4]
NC = C // 16
KEPT = A + K
N1, N2 = KEPT // 16, A // 16
WW = C + K
BIG = 2.0 ** 83
DROP = 2.0 ** 19
XW = KEPT + K
MID = 160.0
MU = 255.0
FLAG = 2.0 ** 17
EL = 2 * A + 16
EH = EL // 2
CODE = "float8_e4m3fn_x4"
TILES = [([0, 19, 18, 17], 320), ([16, 15, 14, 13], 256), ([12, 11, 10, 9], 192), ([8, 7, 6, 5], 128), ([4, 3, 2, 1], 128)]
TOFF = [sum(n for _, n in TILES[:k]) for k in range(len(TILES) + 1)]
RS = C
EW = 520
ORDER = [
    "zero et b1 iu b2 ip d0s jr qcol offu b0 one1 d0t qu small su2 mk qu2 x1 one0 b3 seg qa qb i16 q7 q0 x2 q1 ma codes x0 w1 wa b4 mb "
    "seh ia c16 wb c14 in c10 c2 s19 s17 ig eq c3 c5 gt c6 c4 c8 c15 s18 n16 s12 r17 w0 r18 r19 s13 c9 s11 c1 n10 c7 r12 n2 qg r13 p0 n3 "
    "r11 p1 p2 p3 p4 n4 n1 n15 n7 n8 f0 cols n9 f1 n6 f2 n5 t0 d0g n14 f3 t1 e3s f4 tab pad h2 cw h0 u2 x3 u0 w2 w3 h3 pd kb rw orow fq "
    "t2 places m t3 ox h1 sh fp oa cm u1 d2 d1 u3 d3 cs ml mq qf cg E7 E5 E0 cx v1 d0 E1 pi v3 E4 E6 E3 v0 E2 F0 F1 v2 hr z3 rr eo z1 z2 "
    "sl so g1 g2 z0 g3 sv g0 sk sc skh j3 ny sko qz ne k1 j0 j2 k2 e1 fix e0 k0 e2 e3 nx a2 j1 no +qa a0 k3 l2 +q7 a1 a3 +ma l3 +wa +ia "
    "l0 l1 ",
    "qb q0 mb c14 q1 s18 w0 codes wb s17 r18 c16 c5 c6 s12 in s13 s19 c3 c15 r17 eq c8 c2 c9 r19 n16 w3 c1 c10 w2 n3 n1 c7 s11 p0 r13 w1 "
    "n10 r12 f0 p1 c4 n2 r11 p2 p3 f1 n5 n4 f2 f3 n14 n15 n8 n6 n7 n9 e3s f4 cw qv pd rw places t1 t0 t2 t3 h0 u0 h1 h2 h3 orow u1 u2 d1 "
    "d2 u3 qf v2 fq ox d0 m v1 oa sh fp cm ml cs cg z2 d3 E0 cx E1 mq E4 v0 E2 pi F0 hr E7 sv v3 E5 E3 E6 F1 rr sl z3 eo z1 so z0 sk sc "
    "g3 skh g1 g2 ny g0 j3 j1 j0 sko qz ne k2 fix k3 e3 e2 k1 e1 k0 nx a3 e0 no j2 +qa a0 a1 l3 +q7 a2 +ma l0 l2 l1 +wa +ia ",
    "qb q0 mb q1 c15 wb s18 c14 c9 s19 s17 c3 c2 r18 w1 c8 in r17 w0 c6 s13 c7 c5 w2 eq r19 s12 c16 n8 c4 s11 n5 r13 c1 p0 r11 p3 c10 p1 "
    "r12 p2 f0 e3s n10 n14 w3 n9 t2 f1 n4 f2 n6 n15 n1 t0 f3 f4 n16 n3 n2 codes h0 n7 cw pd h1 rw h2 t1 u0 d2 orow places h3 u2 d0 u1 u3 "
    "fq d1 t3 qf ox m fp oa sh cm v2 z2 ml cs v1 z1 d3 E5 cg v0 E3 E0 E6 cx sv E4 E1 mq pi E2 F0 hr E7 v3 z3 F1 rr sl eo z0 g1 sk g3 so "
    "sc skh g0 ny g2 nc sko qz j2 ne nl j0 fix j1 e2 k2 nx e3 e1 a2 k0 e0 a0 k3 j3 no k1 a1 l0 la oe l1 ya o1 a3 l2 l3 ye lb i2 oc yb i3 "
    "i1 i0 o0 yo "]
WHO = {k: ["ssss"] * 3 for k in "tuzgjelo"}
WHO.update({"z": ["ssss", "vsss", "ssss"], "g": ["ssss", "ssss", "vsss"], "j": ["ssss", "ssss", "svss"], "e": ["ssvs", "svss", "ssss"],
            "l": ["sssv", "svss", "ssvv"], "fq": "sss", "fp": "sss", "sh": "vvv", "sk": "vss"})
ON_S = (11, 12, 13, 17, 18, 19)
COUNT_V = 2
OSQ = "yyss"
FEW, SENDS = 128, "s10"
PICK = (KEPT, KEPT, KEPT)


def _sb(n, d):
    return ("sbuf", [128, n], d)


SCRATCH = {
    "x0": _sb(4 * C, "bfloat16"), "x1": _sb(4 * XW, "bfloat16"), "ut": _sb(512, "bfloat16"), "vt": _sb(512, "bfloat16"),
    "qu": _sb(128, CODE), "su": _sb(128, "uint8"),
    "qu2": _sb(128, CODE), "su2": _sb(128, "uint8"), "qv": _sb(128, CODE), "sv": _sb(128, "uint8"),
    "qw": _sb(512, CODE), "sw": _sb(512, "uint8"), "et": _sb(2 * EW, "bfloat16"),
    "qe": _sb(512, CODE), "se": _sb(512, "uint8"), "qf": _sb(C, CODE), "sf": _sb(C, "uint8"),
    "qz": _sb(K, CODE), "sz": _sb(K, "uint8"), "zt": _sb(4 * K, "bfloat16"), "ff": _sb(4 * C, "bfloat16"),
    "f64": _sb(4 * K, "bfloat16"), "win": _sb(4 * WW, "bfloat16"), "zw": _sb(4 * C, "bfloat16"), "ysb": _sb(C, "float32"),
    "wt": _sb(4 * TOFF[-1], "bfloat16"), "qt": _sb(TOFF[-1], CODE), "stp": _sb(TOFF[-1], "uint8"),
    "ig": _sb(512, "bfloat16"), "gt": _sb(512, "bfloat16"), "qg": _sb(128, CODE), "sg": _sb(128, "uint8"),
    "iu": _sb(8, "int32"), "offu": _sb(8, "uint16"), "jr": _sb(C, "bfloat16"),
    "ipc": _sb(4, "int32"), "i16": _sb(NC, "float32"), "qcol": _sb(8, "float32"), "cols": _sb(WW, "float32"), "kb": _sb(8, "float32"),
    "mk": _sb(C, "bfloat16"), "d0s": _sb(C, "bfloat16"), "seg": _sb(C, "bfloat16"),
    "d0g": _sb(C, "bfloat16"), "tab": _sb(C, "bfloat16"), "zero": _sb(EW, "bfloat16"),
    "rm": _sb(C, "float32"), "wf": _sb(C, "float32"),
    "rk": _sb(NC * RS, "bfloat16"), "pa": _sb(NC, "float32"), "cw": _sb(C, "float32"), "pd": _sb(NC, "float32"),
    "fq": _sb(C, "bfloat16"), "fr": _sb(C, "bfloat16"),
    "sval": _sb(A + C, "float32"), "ox": _sb(KEPT, "float32"), "oa": _sb(N1, "uint16"),
    "mr": _sb(C, "bfloat16"), "cm": _sb(C + 16, "float32"), "ml": _sb(KEPT, "float32"), "cg": _sb(KEPT, "float32"), "cx": _sb(KEPT, "float32"),
    "pi": _sb(NC, "int32"), "hi": _sb(NC, "int32"), "lo": _sb(NC, "int32"), "tot": _sb(2, "float32"),
    "rr": _sb(NC, "float32"), "sl": _sb(NC, "float32"), "so": _sb(NC, "uint16"),
    "sh": _sb(C, "bfloat16"), "cs": _sb(C, "bfloat16"), "ej": _sb(8 * EL, "bfloat16"), "er": _sb(8 * EH, "float32"), "eo": _sb(8, "uint16"),
    "sk": _sb(K, "float32"), "skx": _sb(K, "float32"), "sko": _sb(8, "uint16"),
    "nrow": _sb(C, "float32"), "nlb": _sb(C, "float32"), "nx": _sb(C, "float32"), "no": _sb(NC, "uint16"),
    "hr": _sb(NC, "uint16"), "hq": _sb(C, CODE), "hs": _sb(C, "uint8"),
}
for _r in range(4):
    SCRATCH["qx%d" % _r] = _sb(XW, CODE)
    SCRATCH["sx%d" % _r] = _sb(XW, "uint8")
for _r in range(3):
    SCRATCH["rw%d" % _r] = _sb(NC, "uint16")
    SCRATCH["lr%d" % _r] = _sb(NC, "uint16")
    SCRATCH["lq%d" % _r] = _sb(C, CODE)
    SCRATCH["ls%d" % _r] = _sb(C, "uint8")
for _b in range(8):
    SCRATCH["ps%d" % _b] = ("psum", [128, 512], "float32")

SEMAPHORES = ["cv", "cs", "cp", "cg", "ldx", "ldu", "ldv", "ldw", "lds", "st", "sent", "ha", "hc", "hp",
              "ra0", "ra1", "ra2", "rf0", "rf1", "rf2"]


def _helpers(T, topo, src, dst):
    if topo.may_write(src, dst):
        return []
    c = [h for h in topo.cores_of(src) if T.rank_of(h) is None and topo.may_write(h, dst)]
    near = [h for h in c if topo.die(h) == topo.die(src)]
    return (near or c)[:2]


def _share(j, n):
    return (0, C) if n == 1 else ((0, FEW), (FEW, C))[j]


def _hand_on(g, core, T, topo):
    for r, h in enumerate(STEP):
        for i, src in enumerate(T.cores):
            dst = T.cores[i ^ h]
            hs = _helpers(T, topo, src, dst)
            if core not in hs:
                continue
            j = hs.index(core)
            lo, hi = _share(j, len(hs))
            n_in, n, m = len(topo.engines(src, core)), len(topo.engines(core, dst)), topo.mask(core, dst)
            rid, pid = topo.addr(dst, core)
            for what in SENDS:
                if what == str(j):
                    g.wait_ge(T.sem.hc, n_in)
                    g.remote_dma(T["lq%d" % r][:, lo:hi].bitcast(dt.uint8), T.hq[:, lo:hi].bitcast(dt.uint8),
                                 T.sem["rf%d" % r], T.sem.sent, pid, rid, m)
                if what == "s" and j == 0:
                    g.wait_ge(T.sem.hp, n_in)
                    g.remote_dma(T["ls%d" % r][:], T.hs[:], T.sem["rf%d" % r], T.sem.sent, pid, rid, m)
            if j == len(hs) - 1:
                g.wait_ge(T.sem.ha, n_in)
                g.remote_dma(T["lr%d" % r][:], T.hr[:], T.sem["ra%d" % r], T.sem.sent, pid, rid, m)
            g.wait_ge(T.sem.sent, (1 + (j == 0) + (j == len(hs) - 1)) * n)


def rank_program(g, core, T, topo):
    rank = T.rank_of(core)
    if rank is None:
        _hand_on(g, core, T, topo)
        return
    Q = {"v": g.vector, "s": g.scalar, "p": g.tensor, "g": g, "y": g.sync}
    own = {"v": "cv", "s": "cs", "p": "cp", "g": "cg"}
    total = {}
    know = {q: {} for q in Q}
    hist = {}

    def V(name, lo=0, hi=None, step=1):
        return (name, lo, SCRATCH[name][1][1] if hi is None else hi, step)

    def ap(v):
        return T[v[0]][:, v[1]:v[2]:v[3]] if v[3] != 1 else T[v[0]][:, v[1]:v[2]]

    def cols(v):
        return frozenset([0]) if v[0].startswith("ps") else frozenset(range(v[1], v[2], v[3]))

    def order(q, reads, writes, adds=False):
        need = {}
        for vs, wr in ((reads, False), (writes, True)):
            for v in vs:
                cs_, bank_ = cols(v), v[0].startswith("ps")
                for (c2, w2, q2, s, n, k) in hist.get(v[0], []):
                    if adds and wr and q2 == q and s == own.get(q):
                        continue
                    if (wr or w2 or (bank_ and q2 != q)) and know[q].get(s, 0) < n and cs_ & c2:
                        if need.get(s, (0, None))[0] < n:
                            need[s] = (n, k)
        for s in sorted(need, key=lambda a: -len(need[a][1])):
            n, k = need[s]
            if know[q].get(s, 0) >= n:
                continue
            Q[q].wait_ge(T.sem[s], n)
            for a, b in k.items():
                if know[q].get(a, 0) < b:
                    know[q][a] = b

    def note(q, s, inc, reads, writes):
        total[s] = total.get(s, 0) + inc
        k = dict(know[q]) if q else {}
        k[s] = total[s]
        for vs, wr in ((reads, False), (writes, True)):
            for v in vs:
                hist.setdefault(v[0], []).append((cols(v), wr, q, s, total[s], k))

    def op(q, make, reads, writes, adds=False):
        order(q, reads, writes, adds)
        make().then_inc(T.sem[own[q]], 1)
        note(q, own[q], 1, reads, writes)

    def dma(q, s, out, in_, reads, writes):
        order(q, reads, writes)
        Q[q].dma_start(out, in_).then_inc(T.sem[s], 16)
        note(q, s, 16, reads, writes)

    def aps(x):
        return [x] if isinstance(x, tuple) else []

    def val(x):
        return ap(x) if isinstance(x, tuple) else x

    def src(v, off):
        return ap(v).indirect(ap(off)) if off else ap(v)

    def ts(out, in0, s1, op0, s2=None, op1=None, off=None):
        rd = [in0] + aps(s1) + aps(s2) + aps(off)
        if op1 is None:
            op("v", lambda: g.vector.tensor_scalar(ap(out), src(in0, off), val(s1), None, op0), rd, [out])
        else:
            op("v", lambda: g.vector.tensor_scalar(ap(out), src(in0, off), val(s1), val(s2), op0, op1), rd, [out])

    def tt(out, in0, in1, o, off=None):
        op("v", lambda: g.vector.tensor_tensor(ap(out), src(in0, off), ap(in1), o), [in0, in1] + aps(off), [out])

    def cp(out, in_, off=None):
        op("v", lambda: g.vector.tensor_copy(ap(out), src(in_, off)), [in_] + aps(off), [out])

    def scatter(w, off, in_):
        op("v", lambda: g.vector.tensor_copy(ap(w).indirect(ap(off)), ap(in_)), [in_, off], [w])

    def scan(out, d0, d1, init, o0, o1):
        op("v", lambda: g.vector.tensor_tensor_scan(ap(out), ap(d0), ap(d1), val(init), o0, o1), [d0, d1] + aps(init), [out])

    def hold(out, in_):
        scan(out, V("d0g", 0, in_[2] - in_[1]), in_, 0.0, ALU.add, ALU.min)

    def fill(out, c):
        op("v", lambda: g.vector.memset(ap(out), c), [], [out])

    def quant(q, s, in_):
        op("v", lambda: g.vector.quantize_mx(ap(q), ap(s), ap(in_)), [in_], [q, s])

    def act(out, in_, f, bias=None, scale=None, acc=None, off=None):
        kw = {}
        if bias is not None:
            kw["bias"] = val(bias)
        if scale is not None:
            kw["scale"] = scale
        if acc is not None:
            kw["accum_out"] = ap(acc)
        op("s", lambda: g.scalar.activation(ap(out), src(in_, off), f, **kw), [in_] + aps(bias) + aps(off), [out] + aps(acc))

    def move(q, out, w, off=None, scale=1.0):
        if q == "s":
            act(out, w, ACT.Copy, scale=scale, off=off)
        else:
            ts(out, w, scale, ALU.mult, off=off)

    def mm(out, lq, ls, rq, rs, start=True, stop=True):
        op("p", lambda: g.tensor.matmul_mx(ap(out), ap(lq), ap(ls), ap(rq), ap(rs), start, stop), [lq, ls, rq, rs], [out], not start)

    def iota(out, pattern, base, cm, small=False):
        if small:
            op("g", lambda: g.iota(ap(out), pattern, base, cm, allow_small_or_imprecise_dtypes=True), [], [out])
        else:
            op("g", lambda: g.iota(ap(out), pattern, base, cm), [], [out])

    def send(r, what):
        dst = T.cores[rank ^ STEP[r]]
        hs, back = _helpers(T, topo, core, dst), _helpers(T, topo, dst, core)
        n_in = [len(topo.engines(h, core)) for h in (back or [dst])]

        def write(to, out, in_, s):
            rid, pid = topo.addr(to, core)
            g.remote_dma(out, in_, T.sem[s], T.sem.sent, pid, rid, topo.mask(core, to))
            total["sent"] = total.get("sent", 0) + len(topo.engines(core, to))

        if what == "places":
            order("g", [V("rw%d" % r)], [])
            write(hs[-1] if hs else dst, T["hr" if hs else "lr%d" % r][:], T["rw%d" % r][:], "ha" if hs else "ra%d" % r)
            note(None, "ra%d" % r, n_in[-1], [], [V("lr%d" % r)])
            return
        q, s = T["qx%d" % r], T["sx%d" % r]
        if hs:
            for j in SENDS:
                if j == "s":
                    order("g", [V("sx%d" % r, 0, C)], [])
                    write(hs[0], T.hs[:], s[:, 0:C], "hp")
                elif int(j) < len(hs):
                    lo, hi = _share(int(j), len(hs))
                    order("g", [V("qx%d" % r, lo, hi)], [])
                    write(hs[int(j)], T.hq[:, lo:hi].bitcast(dt.uint8), q[:, lo:hi].bitcast(dt.uint8), "hc")
        else:
            order("g", [V("qx%d" % r, 0, C), V("sx%d" % r, 0, C)], [])
            write(dst, T["lq%d" % r][:].bitcast(dt.uint8), q[:, 0:C].bitcast(dt.uint8), "rf%d" % r)
            write(dst, T["ls%d" % r][:], s[:, 0:C], "rf%d" % r)
        note(None, "rf%d" % r, sum(n_in) + n_in[0], [], [V("lq%d" % r), V("ls%d" % r)])

    def col(name, c):
        return V(name, c, c + 1)

    def wrapped(name, lo=0, hi=None):
        v = V(name, lo, hi)
        return (name, lo + 15, v[2], 16)

    def slot(c, lo, hi):
        for k, (runs, n) in enumerate(TILES):
            if c in runs:
                o = 4 * TOFF[k] + runs.index(c)
                return V("wt", o + 4 * lo, o + 4 * hi - 3, 4)

    def eb(b):
        return V("qe", 128 * b, 128 * b + 128), V("se", 128 * b, 128 * b + 128)

    def cut(b):
        o = EW * (b % 2) + 2 - 2 * (b // 2)
        quant(*eb(b), V("et", o, o + 512))

    def bank(b, n):
        return V("ps%d" % (2 + b), 0, n)

    def win(b, lo, hi):
        return V("win", b * WW + lo, b * WW + hi)

    BACK = col("qcol", 2)
    INRUN = RS - 16

    dma("s", "ldu", T.ut[:], T.u[:], [], [V("ut")])
    dma("y", "ldx", T.x0[:], T.x[:], [], [V("x0")])
    dma("y", "ldw", T.qw[:].bitcast(dt.uint8), T.wc[:], [V("x0"), V("ut")], [V("qw")])
    dma("y", "lds", T.sw[:], T.ws[:], [], [V("sw")])
    dma("y", "ldv", T.vt[:], T.v[:], [], [V("vt")])

    def select(o, z, n, c, base, cm):
        op("g", lambda: g.affine_select(ap(o), ap(z), [[-1, n]], ALU.not_equal, c, base, cm), [z], [o])

    def band(o, z, step, c, base, cm):
        op("g", lambda: g.affine_select(ap(o), ap(z), [[step, 8], [0, 64]], ALU.is_ge, c, base, cm), [z], [o])

    def const(out, c):
        act(out, V("zero", 0, len(range(out[1], out[2], out[3]))), ACT.Identity, bias=c)

    def blank(k):
        act(V("wt", 4 * (TOFF[k] + 16 * TILES[k][0][-1]), 4 * TOFF[k + 1]), V("zero", 0, 4 * TILES[k][1] - 64 * TILES[k][0][-1]), ACT.Copy)

    def partitions():
        ts(col("ipc", 1), col("ipc", 0), 15, ALU.bitwise_and)
        cp(col("qcol", 0), col("ipc", 1))

    def table():
        for lo, hi, f in ((0, A, 2.0), (A, KEPT, 1.0), (KEPT, C, 0.0)):
            iota(V("tab", lo, hi), [[0, hi - lo]], int(f * MU), 0, True)

    def small():
        for c, a, b in ((2, 15 * DROP, -DROP), (3, MID - 15, 1.0), (4, 15 * DROP - A, -DROP), (6, 0.5, 1.0)):
            act(col("qcol", c), col("qcol", 0), ACT.Identity, bias=a, scale=b)
        const(col("cm", 0), 0.0)

    once = {
        "iu": lambda: iota(V("iu"), [[16, 8]], 0, 0), "ip": lambda: iota(col("ipc", 0), [[0, 1]], 0, 1),
        "jr": lambda: iota(V("jr"), [[0, NC], [1, 16]], 0, 0, True), "i16": lambda: iota(V("i16"), [[16, NC]], 0, 0, True),
        "ig": lambda: band(V("ig"), V("zero", 0, 512), 16, 1.0, -1, -1), "cols": lambda: iota(V("cols"), [[1, WW]], 0, 0, True),
        "tab": table, "zero": lambda: fill(V("zero"), 0.0), "et": lambda: fill(V("et"), 0.0),
        "offu": lambda: cp(V("offu"), V("iu")), "qcol": partitions,
        "d0s": lambda: const(V("d0s"), 0.0), "d0t": lambda: const(V("d0s", 0, C, 16), -BIG), "seg": lambda: const(V("seg"), 2 * MID),
        "seh": lambda: act(V("seg", 0, C, 16), V("i16"), ACT.Identity, bias=col("qcol", 3), scale=-1.0),
        "kb": lambda: act(V("kb"), V("i16", 0, 8), ACT.Identity, bias=col("qcol", 6)),
        "qu": lambda: quant(V("qu"), V("su"), V("ut")), "qv": lambda: quant(V("qv"), V("sv"), V("vt")),
        "qu2": lambda: op("v", lambda: g.vector.tensor_copy(T.qu2[:, 0:128].bitcast(dt.uint32), T.qu[:, 0:128].bitcast(dt.uint32)
                                                            .indirect(T.offu[:, 0:8])), [V("qu"), V("offu")], [V("qu2")]),
        "su2": lambda: act(V("su2"), V("su"), ACT.Copy, off=V("offu")),
        "mk": lambda: ts(V("mk"), V("jr"), col("qcol", 0), ALU.not_equal, -BIG, ALU.mult),
        "d0g": lambda: act(V("d0g"), V("mk"), ACT.Identity, bias=63 * DROP, scale=64 * DROP / BIG),
        "pad": lambda: iota(V("x1", 4 * C), [[0, 4 * (XW - C)]], 0, 0, True), "small": small,
        "gt": lambda: band(V("gt"), V("ig"), 16, 0.0, 15, -1), "qg": lambda: quant(V("qg"), V("sg"), V("gt")),
    }
    for h in range(2):
        once["one%d" % h] = lambda h=h: select(V("et", h * EW + 2 + h, h * EW + EW, 4), V("zero", 0, EW // 4), EW // 4, 1.0, 0, 1)

    def round_steps(r):
        rw, lr, qx, sx = "rw%d" % r, "lr%d" % r, V("qx%d" % r, 0, C), V("sx%d" % r, 0, C)

        cut_at = KEPT if r else C - K

        def pack_x(n, lo, hi):
            quant(V("qx%d" % n, lo, hi), V("sx%d" % n, lo, hi), V("x1" if n else "x0", 4 * lo, 4 * hi))

        def score(k):
            lo, hi = (cut_at, cut_at + K) if k == 7 else (0, C)
            mm(V("ps%d" % k, 0, hi - lo), V("qu2"), V("su2"), V(qx[0], lo, hi), V(sx[0], lo, hi))

        def masked(lo, hi):
            p = V("ps7", lo - cut_at, hi - cut_at) if lo else V("ps0", lo, hi)
            tt(V("rm", lo, hi), p, V("mk", lo, hi), ALU.add)

        def picks(lo, hi):
            scan(V("wf", lo, hi), V("d0s", lo, hi), V("rm", lo, hi), -BIG, ALU.add, ALU.max)

        def compare(c):
            ts(slot(c, 0, 16 * c), V("ps0", 0, 16 * c), col("wf", 16 * c + 15), ALU.is_lt)

        def count(c):
            scan(V("rk", RS * (c + 1) - 8 * c, RS * (c + 1)), slot(c, 0, 8 * c), slot(c, 8 * c, 16 * c),
                 col("rk", INRUN + 16 * c + 15), ALU.add, ALU.add)

        def sign(c):
            act(slot(c, 0, 16 * c), V("ps1", 0, 16 * c), ACT.Sign, bias=col("wf", 16 * c + 15), scale=-1.0)

        def sums(c):
            act(slot(c, 0, 16 * c), slot(c, 0, 16 * c), ACT.Relu, acc=col("pa", c))

        def pack(k):
            a, b = TOFF[k], TOFF[k + 1]
            if k == 3 and r:
                b += 16 * TILES[4][0][0]
            quant(V("qt", a, b), V("stp", a, b), V("wt", 4 * a, 4 * b))

        summed = []

        def over_partitions(k):
            a, b = TOFF[k], TOFF[k + 1]
            summed.append(k)
            mm(V("ps6", 0, b - a), V("qg"), V("sg"), V("qt", a, b), V("stp", a, b), k == 0, len(summed) == len(TILES))

        def unpack_own(b):
            mm(bank(b, C), *eb(b), qx, sx)

        def keep(b):
            move(WHO["t"][r][b], win(b, 0, C), bank(b, C), None, 64.0)

        def again(b):
            mm(bank(b, C), *eb(b), qx, sx, True, False)

        def far(b):
            return V(("ps7", "ps1", "ps0", "ps7")[b], 0, C)

        def unpack(b):
            mm(far(b), *eb(b), V("lq%d" % r), V("ls%d" % r))

        def product(b):
            mm(bank(b, K), V("qw", 128 * b, 128 * b + 128), V("sw", 128 * b, 128 * b + 128), V("qz"), V("sz"))

        def sums_on_s():
            for c in ON_S:
                if c - 1 not in ON_S:
                    e = min(k for k in range(c, NC + 1) if k not in ON_S)
                    tt(V("rk", RS * c + RS - 1, RS * e, RS), wrapped("rk", INRUN + 16 * c, INRUN + 16 * e), V("pa", c, e), ALU.add)

        def shared(c):
            e, w = V("ej", EL * c, EL * c + EL), V("cs", 16 * c, 16 * c + EL)
            if c < COUNT_V:
                ts(e, w, col("kb", c), ALU.is_lt)
            else:
                act(e, w, ACT.Sign, bias=col("kb", c), scale=-1.0, acc=col("er", EH * c + EH - 1))

        def shared_sum(c):
            scan(V("er", EH * c, EH * c + EH), V("ej", EL * c, EL * c + EH), V("ej", EL * c + EH, EL * c + EL), 16.0 * c, ALU.add, ALU.add)

        def list_e():
            cp(V("eo", 0, COUNT_V), V("er", EH - 1, EH * COUNT_V, EH))
            for c in range(COUNT_V, 8):
                ts(col("eo", c), col("er", EH * c + EH - 1), 0.5, ALU.mult, 16.0 * c + EH, ALU.add)

        def flags():
            for lo, hi, c in ((0, N2, 1.0), (N2, N1, 0.0)):
                act(V("ml", 16 * lo, 16 * hi), V("mr"), ACT.Identity, bias=2 * FLAG + c, scale=-FLAG / MU, off=V("oa", lo, hi))

        def whole():
            ts(V("pi", 0, N2), wrapped("cx", 0, A), BACK, ALU.add, FLAG + 255.0, ALU.add)
            ts(V("pi", N2, NC), wrapped("cx"), BACK, ALU.add)

        def parts():
            ts(V("hi"), V("pi"), 8, ALU.arith_shift_right, 1535, ALU.bitwise_and)
            ts(V("lo"), V("pi"), 255, ALU.bitwise_and)

        def gather_new(q, b, lo, hi, w):
            move(q, V("x1", 4 * lo + b, 4 * hi, 4), win(b, 0, w), V("no", lo // 16, hi // 16), 0.015625)

        def result(h):
            lo, hi = ((0, KEPT), (KEPT, C))[h]
            move(WHO["o"][r][h], V("ysb", lo, hi), V("ps%d" % h, 0, hi - lo))

        def result_out(q, lo, hi):
            dma(q, "st", T.y[:, lo:hi], T.ysb[:, lo:hi], [V("ysb", lo, hi)], [])

        def codes_out(lo, hi):
            dma("y", "st", T.oc[:, 4 * lo:4 * hi], T.qx3[:, lo:hi].bitcast(dt.uint8), [V("qx3", lo, hi)], [])

        def scales(k):
            dma(OSQ[k], "st", T.osc[4 * k:4 * k + 4, :], T.sx3[32 * k:32 * k + 4, 0:C], [V("sx3", 0, C)], [])

        def last(h):
            lo, hi = ((0, KEPT), (KEPT, KEPT + K))[h]
            mm(V("ps%d" % h, 0, hi - lo), V("qv"), V("sv"), V("qx3", lo, hi), V("sx3", lo, hi))

        steps = {
            "qa": lambda: pack_x(r, cut_at, cut_at + K), "qb": lambda: pack_x(r, 0, cut_at),
            "la": lambda: pack_x(3, KEPT, KEPT + K), "lb": lambda: pack_x(3, 0, KEPT), "ya": lambda: last(1), "yb": lambda: last(0),
            "codes": lambda: send(r, "codes"), "ma": lambda: masked(PICK[r], C), "mb": lambda: masked(0, PICK[r]),
            "wa": lambda: picks(PICK[r], C), "wb": lambda: picks(0, PICK[r]),
            "ia": lambda: tt(slot(0, PICK[r], C), V("ps7", PICK[r] - cut_at, C - cut_at), V("wf", PICK[r], C), ALU.is_le),
            "in": lambda: tt(slot(0, 0, PICK[r]), V("ps0", 0, PICK[r]), V("wf", 0, PICK[r]), ALU.is_le),
            "eq": lambda: scan(V("rk", INRUN, INRUN + C), V("seg"), slot(0, 0, C), 2 * MID, ALU.min, ALU.add),
            "e3s": sums_on_s, "cw": lambda: hold(V("cw"), V("ps6", 0, C)),
            "pd": lambda: tt(V("pd"), wrapped("cw"), V("rk", RS - 1, RS * NC, RS), ALU.subtract),
            "rw": lambda: ts(V(rw), V("pd"), BACK, ALU.add, MID, ALU.add), "places": lambda: send(r, "places"),
            "orow": lambda: scatter(V("sval", A, A + C), V(rw), V("cols", 0, C)),
            "sv": lambda: select(V("sval", 0, A), V("sval", A, 2 * A), A, 0.0, -1, 0),
            "fq": lambda: move(WHO["fq"][r], V("fq"), V("tab"), V(rw)),
            "fp": lambda: move(WHO["fp"][r], V("fr"), V("fq"), None, 1.0 / MU),
            "ox": lambda: hold(V("ox"), V("sval", A, A + KEPT)), "oa": lambda: ts(V("oa"), wrapped("ox"), BACK, ALU.add),
            "qf": lambda: quant(V("qf"), V("sf"), V("ff")),
            "m": lambda: tt(V("mr"), V("tab"), V("fq"), ALU.min, off=V(lr)),
            "sh": lambda: ts(V("sh"), V("mr"), 1.0, ALU.min) if WHO["sh"][r] == "v" else act(V("sh"), V("mr"), ACT.Sign),
            "cs": lambda: scan(V("cs"), V("zero", 0, C), V("sh"), 0.0, ALU.add, ALU.add), "eo": list_e,
            "cm": lambda: scan(V("cm", 1, C + 1), V("fr"), V("mr"), 0.0, ALU.add, ALU.add), "ml": flags,
            "cg": lambda: tt(V("cg"), V("cm", 0, C), V("ml"), ALU.add, off=V("oa")), "cx": lambda: hold(V("cx"), V("cg")),
            "pi": whole, "hr": parts,
            "mq": lambda: act(col("tot", 0), col("cm", C), ACT.Identity, bias=0.25 - C / MU, scale=1.0 / MU),
            "rr": lambda: ts(V("rr"), V("lo"), col("tot", 0), ALU.add),
            "sl": lambda: tt(V("sl"), V("rr"), V("hi"), ALU.min), "so": lambda: cp(V("so"), V("sl")),
            "sc": lambda: scatter(V("nrow"), V("so"), V("sval", 0, C)),
            "ny": lambda: hold(V("nx", KEPT, C), V("nrow", KEPT, C)), "ne": lambda: ts(V("no", N1, NC), wrapped("nx", KEPT, C), BACK, ALU.add),
            "sk": lambda: move(WHO["sk"][r], V("sk"), V("cm", 0, C), V("eo")), "skh": lambda: hold(V("skx"), V("sk")),
            "sko": lambda: ts(V("sko"), wrapped("skx"), col("qcol", 4), ALU.add, 2.0 ** -8, ALU.mult),
            "fix": lambda: scatter(V("nrow", 0, KEPT), V("sko"), V("cols", C)),
            "nx": lambda: hold(V("nx", 0, KEPT), V("nrow", 0, KEPT)), "no": lambda: ts(V("no", 0, N1), wrapped("nx", 0, KEPT), BACK, ALU.add),
            "qz": lambda: quant(V("qz"), V("sz"), V("zt")), "nc": lambda: act(V("nlb"), V("nrow"), ACT.Copy),
            "nl": lambda: dma("y", "st", T.nl[:, :], T.nlb[0:128:16, :], [V("nlb")], []),
            "yo": lambda: result_out("s", 0, KEPT), "ye": lambda: result_out("y", KEPT, C),
            "oc": lambda: codes_out(0, KEPT), "oe": lambda: codes_out(KEPT, C),
        }
        each = {"i": scales, "o": result, "x": cut, "w": unpack_own, "q": score, "b": blank,
                "s": sign, "r": sums, "c": compare, "n": count, "p": pack, "t": keep, "d": again, "h": unpack, "f": over_partitions, "k": product,
                "u": lambda b: move(WHO["u"][r][b], V("ff", b, 4 * C, 4), far(b), None, -1.0),
                "v": lambda b: mm(bank(b, C), *eb(b), V("qf"), V("sf"), False, True),
                "z": lambda b: move(WHO["z"][r][b], V("zw", b * C, b * C + C), bank(b, C)), "E": shared, "F": shared_sum,
                "g": lambda b: move(WHO["g"][r][b], V("zt", b, 4 * K, 4), V("zw", b * C, b * C + C), V("eo")),
                "j": lambda b: move(WHO["j"][r][b], V("f64", b * K, b * K + K), win(b, 0, C), V("eo")),
                "a": lambda b: tt(win(b, C, WW), bank(b, K), V("f64", b * K, b * K + K), ALU.add),
                "e": lambda b: gather_new(WHO["e"][r][b], b, KEPT, C, C), "l": lambda b: gather_new(WHO["l"][r][b], b, 0, KEPT, WW)}

        def do(name):
            if name in steps:
                steps[name]()
            elif name in once:
                once[name]()
            else:
                each[name[0]](int(name[1:]))
        return do

    rounds = [round_steps(r) for r in range(3)]
    for r in range(3):
        for name in ORDER[r].split():
            rounds[r + name.startswith("+")](name.lstrip("+"))

    for s in SEMAPHORES:
        if total.get(s, 0):
            g.wait_ge(T.sem[s], total[s])
